import numpy as np, ml_dtypes
CORES = [24,25,26,27,28,29,30,31]
N = 8
BF = ml_dtypes.bfloat16
B, W, CAP, RO = 2048, 6144, 48, 3
L = N * CAP
def parts(rng):
    share = rng.choice(np.array([0.1, 0.2, 0.4, 0.6]), (N, 8, 1, B))
    v = np.where(rng.random((N, 8, 16, B)) < share, -rng.integers(1, 256, (N, 8, 16, B)), rng.integers(0, 256, (N, 8, 16, B)))
    a = rng.integers(0, 256, (N, 8, 16, W)) * (rng.random((N, 8, 16, W)) < rng.choice(np.array([0.3, 0.6, 0.9]), (N, 8, 1, W))); a[..., W - 1] = 0
    u = rng.integers(0, W - 1, (N, 8, 16, B))
    u = np.where(rng.random(u.shape) < rng.choice(np.array([0.0, 0.0, 0.1, 0.1, 0.4, 0.96]), (N, 8, 1, B)), W - 1, u)
    to = np.where(rng.random((N, 8, W)) < rng.choice(np.array([0.0, 0.1, 0.25]), (N, 8, 1)), rng.integers(0, N, (N, 8, 1)), rng.integers(0, N, (N, 8, W)))
    pay = to * B + rng.integers(0, B, (N, 8, W))
    wk = np.where(rng.random((N, 8, L)) < 0.04, B, rng.integers(0, B, (N, 8, L)))
    return v, a, u, pay, wk
def pack(v, a, u, pay, wk):
    return {"vp": np.ascontiguousarray(v.reshape(N, 128, B)).astype(np.float32).astype(BF), "am": np.ascontiguousarray(a.reshape(N, 128, W)).astype(np.float32).astype(BF),
            "qu": np.ascontiguousarray(u.reshape(N, 128, B)).astype(np.int32), "pay": np.ascontiguousarray(pay).astype(np.int32), "wk": np.ascontiguousarray(wk).astype(np.int32)}
def setup_inputs(rng):
    return pack(*parts(rng))
def plant(rng, v, a, u, pay, wk, q, g, to):
    m = len(to); lanes = rng.permutation(L)[:m]; banks = rng.permutation(B)[:m]; lines = rng.permutation(W - 1)[:m]
    row = rng.integers(0, 16, m); j = rng.integers(0, 16, m)
    u[q, g][:, banks] = W - 1; u[q, g][row, banks] = lines
    v[q, g][j, banks] = -rng.integers(1, 256, m); a[q, g][j, lines] = 255
    order = np.argsort(lanes); pay[q, g][lines[order]] = to
    wk[q, g] = B; wk[q, g][lanes] = banks
def setup_inputs_room(rng):
    v, a, u, pay, wk = parts(rng)
    for q in range(N):
        for g in range(8):
            cnt = [CAP, CAP + 1, CAP - 1, 0, 1, 0, 2, CAP // 2][:N]
            if (q + g) % 4 == 3: cnt = [L] + [0] * (N - 1)
            to = np.concatenate([np.full(n, (q + 1 + g + j) % N, np.int64) for j, n in enumerate(cnt)])
            plant(rng, v, a, u, pay, wk, q, g, rng.permutation(to) * B + rng.integers(0, B, len(to)))
    return pack(v, a, u, pay, wk)
def setup_inputs_ties(rng):
    v, a, u, pay, wk = parts(rng)
    v[:, ::2] = rng.integers(-3, 3, (N, 4, 16, B)); a[:, ::2] = rng.integers(0, 4, (N, 4, 16, W))
    v[:, 1::2] = rng.integers(-3, 2, (N, 4, 16, B)) * 85; a[:, 1::2] = rng.integers(0, 4, (N, 4, 16, W)) * 85
    a = a * (rng.random((N, 8, 1, W)) < 0.6); a[..., W - 1] = 0
    u[:, :, 15] = np.where(rng.random((N, 8, B)) < 0.4, W - 1, u[:, :, 15])
    return pack(v, a, u, pay, wk)
def setup_inputs_alike(rng):
    v, a, u, pay, wk = parts(rng)
    wk[:, 0] = rng.choice(np.array([0, B - 1, 5, B // 2]), (N, L))
    u[:, 2] = rng.choice(np.array([0, W - 2, 7, W // 2, W - 1]), (N, 16, B))
    pay[:, 4] = rng.integers(0, N, (N, W)) * B + rng.choice(np.array([0, B - 1]), (N, W))
    u[:, 6] = np.repeat(u[:, 6, :1], 16, axis=1)
    wk[:, 1::2, L - 1] = wk[:, 1::2, 0]
    return pack(v, a, u, pay, wk)
def setup_inputs_dry(rng):
    v, a, u, pay, wk = parts(rng); o = rng.permutation(8)
    wk[:, o[0]] = B; a[:, o[1]] = 0; u[:, o[2]] = W - 1; v[:, o[3]] = np.abs(v[:, o[3]])
    v[:, o[4]] = -255; a[:, o[4]] = 255; a[..., W - 1] = 0
    wk[rng.integers(0, N), o[5]] = B
    h = int(o[6]); wk[:, h] = B
    for q in range(N):
        b = int(rng.integers(1, B)); n, m = [int(i) for i in rng.permutation(W - 1)[:2]]
        wk[q, h, int(rng.integers(0, L))] = b
        v[q, h, :, b] = -rng.integers(1, 256, 16); u[q, h, :, b] = n; a[q, h, :, n] = 0; pay[q, h, n] = (q + 1) % N * B
        v[q, h, :, 0] = -rng.integers(1, 256, 16); u[q, h, :, 0] = m; a[q, h, :, m] = 255; pay[q, h, m] = rng.integers(0, N) * B + rng.integers(1, B)
    return pack(v, a, u, pay, wk)
def setup_inputs_spread(rng):
    v, a, u, pay, wk = parts(rng)
    v = (np.exp2(8 * rng.random((N, 8, 1, B))) * rng.random((N, 8, 16, B))).astype(np.int64) * np.where(rng.random((N, 8, 16, B)) < 0.4, -1, 1)
    a = (np.exp2(8 * rng.random((N, 8, 1, W))) * rng.random((N, 8, 16, W))).astype(np.int64); a[..., W - 1] = 0
    u = np.where(u == W - 1, u, ((W - 1) * rng.random(u.shape) ** 2).astype(np.int64))
    pay = pay // B * B + (B * rng.random(pay.shape) ** 2).astype(np.int64)
    wk = np.where(wk == B, B, (B * rng.random(wk.shape) ** 2).astype(np.int64))
    return pack(v, a, u, pay, wk)
def check_inputs(d):
    bad = []
    for k, lo, hi in (("vp", -255, 255), ("am", 0, 255)):
        x = np.asarray(d[k]).astype(np.float32)
        if not np.all((x >= lo) & (x <= hi)): bad.append("range of " + k)
        elif not np.all(x == np.rint(x)): bad.append("whole numbers in " + k)
    if not np.all(np.asarray(d["am"]).astype(np.float32)[..., W - 1] == 0): bad.append("zeros in the last column of am")
    for k, hi in (("qu", W - 1), ("pay", N * B - 1), ("wk", B)):
        if np.min(d[k]) < 0 or np.max(d[k]) > hi: bad.append("range of " + k)
    return bad
def reference(vp, am, qu, pay, wk):
    v = vp.astype(np.float32).astype(np.int64).reshape(N, 8, 16, B); a = am.astype(np.float32).astype(np.int64).reshape(N, 8, 16, W)
    u = qu.astype(np.int64).reshape(N, 8, 16, B); payee = pay.astype(np.int64)
    w = wk.astype(np.int64); c = np.zeros((N, 8, 16, L), np.int64)
    for rnd in range(RO):
        w2 = np.full((N, 8, L), B, np.int64); c2 = np.zeros((N, 8, 16, L), np.int64)
        for q in range(N):
            for g in range(8):
                vv, aa, uu = v[q, g], a[q, g], u[q, g]
                lane = np.nonzero(w[q, g] < B)[0]
                lane = lane[np.sort(np.unique(w[q, g][lane], return_index=True)[1])]
                b = w[q, g][lane]
                x = np.maximum(vv[:, b] - c[q, g][:, lane], -255); vv[:, b] = x
                keep = np.any(x < 0, axis=0); b, x = b[keep], x[:, keep]
                n = uu[:, b]
                score = np.sum(x[:, None, :] + aa[:, n] >= 0, axis=0)
                best = 15 - np.argmax(score[::-1], axis=0)
                p = n[best, np.arange(len(b))]
                keep = p != W - 1; b, x, best, p = b[keep], x[:, keep], best[keep], p[keep]
                keep = np.sort(np.unique(p, return_index=True)[1]); b, x, best, p = b[keep], x[:, keep], best[keep], p[keep]
                t = np.minimum(aa[:, p], np.maximum(-x, 0))
                vv[:, b] = x + t; aa[:, p] = aa[:, p] - t; uu[best, b] = W - 1
                to = payee[q, g][p]
                for r in range(N):
                    k = np.nonzero(to // B == r)[0][:CAP]; s = q * CAP + np.arange(len(k))
                    w2[r, g][s] = to[k] % B; c2[r, g][:, s] = t[:, k]
        w, c = w2, c2
    return {"yv": v.reshape(N, 128, B).astype(np.float32).astype(BF), "yw": w.astype(np.float32), "yc": c.reshape(N, 128, L).astype(np.float32).astype(BF)}

@@ -1,0 +1,459 @@
+from concourse.bass import DstId, RemoteDMATransfer
+from concourse.mybir import AluOpType, ActivationFunctionType
+
+A = AluOpType
+F = ActivationFunctionType
+NR, B, W, CAP, RO = 8, 2048, 6144, 48, 3
+L = NR * CAP
+VW = 2560
+AW = 6544
+PITCH = 400
+SW = 3600
+BIG = 8388608.0
+SC = 131072.0
+NA = 4
+K_PAIRS, N_PAIRS, K_ND, K_VAL, K_BASE, K_SCORE, K_BEST = 2, 2, 3, 4, 5, 6, 7
+C_OWN = {2: (0, 4), 4: (4, 8)}
+
+SCRATCH = {
+    "vw": ("sbuf", [128, VW], "bfloat16"), "qw": ("sbuf", [128, VW], "int32"), "aw": ("sbuf", [128, AW], "bfloat16"),
+    "pw": ("sbuf", [128, W], "int32"), "hw": ("sbuf", [128, W], "float32"), "wn": ("sbuf", [128, 32], "float32"),
+    "cc": ("sbuf", [128, 24, 256], "bfloat16"), "gg": ("sbuf", [128, L * 16], "bfloat16"),
+    "vr": ("sbuf", [128, 3072], "bfloat16"), "ee": ("sbuf", [128, 24, L], "bfloat16"),
+    "lm": ("sbuf", [128, 16, 128], "bfloat16"), "tm": ("sbuf", [128, 16, 128], "bfloat16"),
+    "rm": ("sbuf", [128, 2048], "bfloat16"), "ir": ("sbuf", [128, 2048], "bfloat16"),
+    "bo": ("sbuf", [128, 128], "bfloat16"), "bp": ("sbuf", [128, 128], "bfloat16"), "idb": ("sbuf", [128, 128], "bfloat16"),
+    "zb": ("sbuf", [128, L], "bfloat16"), "dsf": ("sbuf", [128, 4, 128], "float32"), "dsb": ("sbuf", [128, 4, 128], "bfloat16"),
+    "pi": ("sbuf", [128, 4], "int32"), "io128": ("sbuf", [128, 128], "bfloat16"), "iog": ("sbuf", [128, 128], "bfloat16"),
+    "io16": ("sbuf", [128, 16], "bfloat16"), "trv": ("sbuf", [128, 24], "float32"), "wc": ("sbuf", [128, 48], "float32"),
+    "col": ("sbuf", [128, 16], "float32"), "wkz": ("sbuf", [128, L], "int32"), "w16": ("sbuf", [128, L], "float16"),
+    "land1": ("sbuf", [128, L], "float32"), "land2": ("sbuf", [128, L], "float32"), "land3": ("sbuf", [128, L], "float32"),
+    "sw0": ("sbuf", [128, SW], "float32"), "sw1": ("sbuf", [128, SW], "float32"), "sw2": ("sbuf", [128, SW], "float32"),
+    "tt": ("sbuf", [128, L], "float32"), "tqi": ("sbuf", [128, 24], "int32"), "tq": ("sbuf", [128, 24], "float16"),
+    "bl": ("sbuf", [128, 24], "uint16"), "bf": ("sbuf", [128, 24], "float32"), "b16": ("sbuf", [128, L], "float16"),
+    "yy": ("sbuf", [128, L], "float32"), "li": ("sbuf", [128, L], "int32"), "ci": ("sbuf", [128, L], "int32"),
+    "cb": ("sbuf", [128, L], "bfloat16"), "q16": ("sbuf", [128, L], "uint16"), "qf": ("sbuf", [128, L], "float32"),
+    "qt": ("sbuf", [128, 12, 32], "float32"), "k1s": ("sbuf", [128, 24, 16], "float32"), "kk": ("sbuf", [128, 24, 16], "float32"),
+    "t8": ("sbuf", [128, 24, 8], "float32"), "t4": ("sbuf", [128, 24, 4], "float32"), "t2": ("sbuf", [128, 24, 2], "float32"),
+    "ki": ("sbuf", [128, 24], "int32"), "ni": ("sbuf", [128, 24], "int32"), "ii": ("sbuf", [128, 24], "int32"),
+    "nl": ("sbuf", [128, 24], "uint16"), "il": ("sbuf", [128, 24], "uint16"), "sl": ("sbuf", [128, 24], "uint16"),
+    "ol": ("sbuf", [128, 24], "uint16"), "al": ("sbuf", [128, 24], "uint16"),
+    "f1": ("sbuf", [128, 24], "float32"), "f2": ("sbuf", [128, 24], "float32"), "f3": ("sbuf", [128, 24], "float32"),
+    "e1": ("sbuf", [128, 24], "float32"), "e2": ("sbuf", [128, 24], "float32"), "e3": ("sbuf", [128, 24], "float32"),
+    "g0": ("sbuf", [128, 24], "float32"), "g1": ("sbuf", [128, 24], "float32"), "g2": ("sbuf", [128, 24], "float32"),
+    "g3": ("sbuf", [128, 24], "float32"), "g4": ("sbuf", [128, 24], "float32"), "g5": ("sbuf", [128, 24], "float32"),
+    "g6": ("sbuf", [128, 24], "float32"), "basev": ("sbuf", [128, 24], "float32"), "ho": ("sbuf", [128, 24], "float32"),
+    "x1": ("sbuf", [128, L], "float32"), "xx": ("sbuf", [128, L], "bfloat16"), "xt": ("sbuf", [128, L], "bfloat16"),
+    "ng": ("sbuf", [128, L], "bfloat16"), "nd": ("sbuf", [128, L], "bfloat16"), "wv": ("sbuf", [128, L], "bfloat16"),
+    "nh": ("sbuf", [128, L], "float16"), "ag": ("sbuf", [128, L], "bfloat16"), "p0": ("sbuf", [128, L], "float32"),
+    "ab": ("sbuf", [128, L], "float32"), "th": ("sbuf", [128, L], "bfloat16"), "tn": ("sbuf", [128, L], "bfloat16"),
+    "td": ("sbuf", [128, L], "bfloat16"), "pp": ("sbuf", [128, L], "float32"), "st": ("sbuf", [128, L], "float32"),
+    "ss": ("sbuf", [128, L], "float16"), "qn": ("sbuf", [128, L], "float32"), "q2": ("sbuf", [128, L], "float32"),
+    "ps0": ("psum", [128, 512], "float32"), "ps1": ("psum", [128, 512], "float32"), "ps2": ("psum", [128, 512], "float32"),
+    "key0": ("psum", [128, 512], "float32"), "key1": ("psum", [128, 512], "float32"), "cv": ("psum", [128, 512], "float32"),
+    "rb": ("psum", [128, 512], "float32"), "k1": ("psum", [128, 12, 2, 16], "float32"),
+}
+SEMAPHORES = ["qv", "qa", "qt", "qp", "dwk", "dvp", "dqu", "dam", "dpay", "dyv", "dyw", "dyc", "arr0", "arr1", "arr2", "sent"]
+
+
+def make_queues(g, T):
+    ops, last_w, readers = [], {}, {}
+
+    def op(q, fn, r=(), w=(), dma=None, ext=None):
+        deps = [(last_w[k], "raw") for k in r if k in last_w]
+        for k in w:
+            if k in last_w:
+                deps.append((last_w[k], "waw"))
+            deps += [(o, "war") for o in readers.get(k, ())]
+        i = len(ops)
+        ops.append({"q": q, "fn": fn, "deps": deps, "dma": dma, "ext": ext, "inc": False})
+        for k in w:
+            last_w[k] = i
+            readers[k] = []
+        for k in r:
+            readers.setdefault(k, []).append(i)
+
+    def emit():
+        engine = {"v": g.vector, "a": g.scalar, "t": g.tensor, "p": g, "s": g.sync}
+        sem = {"v": T.sem.qv, "a": T.sem.qa, "t": T.sem.qt, "p": T.sem.qp}
+        known = {q: {} for q in engine}
+        seq = {q: 0 for q in engine}
+        waits = []
+        for o in ops:
+            o["seq"] = seq[o["q"]]
+            if o["ext"] is None:
+                seq[o["q"]] += 1
+            need = {}
+            kn = known[o["q"]]
+            for j, kind in o["deps"]:
+                d = ops[j]
+                if d["ext"] is not None or d["dma"] is not None:
+                    name = d["ext"] or d["dma"]
+                    if kn.get(name[0], 0) < name[1]:
+                        need[name[0]] = (max(need.get(name[0], (0, 0))[0], name[1]), j)
+                    continue
+                if d["q"] == o["q"] and o["dma"] is None and (kind == "war" or o["q"] == "t"):
+                    continue
+                if kn.get(d["q"], -1) < d["seq"] and need.get(d["q"], (-1, 0))[0] < d["seq"]:
+                    need[d["q"]] = (d["seq"], j)
+            for key, (val, j) in need.items():
+                for k2, v2 in ops[j]["clock"].items():
+                    if k2 != key and kn.get(k2, -1) < v2:
+                        kn[k2] = v2
+            final = []
+            for key, (val, j) in need.items():
+                if not any(k2 != key and ops[j2]["clock"].get(key, -1) >= val for k2, (v2, j2) in need.items()):
+                    final.append((key, val, j))
+                    if key in sem:
+                        ops[j]["inc"] = True
+                kn[key] = max(kn.get(key, -1), val)
+            o["clock"] = dict(kn)
+            waits.append(final)
+        count = {q: 0 for q in engine}
+        for o in ops:
+            count[o["q"]] += 1 if o["inc"] else 0
+            o["count"] = count[o["q"]]
+        for i, o in enumerate(ops):
+            if o["ext"] is not None:
+                continue
+            e = engine[o["q"]]
+            for key, val, j in waits[i]:
+                e.wait_ge(sem[key] if key in sem else T.sem[key], ops[j]["count"] if key in sem else val)
+            ins = o["fn"](e)
+            if o["dma"] is not None:
+                ins.then_inc(T.sem[o["dma"][0]], 16)
+            elif o["inc"]:
+                ins.then_inc(sem[o["q"]], 1)
+        for q in sem:
+            if count[q]:
+                g.wait_ge(sem[q], count[q])
+    return op, emit
+
+
+def rank_program(g, core, T, topo):
+    rank = T.rank_of(core)
+    if rank is None:
+        return
+    op, emit = make_queues(g, T)
+    c_m, c_g, c_p, c_x, c_h0, c_h1, c_ctr, c_sub, c_sgn, c_ini, c_i13, c_n13, c_wn, c_t, c_sg2 = range(15)
+
+    def col(k):
+        return T.col[:, k:k + 1]
+
+    def ts(out, in0, s1, s2, o0, o1, r, w):
+        op("v", (lambda e: e.tensor_scalar(out, in0, s1, s2, o0, o1)) if o1 else (lambda e: e.tensor_scalar(out, in0, s1, None, o0)), r, w)
+
+    def tt(out, in0, in1, o, r, w):
+        op("v", lambda e: e.tensor_tensor(out, in0, in1, o), r, w)
+
+    def tc(out, in_, r, w):
+        op("v", lambda e: e.tensor_copy(out, in_), r, w)
+
+    def fill(out, k, w):
+        op("v", lambda e: e.memset(out, k), [], w)
+
+    def act(out, in_, f, r, w, bias=0.0, scale=1.0):
+        op("a", lambda e: e.activation(out, in_, f, bias=bias, scale=scale), r, w)
+
+    def mm(out, lhs, rhs, start, stop, r, w):
+        op("t", lambda e: e.matmul(out, lhs, rhs, start, stop), r, w)
+
+    def iota(out, pattern, base, cm, w):
+        op("p", lambda e: e.iota(out, pattern, base, cm, allow_small_or_imprecise_dtypes=True), [], w)
+
+    fill(T.wkz[:], 0, ["wkz"])
+    op("s", lambda e: e.dma_start(T.wkz[0::16, :], T.wk[:]), [], ["wkz"], dma=("dwk", 16))
+    op("s", lambda e: e.dma_start(T.qw[:, 0:B], T.qu[:]), [], ["qw"], dma=("dqu", 16))
+    op("a", lambda e: e.dma_start(T.vw[:, 0:B], T.vp[:]), [], ["vw"], dma=("dvp", 16))
+    op("s", lambda e: e.dma_start(T.aw[:, 0:W], T.am[:]), [], ["aw"], dma=("dam", 16))
+    for j in range(16):
+        op("s", lambda e, j=j: e.dma_start(T.pw[j::16, :], T.pay[:]), ["aw"] if j == 0 else [], ["pw%d" % j], dma=("dpay", 256))
+
+    op("p", lambda e: e.iota(T.pi[:, 0:1], [[1, 1]], 0, 1), [], ["pi0"])
+    iota(T.iog[:], [[1, 8], [0, 16]], 0, 0, ["iog"])
+    iota(T.io128[:], [[1, 128]], 0, 0, ["io128"])
+    iota(T.io16[:], [[1, 16]], 0, 0, ["io16"])
+    iota(T.trv[:], [[16, 24]], 2064, 1, ["trv"])
+    iota(T.ir[:], [[1, 128], [0, 16]], 0, 0, ["ir"])
+    iota(T.hw[:, 0:4096], [[2, 4096]], -4096, 0, ["hw"])
+    iota(T.hw[:, 4096:W - 1], [[2, W - 1 - 4096]], -2047, 0, ["hwb"])
+    iota(T.hw[:, W - 1:W], [[1, 1]], 5000, 0, ["hwc"])
+    for s in range(RO):
+        for d in range(NR):
+            a0 = PITCH * d + 1
+            iota(T["sw%d" % s][:, a0:a0 + CAP], [[0, CAP]], (d * B + B) * 512, 0, ["sw%d_%d" % (s, d)])
+    fill(T.vw[:, B:B + 16], 0.0, ["vwp"])
+    fill(T.qw[:, B:B + 16], W - 1, ["qwp"])
+    fill(T.zb[:], 0.0, ["zb"])
+    fill(T.lm[:], 0.0, ["lm0"])
+    fill(T.wn[:, 16:32], 0.0, ["wnb"])
+    ts(T.pi[:, 1:2], T.pi[:, 0:1], 15, None, A.bitwise_and, None, ["pi0"], ["pi1"])
+    ts(T.pi[:, 2:3], T.pi[:, 0:1], 4, None, A.arith_shift_right, None, ["pi0"], ["pi2"])
+    ts(T.pi[:, 3:4], T.pi[:, 0:1], 4, 1, A.arith_shift_right, A.bitwise_and, ["pi0"], ["pi3"])
+    tc(col(c_p), T.pi[:, 0:1], ["pi0"], ["c_p"])
+    tc(col(c_m), T.pi[:, 1:2], ["pi1"], ["c_m"])
+    tc(col(c_g), T.pi[:, 2:3], ["pi2"], ["c_g"])
+    tc(col(c_h1), T.pi[:, 3:4], ["pi3"], ["c_h1"])
+    ts(col(c_h0), col(c_h1), -1.0, 1.0, A.mult, A.add, ["c_h1"], ["c_h0"])
+    ts(col(c_x), col(c_h1), -32.0, 16.0, A.mult, A.add, ["c_h1"], ["c_x0"])
+    ts(T.bo[:], T.iog[:], col(c_g), None, A.is_equal, None, ["iog", "c_g"], ["bo"])
+    tt(col(c_x), col(c_x), col(c_p), A.add, ["c_x0", "c_p"], ["c_x"])
+    for k, (pc, hc) in enumerate(((c_p, c_h0), (c_x, c_h0), (c_p, c_h1), (c_x, c_h1))):
+        ts(T.dsf[:, k, :], T.io128[:], col(pc), col(hc), A.is_equal, A.mult, ["io128", "c_p", "c_x", "c_h0", "c_h1"], ["dsf%d" % k])
+    for k in range(4):
+        tc(T.dsb[:, k, :], T.dsf[:, k, :], ["dsf%d" % k], ["dsb%d" % k])
+    dsf = ["dsf%d" % k for k in range(4)]
+    dsb = ["dsb%d" % k for k in range(4)]
+    ts(T.idb[:], T.io128[:], col(c_p), None, A.is_equal, None, ["io128", "c_p"], ["idb"])
+    for a in range(16):
+        ts(T.lm[:, a, a::16], T.bo[:, 0::16], SC, None, A.mult, None, ["bo", "lm0"], ["lm%d" % (a + 1)])
+    ts(col(c_i13), col(c_m), 8192.0, None, A.mult, None, ["c_m"], ["c_i13"])
+    ts(col(c_n13), col(c_m), -8192.0, None, A.mult, None, ["c_m"], ["c_n13"])
+    ts(col(c_wn), col(c_m), 8192.0, float(W - 1), A.mult, A.add, ["c_m"], ["c_wn"])
+    ts(col(c_ctr), col(c_m), -2048.0, -1023.5, A.mult, A.add, ["c_m"], ["c_ctr"])
+    ts(col(c_ini), col(c_m), float(PITCH), -1592.0, A.mult, A.add, ["c_m"], ["c_ini"])
+    ts(col(c_sgn), col(c_m), 8.0, -2.0, A.is_equal, A.mult, ["c_m"], ["c_sgn0"])
+    ts(col(c_t), col(c_m), 8.0, 999.0, A.is_gt, A.mult, ["c_m"], ["c_t"])
+    ts(col(c_sub), col(c_m), 8.0, -1.25, A.is_equal, A.mult, ["c_m"], ["c_sub0"])
+    ts(T.wc[:, 0:16], T.io16[:], col(c_m), None, A.is_gt, None, ["io16", "c_m"], ["wc0"])
+    ts(T.wc[:, 16:32], T.io16[:], col(c_m), -0.5, A.is_equal, A.mult, ["io16", "c_m"], ["wc1"])
+    tc(T.bp[:], T.bo[:], ["bo"], ["bp0"])
+    ts(T.wn[:, 0:16], T.io16[:], col(c_m), col(c_wn), A.is_equal, A.mult, ["io16", "c_m", "c_wn"], ["wna"])
+    ts(col(c_sgn), col(c_sgn), 1.0, None, A.add, None, ["c_sgn0"], ["c_sgn"])
+    ts(col(c_sg2), col(c_sgn), -2.0, None, A.mult, None, ["c_sgn"], ["c_sg2"])
+    tt(col(c_sub), col(c_sub), col(c_t), A.add, ["c_sub0", "c_t"], ["c_sub1"])
+    tt(T.wc[:, 32:48], T.wc[:, 0:16], T.wc[:, 16:32], A.add, ["wc0", "wc1"], ["wc"])
+    ts(T.bp[:, 8::16], T.bo[:, 8::16], -1.0, None, A.mult, None, ["bo", "bp0"], ["bp"])
+    ts(col(c_sub), col(c_sub), 1.0, None, A.add, None, ["c_sub1"], ["c_sub"])
+    for a in range(16):
+        ts(T.tm[:, a, :], T.bp[:], T.wc[:, 32 + a:33 + a], None, A.mult, None, ["bp", "wc"], ["tm%d" % a])
+    ts(T.rm[:], T.ir[:], col(c_p), None, A.is_equal, None, ["ir", "c_p"], ["rm"])
+    tc(T.w16[:], T.wkz[:], ["wkz"], ["w16"])
+    tc(T.tt[:], T.wkz[:], ["wkz"], ["tt"])
+    op("v", lambda e: e.transpose(T.yy[:], T.tt[:]), ["tt"], ["yy"])
+    tc(T.tq[:], T.yy[:, 0::16], ["yy"], ["tq"])
+
+    lms = ["lm%d" % a for a in range(17)]
+    tms = ["tm%d" % a for a in range(16)]
+    ees = ["ee%d" % c for c in range(24)] + ["ee%dx" % c for c in range(12)]
+
+    def compare(buf, own, key, own_key, h=None):
+        for c in range(12 if h == 0 else 24):
+            lo = 192 if h == 1 and c < 12 else 16 * c
+            hi = 192 if h == 0 else L
+            ts(T.ee[:, c, lo - 16 * c:hi - 16 * c], buf[:, lo:hi], own[:, c:c + 1], None, A.is_equal, None,
+               [key + "0" if h is not None else key, own_key + "0" if c < 12 and h is not None else own_key] + ([key] if h == 1 else []),
+               ["ee%d%s" % (c, "x" if h == 0 else "")])
+
+    def pairs(part=0, parts=1):
+        calls = [lambda: mm(T.rb[:, 0:L], T.lm[:, 15, :], T.zb[:], True, False, lms + ["zb"], ["rb"])]
+        for c in range(23):
+            calls.append(lambda c=c: mm(T.rb[:, 16 * (c + 1):L], T.bp[:], T.ee[:, c, 16:L - 16 * c], False, False,
+                                        ["bp", "ee%d" % c] + (["ee%dx" % c] if c < 12 else []), ["rb"]))
+        for a in range(16):
+            calls.append(lambda a=a: mm(T.rb[:, a:L:16], T.tm[:, a, :], T.ee[:, :, a], False, a == 15, tms + ees, ["rb"]))
+        n = len(calls)
+        for f in calls[n * part // parts:n * (part + 1) // parts]:
+            f()
+
+    def spread(src, key, c0):
+        for a in range(16):
+            mm(T.cv[:, c0:c0 + 24], T.lm[:, a, :], src[:, a::16], a == 0, a == 15, lms + [key], ["cv"])
+
+    def gather(u):
+        act(T.gg[:, 512 * u:512 * (u + 1)], T.aw[:, 0:W].indirect(T.q16[:, 32 * u:32 * (u + 1)]), F.Copy, ["aw", "q16"], ["gg%d" % u])
+
+    def addv(u):
+        pk = "ps%d" % (u % 3)
+        mm(T[pk][:], T.idb[:], T.gg[:, 512 * u:512 * (u + 1)], True, False, ["idb", "gg%d" % u], [pk])
+        mm(T[pk][:], T.xt[:, 128 * (u // 4):128 * (u // 4 + 1)], T.rm[:, 512 * (u % 4):512 * (u % 4 + 1)], False, True, ["xt", "rm"], [pk])
+
+    def sign(u):
+        pk = "ps%d" % (u % 3)
+        act(T.cc[:, 2 * u:2 * u + 2, :], T[pk][:], F.Sign, [], [pk, "cc%d" % u, "ccb%d" % u], bias=0.5)
+
+    def score(q):
+        kb, off = "key%d" % (q // 3), 64 * (q % 3)
+        for a in range(16):
+            mm(T[kb][:, off:off + 64], T.lm[:, a, :], T.cc[:, 4 * q:4 * q + 4, 16 * a:16 * a + 16], a == 0, a == 15,
+               lms + ["cc%d" % (2 * q), "cc%d" % (2 * q + 1), "ccb%d" % (2 * q), "ccb%d" % (2 * q + 1)], [kb])
+
+    def best(h):
+        kb, hs, n = "key%d" % h, slice(12 * h, 12 * h + 12), "%d" % h
+        tt(T.kk[:, hs, :], T[kb][:, 0:192], T.k1s[:, hs, :], A.add, ["k1s"], [kb, "kk" + n])
+        tt(T.t8[:, hs, :], T.kk[:, hs, 0:8], T.kk[:, hs, 8:16], A.max, ["kk" + n], ["t8" + n])
+        tt(T.t4[:, hs, :], T.t8[:, hs, 0:4], T.t8[:, hs, 4:8], A.max, ["t8" + n], ["t4" + n])
+        tt(T.t2[:, hs, :], T.t4[:, hs, 0:2], T.t4[:, hs, 2:4], A.max, ["t4" + n], ["t2" + n])
+        tt(T.ki[:, hs], T.t2[:, hs, 0], T.t2[:, hs, 1], A.max, ["t2" + n], ["ki" + n])
+
+    def own_units(c0, c1):
+        for c in range(c0, c1):
+            tt(T.cc[:, c, :], T.aw[:, 0:W].indirect(T.q16[:, 16 * c:16 * c + 16]), T.vr[:, 256 * c:256 * c + 256], A.is_ge,
+               ["aw", "q16"] + ["vr%d" % i for i in range(16)], ["cc%d" % (c // 2) if c % 2 else "ccb%d" % (c // 2)])
+
+    def lines(h):
+        hs, n, ls = slice(12 * h, 12 * h + 12), "%d" % h, slice(192 * h, 192 * h + 192)
+        ts(T.ni[:, hs], T.ki[:, hs], 8191, None, A.bitwise_and, None, ["ki" + n], ["ni" + n])
+        tc(T.nl[:, hs], T.ni[:, hs], ["ni" + n], ["nl" + n])
+        ts(T.f1[:, hs], T.ni[:, hs], 4096.0, -6143.0, A.is_ge, A.mult, ["ni" + n], ["f1" + n])
+        ts(T.f2[:, hs], T.ni[:, hs], 2.0, -4096.0, A.mult, A.add, ["ni" + n], ["f2" + n])
+        tc(T.nh[:, ls], T.hw[:].indirect(T.nl[:, hs]), ["hw", "hwb", "hwc", "nl" + n], ["nh" + n if h == 0 else "nh"])
+        tt(T.f3[:, hs], T.f1[:, hs], T.basev[:, hs], A.add, ["f1" + n, "basev"], ["f3" + n])
+        tt(T.ho[:, hs], T.f3[:, hs], T.f2[:, hs], A.add, ["f3" + n, "f2" + n], ["ho" + n if h == 0 else "ho"])
+
+    def send(s, to_buf):
+        def fn(e):
+            tr = []
+            nth = [0, 0]
+            for d in range(1, NR):
+                to = (rank + d) % NR
+                dst = T.cores[to]
+                rid, pid, _ = topo.addr(dst)
+                near = int(topo.die(dst) == topo.die(core))
+                k = 4 * nth[near] + near
+                nth[near] += 1
+                m = sum(1 << x for x in topo.engines(core, dst)[k:k + 3:2])
+                tr.append(RemoteDMATransfer(dst_ids=[DstId(rid=rid, pnc=pid)], dma_engine_mask=m, remote_sem=T.sem["arr%d" % s],
+                                            srcs=[T["sw%d" % s][:, PITCH * to + 1:PITCH * to + 1 + CAP]],
+                                            dsts=[T[to_buf][:, CAP * rank:CAP * (rank + 1)]]))
+            return e.remote_dma_fused(tr, local_sem=T.sem.sent)
+        return fn
+
+    for s in range(RO):
+        lk = "land%d" % s
+        lks = [lk, lk + "o"]
+        if s:
+            land = T[lk]
+            op("v", lambda e, land=land: e.transpose(T.tt[:], land[:]), lks, ["tt"])
+            ts(T.tqi[:], T.tt[:, 0::16], 1.0 / 512, -float(B * rank), A.mult, A.add, ["tt"], ["tqi"])
+            tc(T.tq[:], T.tqi[:], ["tqi"], ["tq"])
+            act(T.yy[:], land[:], F.Identity, lks, ["yy"], bias=BIG - B * rank, scale=1.0 / 512)
+            tc(T.li[:], land[:], lks, ["li"])
+        else:
+            mm(T.rb[:, 0:L], T.bo[:], T.w16[:], True, True, ["bo", "w16"], ["rb"])
+        for cc in range(2):
+            for k in range(2):
+                mm(T.cv[:, cc:24:2], T.dsb[:, 2 * cc + k, :], T.tq[:, (cc ^ k)::2], k == 0, k == 1, dsb + ["tq"], ["cv"])
+        tc(T.bl[:], T.cv[:, 0:24], [], ["cv", "bl"])
+        act(T.bf[:], T.cv[:, 0:24], F.Copy, [], ["cv", "bf"])
+        tc(T.q16[:], T.qw[:, 0:B + 16].indirect(T.bl[:]), ["qw", "qwp", "bl"], ["q16"])
+        ts(T.qf[:], T.q16[:], col(c_i13), None, A.add, None, ["q16", "c_i13"], ["qf"])
+        op("v", lambda e: e.transpose(T.qt[:], T.qf[:]), ["qf"], ["qt"])
+        for cc in range(2):
+            for j in range(2):
+                gx = 16 * (cc ^ j)
+                mm(T.k1[:, :, cc, :], T.dsf[:, 2 * cc + j, :], T.qt[:, :, gx:gx + 16], j == 0, j == 1, dsf + ["qt"], ["k1"])
+        if s:
+            ts(T.ci[:], T.li[:], 511, None, A.bitwise_and, None, ["li"], ["ci"])
+            tt(T.x1[:], T.vw[:, 0:B + 16].indirect(T.bl[:]), T.ci[:], A.subtract, ["vw", "vwp", "bl", "ci"], ["x1"])
+            ts(T.xx[:], T.x1[:], -255.0, None, A.max, None, ["x1"], ["xx"])
+        else:
+            act(T.xx[:], T.vw[:, 0:B + 16].indirect(T.bl[:]), F.Copy, ["vw", "vwp", "bl"], ["xx"])
+        k0 = NA // 4
+        for k in range(k0, 3):
+            mm(T.cv[:, 128 * (k + 1):128 * (k + 2)], T.xx[:, 128 * k:128 * (k + 1)], T.idb[:], True, True, ["xx", "idb"], ["cv"])
+        units = list(range(NA, 12))
+        gather(units[0])
+        gather(units[1])
+        act(T.xt[:, 128 * k0:L], T.cv[:, 128 * (k0 + 1):512], F.Copy, [], ["cv", "xt"])
+        if s:
+            ts(T.b16[:], T.yy[:], -BIG, None, A.add, None, ["yy"], ["b16"])
+        else:
+            tc(T.b16[:], T.rb[:, 0:L], [], ["rb", "b16"])
+        ts(T.ng[:], T.xx[:], 0.0, 64.0, A.is_lt, A.add, ["xx"], ["ng"])
+        compare(T.b16, T.bf, "b16", "bf")
+        for i in range(16):
+            ts(T.vr[:, i:512 * NA:16], T.xx[:, 0:32 * NA], -1.0, None, A.mult, None, ["xx"], ["vr%d" % i])
+        addv(units[0])
+        for k in range(2, len(units) + 2):
+            if k < len(units):
+                gather(units[k])
+            sign(units[k - 2])
+            if k - 1 < len(units):
+                addv(units[k - 1])
+            own_units(*C_OWN.get(k, (0, 0)))
+            if K_PAIRS <= k < K_PAIRS + N_PAIRS:
+                pairs(k - K_PAIRS, N_PAIRS)
+            if k == K_ND:
+                ts(T.rb[:, 0:L], T.rb[:, 0:L], col(c_sgn), 0.0, A.mult, A.is_lt, ["c_sgn"], ["rb"])
+                tt(T.wv[:], T.ng[:], T.rb[:, 0:L], A.mult, ["ng"], ["rb", "wv"])
+            if k == K_VAL:
+                spread(T.wv, "wv", 48)
+            if k == K_BASE:
+                ts(T.basev[:], T.cv[:, 48:72], 1024.5 * SC, 20000.0, A.is_lt, A.mult, [], ["cv", "basev"])
+                ts(T.e1[:], T.cv[:, 48:72], 0.5 * SC, None, A.is_lt, None, [], ["cv", "e1"])
+                tt(T.e2[:], T.e1[:], T.trv[:], A.mult, ["e1", "trv"], ["e2"])
+                tt(T.e3[:], T.e2[:], T.bf[:], A.max, ["e2", "bf"], ["e3"])
+                tc(T.ol[:], T.e3[:], ["e3"], ["ol"])
+            if k == K_SCORE:
+                for q in range(NA // 2):
+                    score(q)
+                tc(T.k1s[:], T.k1[:], [], ["k1", "k1s"])
+            if units[k - 2] % 2:
+                score(units[k - 2] // 2)
+            if k == K_BEST:
+                best(0)
+                lines(0)
+                compare(T.nh, T.ho, "nh", "ho", 0)
+        act(T.k1[:], T.xx[:], F.Relu, ["xx"], ["k1"], scale=-1.0)
+        best(1)
+        lines(1)
+        act(T.p0[:], T.pw[:, 0:W].indirect(T.nl[:]), F.Copy, ["pw15", "nl0", "nl1"], ["p0"], scale=512.0)
+        act(T.ag[:], T.aw[:, 0:W].indirect(T.nl[:]), F.Copy, ["aw", "nl0", "nl1"], ["ag"])
+        act(T.ab[:], T.p0[:], F.Abs, ["p0", "c_ctr"], ["ab"], bias=col(c_ctr), scale=1.0 / 512)
+        compare(T.nh, T.ho, "nh", "ho", 1)
+        pairs()
+        ts(T.th[:], T.ab[:], 1024.0, col(c_sub), A.is_lt, A.subtract, ["ab", "c_sub"], ["th"])
+        tt(T.k1[:], T.ag[:], T.k1[:], A.min, ["ag"], ["k1"])
+        tt(T.ps2[:, 0:L], T.rb[:, 0:L], T.th[:], A.is_lt, ["th"], ["rb", "ps2"])
+        op("v", lambda e: e.tensor_tensor_scan(T.st[:], T.ps2[:, 0:L], T.zb[:], col(c_ini), A.add, A.add), ["zb", "c_ini"], ["ps2", "st"])
+        tt(T.ss[:], T.st[:], T.ps2[:, 0:L], A.mult, ["st"], ["ps2", "ss"])
+        spread(T.ss, "ss", 24)
+        tt(T.pp[:], T.p0[:], T.k1[:], A.add, ["p0"], ["k1", "pp"])
+        ts(T.sl[:], T.cv[:, 24:48], 1.0 / SC, 1592.0, A.mult, A.add, [], ["cv", "sl"])
+        swk = ["sw%d_%d" % (s, d) for d in range(NR)]
+        tc(T["sw%d" % s][:].indirect(T.sl[:]), T.pp[:], ["sl", "pp"], swk)
+        nk = "land%d" % (s + 1)
+        op("p", send(s, nk), swk, [])
+        op("p", None, [], [nk], ext=("arr%d" % s, 2 * (NR - 1)))
+        if s < RO - 1:
+            act(T.g0[:], T.cv[:, 24:48], F.Sign, [], ["cv", "g0"], bias=-1600.0, scale=1.0 / SC)
+            act(T.g2[:], T.cv[:, 24:48], F.Copy, [], ["cv", "g2"], bias=4535.0, scale=1.0 / SC)
+            act(T.tn[:], T.k1[:], F.Copy, [], ["k1", "tn"], scale=-1.0)
+            act(T.g1[:], T.g0[:], F.Relu, ["g0"], ["g1"])
+            act(T.g4[:], T.g0[:], F.Relu, ["g0"], ["g4"], scale=16.0)
+        act(T.nd[:], T.rb[:, 0:L], F.Relu, ["c_sg2"], ["rb", "nd"], scale=col(c_sg2))
+        a0 = PITCH * rank + 1
+        act(T[nk][:, CAP * rank:CAP * (rank + 1)], T["sw%d" % s][:, a0:a0 + CAP], F.Copy, swk, [nk + "o"])
+        if s < RO - 1:
+            ts(T.ii[:], T.ki[:], 13, 15, A.arith_shift_right, A.bitwise_and, ["ki0", "ki1"], ["ii"])
+            tt(T.g3[:], T.g1[:], T.g2[:], A.mult, ["g1", "g2"], ["g3"])
+            tt(T.g5[:], T.g4[:], T.ii[:], A.add, ["g4", "ii"], ["g5"])
+            tc(T.il[:], T.g5[:], ["g5"], ["il"])
+            tt(T.qn[:], T.wn[:].indirect(T.il[:]), T.qf[:], A.max, ["wna", "wnb", "il", "qf"], ["qn"])
+            act(T.q2[:], T.qn[:], F.Identity, ["qn", "c_n13"], ["q2"], bias=col(c_n13))
+        tt(T.td[:], T.nd[:], T.k1[:], A.mult, ["nd"], ["k1", "td"])
+        if s < RO - 1:
+            tt(T.g6[:], T.g3[:], T.ni[:], A.max, ["g3", "ni0", "ni1"], ["g6"])
+            tc(T.qw[:].indirect(T.ol[:]), T.q2[:], ["ol", "q2"], ["qw", "qwp"])
+            tc(T.al[:], T.g6[:], ["g6"], ["al"])
+        tt(T.vw[:].indirect(T.ol[:]), T.xx[:], T.td[:], A.add, ["ol", "xx", "td"], ["vw", "vwp"])
+        if s < RO - 1:
+            tt(T.aw[:].indirect(T.al[:]), T.ag[:], T.tn[:], A.add, ["al", "ag", "tn"], ["aw"])
+        else:
+            op("s", lambda e: e.dma_start(T.yv[:], T.vw[:, 0:B]), ["vw"], ["yv"], dma=("dyv", 16))
+
+    lk = "land%d" % RO
+    lks = [lk, lk + "o"]
+    act(T.yy[:], T[lk][:], F.Identity, lks, ["yy"], bias=BIG - B * rank, scale=1.0 / 512)
+    act(T.x1[:], T.yy[:], F.Identity, ["yy"], ["x1"], bias=-BIG)
+    op("a", lambda e: e.dma_start(T.yw[:], T.x1[0::16, :]), ["x1"], ["yw"], dma=("dyw", 16))
+    tc(T.li[:], T[lk][:], lks, ["li"])
+    ts(T.ci[:], T.li[:], 511, None, A.bitwise_and, None, ["li"], ["ci"])
+    tc(T.cb[:], T.ci[:], ["ci"], ["cb"])
+    op("s", lambda e: e.dma_start(T.yc[:], T.cb[:]), ["cb"], ["yc"], dma=("dyc", 16))
+    emit()
+    g.wait_ge(T.sem.sent, 2 * (NR - 1) * RO)
+    for n in ("dyv", "dyw", "dyc", "dwk", "dvp", "dqu", "dam"):
+        g.wait_ge(T.sem[n], 16)
+    g.wait_ge(T.sem.dpay, 256)

@@ -6,119 +6,164 @@ F = ActivationFunctionType
 NR, B, W, CAP, RO = 8, 2048, 6144, 48, 3
 L = NR * CAP
 VW = 2560
-AW = 6544
+AW = 6640
 PITCH = 400
 SW = 3600
-BIG = 8388608.0
+PK = 1024
+MID = NR * B // 2
 SC = 131072.0
-NA = 4
-K_PAIRS, N_PAIRS, K_ND, K_VAL, K_BASE, K_SCORE, K_BEST = 2, 2, 3, 4, 5, 6, 7
-C_OWN = {2: (0, 4), 4: (4, 8)}
+OWN = [[8, 7, 6, 5, 4], [7, 6, 5], [7, 6, 5]]
+CHUNKS = [(12, 24), (4, 12), (0, 4)]
+KEYS = ["key1", "key0", "rb1"]
+CYC, WAKE, FLIGHT = 0.9e-3, 0.1, 2.8
+SWEEPS = 4
 
 SCRATCH = {
-    "vw": ("sbuf", [128, VW], "bfloat16"), "qw": ("sbuf", [128, VW], "int32"), "aw": ("sbuf", [128, AW], "bfloat16"),
-    "pw": ("sbuf", [128, W], "int32"), "hw": ("sbuf", [128, W], "float32"), "wn": ("sbuf", [128, 32], "float32"),
-    "cc": ("sbuf", [128, 24, 256], "bfloat16"), "gg": ("sbuf", [128, L * 16], "bfloat16"),
-    "vr": ("sbuf", [128, 3072], "bfloat16"), "ee": ("sbuf", [128, 24, L], "bfloat16"),
+    "vw": ("sbuf", [128, VW], "bfloat16"), "qi": ("sbuf", [128, B + 16], "int32"), "qw": ("sbuf", [128, VW], "float32"),
+    "aw": ("sbuf", [128, AW], "bfloat16"), "pw": ("sbuf", [128, W], "int32"), "hw": ("sbuf", [128, W], "float32"),
+    "wn": ("sbuf", [128, 32], "float32"), "cc": ("sbuf", [128, 24, 256], "bfloat16"), "gg": ("sbuf", [128, L * 16], "bfloat16"),
+    "vr": ("sbuf", [128, 2560], "bfloat16"), "ee": ("sbuf", [128, 24, L], "bfloat16"),
     "lm": ("sbuf", [128, 16, 128], "bfloat16"), "tm": ("sbuf", [128, 16, 128], "bfloat16"),
     "rm": ("sbuf", [128, 2048], "bfloat16"), "ir": ("sbuf", [128, 2048], "bfloat16"),
     "bo": ("sbuf", [128, 128], "bfloat16"), "bp": ("sbuf", [128, 128], "bfloat16"), "idb": ("sbuf", [128, 128], "bfloat16"),
-    "zb": ("sbuf", [128, L], "bfloat16"), "dsf": ("sbuf", [128, 4, 128], "float32"), "dsb": ("sbuf", [128, 4, 128], "bfloat16"),
+    "dg1": ("sbuf", [128, 128], "bfloat16"), "row8": ("sbuf", [128, 128], "bfloat16"),
+    "zb": ("sbuf", [128, L], "bfloat16"), "c32": ("sbuf", [128, L], "bfloat16"), "rowc": ("sbuf", [128, 192], "bfloat16"),
+    "rst": ("sbuf", [128, 192], "bfloat16"), "dsf": ("sbuf", [128, 4, 128], "float32"),
     "pi": ("sbuf", [128, 4], "int32"), "io128": ("sbuf", [128, 128], "bfloat16"), "iog": ("sbuf", [128, 128], "bfloat16"),
-    "io16": ("sbuf", [128, 16], "bfloat16"), "trv": ("sbuf", [128, 24], "float32"), "wc": ("sbuf", [128, 48], "float32"),
-    "col": ("sbuf", [128, 16], "float32"), "wkz": ("sbuf", [128, L], "int32"), "w16": ("sbuf", [128, L], "float16"),
-    "land1": ("sbuf", [128, L], "float32"), "land2": ("sbuf", [128, L], "float32"), "land3": ("sbuf", [128, L], "float32"),
-    "sw0": ("sbuf", [128, SW], "float32"), "sw1": ("sbuf", [128, SW], "float32"), "sw2": ("sbuf", [128, SW], "float32"),
-    "tt": ("sbuf", [128, L], "float32"), "tqi": ("sbuf", [128, 24], "int32"), "tq": ("sbuf", [128, 24], "float16"),
-    "bl": ("sbuf", [128, 24], "uint16"), "bf": ("sbuf", [128, 24], "float32"), "b16": ("sbuf", [128, L], "float16"),
-    "yy": ("sbuf", [128, L], "float32"), "li": ("sbuf", [128, L], "int32"), "ci": ("sbuf", [128, L], "int32"),
+    "io16": ("sbuf", [128, 16], "bfloat16"), "trv": ("sbuf", [128, 24], "float32"), "tra": ("sbuf", [128, 24], "float32"),
+    "wc": ("sbuf", [128, 48], "float32"), "col": ("sbuf", [128, 20], "float32"), "wkz": ("sbuf", [128, L], "int32"),
+    "land1": ("sbuf", [128, L], "int32"), "land2": ("sbuf", [128, L], "int32"), "land3": ("sbuf", [128, L], "int32"),
+    "sw0": ("sbuf", [128, SW], "int32"), "sw1": ("sbuf", [128, SW], "int32"), "sw2": ("sbuf", [128, SW], "int32"),
+    "bq": ("sbuf", [128, L], "float16"), "bl": ("sbuf", [128, 24], "uint16"), "bf": ("sbuf", [128, 24], "float32"),
+    "b16": ("sbuf", [128, L], "uint16"), "ci": ("sbuf", [128, L], "int32"), "yi": ("sbuf", [128, L], "int32"),
     "cb": ("sbuf", [128, L], "bfloat16"), "q16": ("sbuf", [128, L], "uint16"), "qf": ("sbuf", [128, L], "float32"),
-    "qt": ("sbuf", [128, 12, 32], "float32"), "k1s": ("sbuf", [128, 24, 16], "float32"), "kk": ("sbuf", [128, 24, 16], "float32"),
-    "t8": ("sbuf", [128, 24, 8], "float32"), "t4": ("sbuf", [128, 24, 4], "float32"), "t2": ("sbuf", [128, 24, 2], "float32"),
+    "qt": ("sbuf", [128, 12, 32], "float32"), "kk": ("sbuf", [128, L], "float32"),
     "ki": ("sbuf", [128, 24], "int32"), "ni": ("sbuf", [128, 24], "int32"), "ii": ("sbuf", [128, 24], "int32"),
     "nl": ("sbuf", [128, 24], "uint16"), "il": ("sbuf", [128, 24], "uint16"), "sl": ("sbuf", [128, 24], "uint16"),
     "ol": ("sbuf", [128, 24], "uint16"), "al": ("sbuf", [128, 24], "uint16"),
-    "f1": ("sbuf", [128, 24], "float32"), "f2": ("sbuf", [128, 24], "float32"), "f3": ("sbuf", [128, 24], "float32"),
     "e1": ("sbuf", [128, 24], "float32"), "e2": ("sbuf", [128, 24], "float32"), "e3": ("sbuf", [128, 24], "float32"),
-    "g0": ("sbuf", [128, 24], "float32"), "g1": ("sbuf", [128, 24], "float32"), "g2": ("sbuf", [128, 24], "float32"),
-    "g3": ("sbuf", [128, 24], "float32"), "g4": ("sbuf", [128, 24], "float32"), "g5": ("sbuf", [128, 24], "float32"),
-    "g6": ("sbuf", [128, 24], "float32"), "basev": ("sbuf", [128, 24], "float32"), "ho": ("sbuf", [128, 24], "float32"),
-    "x1": ("sbuf", [128, L], "float32"), "xx": ("sbuf", [128, L], "bfloat16"), "xt": ("sbuf", [128, L], "bfloat16"),
-    "ng": ("sbuf", [128, L], "bfloat16"), "nd": ("sbuf", [128, L], "bfloat16"), "wv": ("sbuf", [128, L], "bfloat16"),
-    "nh": ("sbuf", [128, L], "float16"), "ag": ("sbuf", [128, L], "bfloat16"), "p0": ("sbuf", [128, L], "float32"),
+    "g0": ("sbuf", [128, 24], "float32"), "g1": ("sbuf", [128, 24], "float32"), "g3": ("sbuf", [128, 24], "float32"),
+    "g5": ("sbuf", [128, 24], "float32"), "g6": ("sbuf", [128, 24], "float32"),
+    "basev": ("sbuf", [128, 24], "float32"), "ho": ("sbuf", [128, 24], "float32"),
+    "x1": ("sbuf", [128, L], "bfloat16"), "xx": ("sbuf", [128, L], "bfloat16"), "xt": ("sbuf", [128, L], "bfloat16"),
+    "nx": ("sbuf", [128, L], "bfloat16"), "wv": ("sbuf", [128, L], "bfloat16"),
+    "nh": ("sbuf", [128, L], "uint16"), "ag": ("sbuf", [128, L], "bfloat16"), "p0": ("sbuf", [128, L], "float32"),
     "ab": ("sbuf", [128, L], "float32"), "th": ("sbuf", [128, L], "bfloat16"), "tn": ("sbuf", [128, L], "bfloat16"),
     "td": ("sbuf", [128, L], "bfloat16"), "pp": ("sbuf", [128, L], "float32"), "st": ("sbuf", [128, L], "float32"),
-    "ss": ("sbuf", [128, L], "float16"), "qn": ("sbuf", [128, L], "float32"), "q2": ("sbuf", [128, L], "float32"),
+    "ss": ("sbuf", [128, L], "float16"), "mk": ("sbuf", [128, L], "float32"),
     "ps0": ("psum", [128, 512], "float32"), "ps1": ("psum", [128, 512], "float32"), "ps2": ("psum", [128, 512], "float32"),
-    "key0": ("psum", [128, 512], "float32"), "key1": ("psum", [128, 512], "float32"), "cv": ("psum", [128, 512], "float32"),
-    "rb": ("psum", [128, 512], "float32"), "k1": ("psum", [128, 12, 2, 16], "float32"),
+    "key0": ("psum", [128, 512], "float32"), "key1": ("psum", [128, 512], "float32"),
+    "bx": ("sbuf", [128, 24], "uint16"), "qx": ("sbuf", [128, L], "float32"),
+    "cv": ("psum", [128, 512], "float32"), "rb1": ("psum", [128, 512], "float32"), "rb5": ("psum", [128, 512], "float32"),
 }
+BANKS = [k for k, v in SCRATCH.items() if v[0] == "psum"]
 SEMAPHORES = ["qv", "qa", "qt", "qp", "dwk", "dvp", "dqu", "dam", "dpay", "dyv", "dyw", "dyc", "arr0", "arr1", "arr2", "sent"]
 
 
 def make_queues(g, T):
-    ops, last_w, readers = [], {}, {}
+    calls, last_w, readers = [], {}, {}
 
-    def op(q, fn, r=(), w=(), dma=None, ext=None):
+    def op(q, fn, r=(), w=(), us=0.1, dma=None, ext=None):
         deps = [(last_w[k], "raw") for k in r if k in last_w]
+        if q == "s":
+            deps += [(o["id"], "order") for o in calls if o["q"] == q][-1:]
         for k in w:
             if k in last_w:
                 deps.append((last_w[k], "waw"))
             deps += [(o, "war") for o in readers.get(k, ())]
-        i = len(ops)
-        ops.append({"q": q, "fn": fn, "deps": deps, "dma": dma, "ext": ext, "inc": False})
+        i = len(calls)
+        calls.append({"q": q, "fn": fn, "deps": deps, "dma": dma, "ext": ext, "inc": False, "us": us, "id": i})
         for k in w:
             last_w[k] = i
             readers[k] = []
         for k in r:
             readers.setdefault(k, []).append(i)
 
+    def free_edge(o, d, kind):
+        return d["q"] == o["q"] and o["dma"] is None and d["dma"] is None and d["ext"] is None and (kind == "war" or o["q"] == "t")
+
+    def order():
+        before, after = [[] for o in calls], [[] for o in calls]
+        for o in calls:
+            o["hold"] = 0.05 if o["dma"] else 0.0 if o["ext"] else o["us"]
+            for j, kind in o["deps"]:
+                lag = 0.05 - calls[j]["us"] if kind == "order" else 0.0 if free_edge(o, calls[j], kind) else WAKE
+                before[o["id"]].append((j, lag))
+                after[j].append((o["id"], lag))
+
+        def place(turn, edges, back):
+            end, busy = {}, {q: [] for q in "vatps"}
+            for i in turn:
+                o = calls[i]
+                skip = o["us"] - o["hold"] if back else 0.0
+                t = max([end[j] + lag for j, lag in edges[i]] + [0.0]) + skip
+                row, k = busy[o["q"]], 0
+                for k in range(len(row) + 1):
+                    if k == len(row) or row[k][0] >= t + o["hold"]:
+                        break
+                    t = max(t, row[k][1])
+                row.insert(k, (t, t + o["hold"]))
+                end[i] = t - skip + o["us"]
+            return end
+
+        turn, best = list(range(len(calls))), None
+        for sweep in range(SWEEPS):
+            end = place(turn, before, False)
+            if best is None or max(end.values()) < max(best.values()):
+                best = end
+            end = place(sorted(turn, key=lambda i: (-end[i] + calls[i]["us"] - calls[i]["hold"], -i)), after, True)
+            turn = sorted(turn, key=lambda i: (-end[i], i))
+        return [calls[i] for i in sorted(turn, key=lambda i: (best[i] - calls[i]["us"], i))]
+
     def emit():
         engine = {"v": g.vector, "a": g.scalar, "t": g.tensor, "p": g, "s": g.sync}
         sem = {"v": T.sem.qv, "a": T.sem.qa, "t": T.sem.qt, "p": T.sem.qp}
         known = {q: {} for q in engine}
         seq = {q: 0 for q in engine}
-        waits = []
+        ops = order()
         for o in ops:
             o["seq"] = seq[o["q"]]
-            if o["ext"] is None:
-                seq[o["q"]] += 1
+            o["waits"] = []
+            o["clock"] = {}
+            if o["ext"] is not None:
+                continue
+            seq[o["q"]] += 1
             need = {}
             kn = known[o["q"]]
             for j, kind in o["deps"]:
-                d = ops[j]
+                d = calls[j]
+                if kind == "order":
+                    continue
                 if d["ext"] is not None or d["dma"] is not None:
                     name = d["ext"] or d["dma"]
                     if kn.get(name[0], 0) < name[1]:
                         need[name[0]] = (max(need.get(name[0], (0, 0))[0], name[1]), j)
                     continue
-                if d["q"] == o["q"] and o["dma"] is None and (kind == "war" or o["q"] == "t"):
+                if free_edge(o, d, kind):
                     continue
                 if kn.get(d["q"], -1) < d["seq"] and need.get(d["q"], (-1, 0))[0] < d["seq"]:
                     need[d["q"]] = (d["seq"], j)
             for key, (val, j) in need.items():
-                for k2, v2 in ops[j]["clock"].items():
+                for k2, v2 in calls[j]["clock"].items():
                     if k2 != key and kn.get(k2, -1) < v2:
                         kn[k2] = v2
-            final = []
             for key, (val, j) in need.items():
-                if not any(k2 != key and ops[j2]["clock"].get(key, -1) >= val for k2, (v2, j2) in need.items()):
-                    final.append((key, val, j))
+                if not any(k2 != key and calls[j2]["clock"].get(key, -1) >= val for k2, (v2, j2) in need.items()):
+                    o["waits"].append((key, val, j))
                     if key in sem:
-                        ops[j]["inc"] = True
+                        calls[j]["inc"] = True
                 kn[key] = max(kn.get(key, -1), val)
             o["clock"] = dict(kn)
-            waits.append(final)
         count = {q: 0 for q in engine}
         for o in ops:
             count[o["q"]] += 1 if o["inc"] else 0
             o["count"] = count[o["q"]]
-        for i, o in enumerate(ops):
+        for o in ops:
             if o["ext"] is not None:
                 continue
             e = engine[o["q"]]
-            for key, val, j in waits[i]:
-                e.wait_ge(sem[key] if key in sem else T.sem[key], ops[j]["count"] if key in sem else val)
+            for key, val, j in o["waits"]:
+                e.wait_ge(sem[key] if key in sem else T.sem[key], calls[j]["count"] if key in sem else val)
             ins = o["fn"](e)
             if o["dma"] is not None:
                 ins.then_inc(T.sem[o["dma"][0]], 16)
@@ -135,171 +180,204 @@ def rank_program(g, core, T, topo):
     if rank is None:
         return
     op, emit = make_queues(g, T)
-    c_m, c_g, c_p, c_x, c_h0, c_h1, c_ctr, c_sub, c_sgn, c_ini, c_i13, c_n13, c_wn, c_t, c_sg2 = range(15)
+    c_m, c_g, c_p, c_x, c_h0, c_h1, c_ctr, c_sgn, c_ini, c_lt8, c_ts, c_tb, c_d1, c_d5, c_sc = range(15)
 
     def col(k):
         return T.col[:, k:k + 1]
 
+    def size(ap):
+        n = 1
+        for k in ap.shape[1:]:
+            n *= k
+        return n
+
+    def ind(win, off):
+        return (win.indirect(off), 16 * size(off))
+
+    def length(out, in_, cycles, *others):
+        if isinstance(out, tuple):
+            return 0.055 + out[1] * 3.8 * CYC, out[0], in_
+        if isinstance(in_, tuple):
+            return 0.06 + in_[1] * 1.56 * CYC, out, in_[0]
+        if cycles is None:
+            cycles = 0.5 if all("16" in str(x.dtype) for x in (out, in_) + others) else 1.0
+        return 0.055 + size(out) * cycles * CYC, out, in_
+
     def ts(out, in0, s1, s2, o0, o1, r, w):
-        op("v", (lambda e: e.tensor_scalar(out, in0, s1, s2, o0, o1)) if o1 else (lambda e: e.tensor_scalar(out, in0, s1, None, o0)), r, w)
+        us, out, in0 = length(out, in0, None)
+        op("v", (lambda e: e.tensor_scalar(out, in0, s1, s2, o0, o1)) if o1 else (lambda e: e.tensor_scalar(out, in0, s1, None, o0)), r, w, us)
 
     def tt(out, in0, in1, o, r, w):
-        op("v", lambda e: e.tensor_tensor(out, in0, in1, o), r, w)
+        us, out, in0 = length(out, in0, 1.0 if any(k in BANKS for k in w) else 2.0)
+        op("v", lambda e: e.tensor_tensor(out, in0, in1, o), r, w, us)
 
     def tc(out, in_, r, w):
-        op("v", lambda e: e.tensor_copy(out, in_), r, w)
+        us, out, in_ = length(out, in_, None)
+        op("v", lambda e: e.tensor_copy(out, in_), r, w, us)
+
+    def scan(out, d0, d1, ini, o0, o1, r, w):
+        op("v", lambda e: e.tensor_tensor_scan(out, d0, d1, ini, o0, o1), r, w, length(out, d0, None, d1)[0])
 
     def fill(out, k, w):
-        op("v", lambda e: e.memset(out, k), [], w)
+        op("v", lambda e: e.memset(out, k), [], w, length(out, out, None)[0])
 
     def act(out, in_, f, r, w, bias=0.0, scale=1.0):
-        op("a", lambda e: e.activation(out, in_, f, bias=bias, scale=scale), r, w)
+        us, out, in_ = length(out, in_, 1.0)
+        op("a", lambda e: e.activation(out, in_, f, bias=bias, scale=scale), r, w, us)
 
     def mm(out, lhs, rhs, start, stop, r, w):
-        op("t", lambda e: e.matmul(out, lhs, rhs, start, stop), r, w)
+        op("t", lambda e: e.matmul(out, lhs, rhs, start, stop), r, w, max(64, size(rhs)) * (2.0 if "32" in str(rhs.dtype) else 0.5) * CYC)
 
     def iota(out, pattern, base, cm, w):
-        op("p", lambda e: e.iota(out, pattern, base, cm, allow_small_or_imprecise_dtypes=True), [], w)
+        op("p", lambda e: e.iota(out, pattern, base, cm, allow_small_or_imprecise_dtypes=True), [], w, 0.14 + 2 * size(out) * CYC)
+
+    def pcopy(out, in_, n, r, w):
+        op("p", lambda e: e.affine_select(out, in_, [[0, n]], A.is_ge, 0.0, 0, 0), r, w, 0.19 + 2 * size(out) * CYC)
 
     fill(T.wkz[:], 0, ["wkz"])
-    op("s", lambda e: e.dma_start(T.wkz[0::16, :], T.wk[:]), [], ["wkz"], dma=("dwk", 16))
-    op("s", lambda e: e.dma_start(T.qw[:, 0:B], T.qu[:]), [], ["qw"], dma=("dqu", 16))
-    op("a", lambda e: e.dma_start(T.vw[:, 0:B], T.vp[:]), [], ["vw"], dma=("dvp", 16))
-    op("s", lambda e: e.dma_start(T.aw[:, 0:W], T.am[:]), [], ["aw"], dma=("dam", 16))
+    op("s", lambda e: e.dma_start(T.vw[:, 0:B], T.vp[:]), [], ["vw"], 3.7, dma=("dvp", 16))
+    op("s", lambda e: e.dma_start(T.wkz[0::16, :], T.wk[:]), [], ["wkz"], 3.2, dma=("dwk", 16))
+    op("s", lambda e: e.dma_start(T.qi[:, 0:B], T.qu[:]), [], ["qi"], 7.4, dma=("dqu", 16))
+    op("s", lambda e: e.dma_start(T.aw[:, 0:W], T.am[:]), [], ["aw"], 13.4, dma=("dam", 16))
     for j in range(16):
-        op("s", lambda e, j=j: e.dma_start(T.pw[j::16, :], T.pay[:]), ["aw"] if j == 0 else [], ["pw%d" % j], dma=("dpay", 256))
+        op("s", lambda e, j=j: e.dma_start(T.pw[j::16, :], T.pay[:]), ["aw"], ["pw%d" % j], 12.0, dma=("dpay", 256))
 
-    op("p", lambda e: e.iota(T.pi[:, 0:1], [[1, 1]], 0, 1), [], ["pi0"])
+    op("p", lambda e: e.iota(T.pi[:, 0:1], [[1, 1]], 0, 1), [], ["pi0"], 0.14)
     iota(T.iog[:], [[1, 8], [0, 16]], 0, 0, ["iog"])
     iota(T.io128[:], [[1, 128]], 0, 0, ["io128"])
     iota(T.io16[:], [[1, 16]], 0, 0, ["io16"])
+    iota(T.rowc[:], [[0, 12], [8192, 16]], 0, 0, ["rowc"])
     iota(T.trv[:], [[16, 24]], 2064, 1, ["trv"])
     iota(T.ir[:], [[1, 128], [0, 16]], 0, 0, ["ir"])
-    iota(T.hw[:, 0:4096], [[2, 4096]], -4096, 0, ["hw"])
-    iota(T.hw[:, 4096:W - 1], [[2, W - 1 - 4096]], -2047, 0, ["hwb"])
-    iota(T.hw[:, W - 1:W], [[1, 1]], 5000, 0, ["hwc"])
+    iota(T.hw[:, 0:W - 1], [[1, W - 1]], 0, 0, ["hw"])
+    iota(T.hw[:, W - 1:W], [[1, 1]], 60000, 0, ["hwc"])
     for s in range(RO):
         for d in range(NR):
             a0 = PITCH * d + 1
-            iota(T["sw%d" % s][:, a0:a0 + CAP], [[0, CAP]], (d * B + B) * 512, 0, ["sw%d_%d" % (s, d)])
-    fill(T.vw[:, B:B + 16], 0.0, ["vwp"])
-    fill(T.qw[:, B:B + 16], W - 1, ["qwp"])
-    fill(T.zb[:], 0.0, ["zb"])
+            op("p", lambda e, s=s, d=d, a0=a0: e.iota(T["sw%d" % s][:, a0:a0 + CAP], [[0, CAP]], (d * B + B - MID) * PK, 0),
+               ["hw"], ["sw%d_%d" % (s, d)], 0.23)
     fill(T.lm[:], 0.0, ["lm0"])
-    fill(T.wn[:, 16:32], 0.0, ["wnb"])
     ts(T.pi[:, 1:2], T.pi[:, 0:1], 15, None, A.bitwise_and, None, ["pi0"], ["pi1"])
     ts(T.pi[:, 2:3], T.pi[:, 0:1], 4, None, A.arith_shift_right, None, ["pi0"], ["pi2"])
     ts(T.pi[:, 3:4], T.pi[:, 0:1], 4, 1, A.arith_shift_right, A.bitwise_and, ["pi0"], ["pi3"])
     tc(col(c_p), T.pi[:, 0:1], ["pi0"], ["c_p"])
-    tc(col(c_m), T.pi[:, 1:2], ["pi1"], ["c_m"])
     tc(col(c_g), T.pi[:, 2:3], ["pi2"], ["c_g"])
+    tc(col(c_m), T.pi[:, 1:2], ["pi1"], ["c_m"])
     tc(col(c_h1), T.pi[:, 3:4], ["pi3"], ["c_h1"])
+    ts(T.bo[:], T.iog[:], col(c_g), None, A.is_equal, None, ["iog", "c_g"], ["bo"])
+    for a in range(16):
+        act(T.lm[:, a, a::16], T.bo[:, 0::16], F.Copy, ["bo", "lm0"], ["lm%d" % (a + 1)], scale=SC)
+    fill(T.vw[:, B:B + 16], 0.0, ["vwp"])
+    fill(T.qw[:, B:B + 16], W - 1.0, ["qwp"])
+    fill(T.qi[:, B:B + 16], W - 1, ["qip"])
+    ts(col(c_sgn), col(c_m), 8.0, -2.0, A.is_equal, A.mult, ["c_m"], ["c_sgn0"])
     ts(col(c_h0), col(c_h1), -1.0, 1.0, A.mult, A.add, ["c_h1"], ["c_h0"])
     ts(col(c_x), col(c_h1), -32.0, 16.0, A.mult, A.add, ["c_h1"], ["c_x0"])
-    ts(T.bo[:], T.iog[:], col(c_g), None, A.is_equal, None, ["iog", "c_g"], ["bo"])
-    tt(col(c_x), col(c_x), col(c_p), A.add, ["c_x0", "c_p"], ["c_x"])
-    for k, (pc, hc) in enumerate(((c_p, c_h0), (c_x, c_h0), (c_p, c_h1), (c_x, c_h1))):
-        ts(T.dsf[:, k, :], T.io128[:], col(pc), col(hc), A.is_equal, A.mult, ["io128", "c_p", "c_x", "c_h0", "c_h1"], ["dsf%d" % k])
-    for k in range(4):
-        tc(T.dsb[:, k, :], T.dsf[:, k, :], ["dsf%d" % k], ["dsb%d" % k])
-    dsf = ["dsf%d" % k for k in range(4)]
-    dsb = ["dsb%d" % k for k in range(4)]
-    ts(T.idb[:], T.io128[:], col(c_p), None, A.is_equal, None, ["io128", "c_p"], ["idb"])
-    for a in range(16):
-        ts(T.lm[:, a, a::16], T.bo[:, 0::16], SC, None, A.mult, None, ["bo", "lm0"], ["lm%d" % (a + 1)])
-    ts(col(c_i13), col(c_m), 8192.0, None, A.mult, None, ["c_m"], ["c_i13"])
-    ts(col(c_n13), col(c_m), -8192.0, None, A.mult, None, ["c_m"], ["c_n13"])
-    ts(col(c_wn), col(c_m), 8192.0, float(W - 1), A.mult, A.add, ["c_m"], ["c_wn"])
-    ts(col(c_ctr), col(c_m), -2048.0, -1023.5, A.mult, A.add, ["c_m"], ["c_ctr"])
-    ts(col(c_ini), col(c_m), float(PITCH), -1592.0, A.mult, A.add, ["c_m"], ["c_ini"])
-    ts(col(c_sgn), col(c_m), 8.0, -2.0, A.is_equal, A.mult, ["c_m"], ["c_sgn0"])
-    ts(col(c_t), col(c_m), 8.0, 999.0, A.is_gt, A.mult, ["c_m"], ["c_t"])
-    ts(col(c_sub), col(c_m), 8.0, -1.25, A.is_equal, A.mult, ["c_m"], ["c_sub0"])
     ts(T.wc[:, 0:16], T.io16[:], col(c_m), None, A.is_gt, None, ["io16", "c_m"], ["wc0"])
     ts(T.wc[:, 16:32], T.io16[:], col(c_m), -0.5, A.is_equal, A.mult, ["io16", "c_m"], ["wc1"])
-    tc(T.bp[:], T.bo[:], ["bo"], ["bp0"])
-    ts(T.wn[:, 0:16], T.io16[:], col(c_m), col(c_wn), A.is_equal, A.mult, ["io16", "c_m", "c_wn"], ["wna"])
+    ts(T.bp[:], T.bo[:], 4.0, None, A.mult, None, ["bo"], ["bp0"])
     ts(col(c_sgn), col(c_sgn), 1.0, None, A.add, None, ["c_sgn0"], ["c_sgn"])
-    ts(col(c_sg2), col(c_sgn), -2.0, None, A.mult, None, ["c_sgn"], ["c_sg2"])
-    tt(col(c_sub), col(c_sub), col(c_t), A.add, ["c_sub0", "c_t"], ["c_sub1"])
+    tt(col(c_x), col(c_x), col(c_p), A.add, ["c_x0", "c_p"], ["c_x"])
     tt(T.wc[:, 32:48], T.wc[:, 0:16], T.wc[:, 16:32], A.add, ["wc0", "wc1"], ["wc"])
-    ts(T.bp[:, 8::16], T.bo[:, 8::16], -1.0, None, A.mult, None, ["bo", "bp0"], ["bp"])
-    ts(col(c_sub), col(c_sub), 1.0, None, A.add, None, ["c_sub1"], ["c_sub"])
+    ts(T.bp[:, 8::16], T.bo[:, 8::16], -4.0, None, A.mult, None, ["bo", "bp0"], ["bp"])
+    ts(T.idb[:], T.io128[:], col(c_p), None, A.is_equal, None, ["io128", "c_p"], ["idb"])
+    ts(col(c_d5), col(c_m), 8.0, None, A.is_equal, None, ["c_m"], ["c_d5"])
+    ts(col(c_d1), col(c_sgn), -1.0 / 256, None, A.mult, None, ["c_sgn"], ["c_d1"])
+    ts(col(c_sc), col(c_sgn), -256.0, None, A.mult, None, ["c_sgn"], ["c_sc"])
     for a in range(16):
-        ts(T.tm[:, a, :], T.bp[:], T.wc[:, 32 + a:33 + a], None, A.mult, None, ["bp", "wc"], ["tm%d" % a])
+        act(T.tm[:, a, :], T.bp[:], F.Copy, ["bp", "wc"], ["tm%d" % a], scale=T.wc[:, 32 + a:33 + a])
+    fill(T.c32[:], 1.0 / 32, ["c32"])
+    ts(T.dg1[:], T.io128[:], col(c_p), col(c_d1), A.is_equal, A.mult, ["io128", "c_p", "c_d1"], ["dg1"])
+    for k, (pc, hc) in enumerate(((c_p, c_h0), (c_x, c_h0), (c_p, c_h1), (c_x, c_h1))):
+        ts(T.dsf[:, k, :], T.io128[:], col(pc), col(hc), A.is_equal, A.mult, ["io128", "c_p", "c_x", "c_h0", "c_h1"], ["dsf%d" % k])
     ts(T.rm[:], T.ir[:], col(c_p), None, A.is_equal, None, ["ir", "c_p"], ["rm"])
-    tc(T.w16[:], T.wkz[:], ["wkz"], ["w16"])
-    tc(T.tt[:], T.wkz[:], ["wkz"], ["tt"])
-    op("v", lambda e: e.transpose(T.yy[:], T.tt[:]), ["tt"], ["yy"])
-    tc(T.tq[:], T.yy[:, 0::16], ["yy"], ["tq"])
+    fill(T.zb[:], 0.0, ["zb"])
+    fill(T.rst[:], 0.0, ["rst0"])
+    fill(T.wn[:, 16:32], 0.0, ["wnb"])
+    ts(T.row8[:], T.bo[:], col(c_d5), None, A.mult, None, ["bo", "c_d5"], ["row8"])
+    ts(col(c_ctr), col(c_m), -2048.0, MID - 1023.5, A.mult, A.add, ["c_m"], ["c_ctr"])
+    ts(col(c_ini), col(c_m), float(PITCH), -1592.0, A.mult, A.add, ["c_m"], ["c_ini"])
+    ts(col(c_ts), col(c_m), 8.0, -1.0, A.is_lt, A.mult, ["c_m"], ["c_ts"])
+    ts(col(c_lt8), col(c_m), 8.0, 1025.0, A.is_lt, A.mult, ["c_m"], ["c_lt8"])
+    ts(T.wn[:, 0:16], T.io16[:], col(c_m), float(W - 1), A.is_equal, A.mult, ["io16", "c_m"], ["wna"])
+    ts(T.tra[:], T.trv[:], 1.0 / 16, (W - 2064.0) / 16, A.mult, A.add, ["trv"], ["tra"])
+    fill(T.rst[:, 0::16], -16777216.0, ["rst0"])
+    ts(col(c_tb), col(c_lt8), -1.0, None, A.add, None, ["c_lt8"], ["c_tb"])
 
     lms = ["lm%d" % a for a in range(17)]
     tms = ["tm%d" % a for a in range(16)]
-    ees = ["ee%d" % c for c in range(24)] + ["ee%dx" % c for c in range(12)]
+    ees = ["ee%d" % c for c in range(24)]
+    dsf = ["dsf%d" % k for k in range(4)]
 
-    def compare(buf, own, key, own_key, h=None):
-        for c in range(12 if h == 0 else 24):
-            lo = 192 if h == 1 and c < 12 else 16 * c
-            hi = 192 if h == 0 else L
-            ts(T.ee[:, c, lo - 16 * c:hi - 16 * c], buf[:, lo:hi], own[:, c:c + 1], None, A.is_equal, None,
-               [key + "0" if h is not None else key, own_key + "0" if c < 12 and h is not None else own_key] + ([key] if h == 1 else []),
-               ["ee%d%s" % (c, "x" if h == 0 else "")])
+    def pairs(rb, buf, own, r, c0, c1):
+        if c1 == 24:
+            mm(T[rb][:, 0:L], T.bp[:], T.c32[:], True, False, ["bp", "c32"], [rb])
+        for c in range(c1 - 1, c0 - 1, -1):
+            ts(T.ee[:, c, 0:L - 16 * c], buf[:, 16 * c:L], own[:, c:c + 1], None, A.is_equal, None, r, ["ee%d" % c])
+            if c < 23:
+                mm(T[rb][:, 16 * (c + 1):L], T.bp[:], T.ee[:, c, 16:L - 16 * c], False, False, ["bp", "ee%d" % c], [rb])
+        if c0 == 0:
+            for a in range(16):
+                mm(T[rb][:, a:L:16], T.tm[:, a, :], T.ee[:, :, a], False, a == 15, tms + ees, [rb])
 
-    def pairs(part=0, parts=1):
-        calls = [lambda: mm(T.rb[:, 0:L], T.lm[:, 15, :], T.zb[:], True, False, lms + ["zb"], ["rb"])]
-        for c in range(23):
-            calls.append(lambda c=c: mm(T.rb[:, 16 * (c + 1):L], T.bp[:], T.ee[:, c, 16:L - 16 * c], False, False,
-                                        ["bp", "ee%d" % c] + (["ee%dx" % c] if c < 12 else []), ["rb"]))
+    def spread(src, keys, c0):
         for a in range(16):
-            calls.append(lambda a=a: mm(T.rb[:, a:L:16], T.tm[:, a, :], T.ee[:, :, a], False, a == 15, tms + ees, ["rb"]))
-        n = len(calls)
-        for f in calls[n * part // parts:n * (part + 1) // parts]:
-            f()
+            mm(T.cv[:, c0:c0 + 24], T.lm[:, a, :], src[:, a::16], a == 0, a == 15, lms + keys, ["cv"])
 
-    def spread(src, key, c0):
-        for a in range(16):
-            mm(T.cv[:, c0:c0 + 24], T.lm[:, a, :], src[:, a::16], a == 0, a == 15, lms + [key], ["cv"])
-
-    def gather(u):
-        act(T.gg[:, 512 * u:512 * (u + 1)], T.aw[:, 0:W].indirect(T.q16[:, 32 * u:32 * (u + 1)]), F.Copy, ["aw", "q16"], ["gg%d" % u])
-
-    def addv(u):
-        pk = "ps%d" % (u % 3)
+    def scalar_unit(u, pk):
+        act(T.gg[:, 512 * u:512 * (u + 1)], ind(T.aw[:, 0:W], T.q16[:, 32 * u:32 * (u + 1)]), F.Copy, ["aw", "q16"], ["gg%d" % u])
         mm(T[pk][:], T.idb[:], T.gg[:, 512 * u:512 * (u + 1)], True, False, ["idb", "gg%d" % u], [pk])
         mm(T[pk][:], T.xt[:, 128 * (u // 4):128 * (u // 4 + 1)], T.rm[:, 512 * (u % 4):512 * (u % 4 + 1)], False, True, ["xt", "rm"], [pk])
+        act(T.cc[:, 2 * u:2 * u + 2, :], T[pk][:], F.Sign, [], [pk, "cc%d" % (2 * u), "cc%d" % (2 * u + 1)], bias=0.5)
 
-    def sign(u):
-        pk = "ps%d" % (u % 3)
-        act(T.cc[:, 2 * u:2 * u + 2, :], T[pk][:], F.Sign, [], [pk, "cc%d" % u, "ccb%d" % u], bias=0.5)
+    def vector_unit(u, u0):
+        for c in (2 * u + 1, 2 * u):
+            tt(T.cc[:, c, :], ind(T.aw[:, 0:W], T.q16[:, 16 * c:16 * (c + 1)]), T.vr[:, 256 * (c - 2 * u0):256 * (c - 2 * u0 + 1)],
+               A.is_ge, ["aw", "q16", "vr%d" % u], ["cc%d" % c])
 
-    def score(q):
-        kb, off = "key%d" % (q // 3), 64 * (q % 3)
+    def repeat(copy, units, u0):
+        lo, hi, keys = 512 * (units[-1] - u0), 512 * (units[0] - u0 + 1), ["vr%d" % u for u in units]
+        for i in (0, 8):
+            copy(T.vr[:, lo + i:hi:16], T.nx[:, 32 * units[-1]:32 * units[0] + 32], (hi - lo) // 16, ["nx"], [k + "_%d" % i for k in keys])
+        for k in (8, 4, 2):
+            copy(T.vr[:, lo + k // 2:hi:k], T.vr[:, lo:hi:k], (hi - lo) // k, [x + y for x in keys for y in ("_0", "_8")], keys)
+
+    def score(q, n):
+        kb, off = KEYS[n], 64 * q - 16 * CHUNKS[n][0]
         for a in range(16):
-            mm(T[kb][:, off:off + 64], T.lm[:, a, :], T.cc[:, 4 * q:4 * q + 4, 16 * a:16 * a + 16], a == 0, a == 15,
-               lms + ["cc%d" % (2 * q), "cc%d" % (2 * q + 1), "ccb%d" % (2 * q), "ccb%d" % (2 * q + 1)], [kb])
+            mm(T[kb][:, off:off + 64], T.lm[:, a, :], T.cc[:, 4 * q:4 * q + 4, 16 * a:16 * a + 16], False, a == 15 and off == 0,
+               lms + ["cc%d" % c for c in range(4 * q, 4 * q + 4)], [kb])
 
-    def best(h):
-        kb, hs, n = "key%d" % h, slice(12 * h, 12 * h + 12), "%d" % h
-        tt(T.kk[:, hs, :], T[kb][:, 0:192], T.k1s[:, hs, :], A.add, ["k1s"], [kb, "kk" + n])
-        tt(T.t8[:, hs, :], T.kk[:, hs, 0:8], T.kk[:, hs, 8:16], A.max, ["kk" + n], ["t8" + n])
-        tt(T.t4[:, hs, :], T.t8[:, hs, 0:4], T.t8[:, hs, 4:8], A.max, ["t8" + n], ["t4" + n])
-        tt(T.t2[:, hs, :], T.t4[:, hs, 0:2], T.t4[:, hs, 2:4], A.max, ["t4" + n], ["t2" + n])
-        tt(T.ki[:, hs], T.t2[:, hs, 0], T.t2[:, hs, 1], A.max, ["t2" + n], ["ki" + n])
+    def queue_keys(n):
+        (c0, c1), kb = CHUNKS[n], KEYS[n]
+        h = c0 // 12
+        mm(T[kb][:, 0:16 * (c1 - c0)], T.idb[:], T.rowc[:, 0:16 * (c1 - c0)], True, False, ["idb", "rowc"], [kb])
+        for j in range(2):
+            gx = 16 * (h ^ j)
+            mm(T[kb][:, 0:16 * (c1 - c0)], T.dsf[:, 2 * h + j, :], T.qt[:, c0 - 12 * h:c1 - 12 * h, gx:gx + 16], False, False, dsf + ["qt"], [kb])
 
-    def own_units(c0, c1):
-        for c in range(c0, c1):
-            tt(T.cc[:, c, :], T.aw[:, 0:W].indirect(T.q16[:, 16 * c:16 * c + 16]), T.vr[:, 256 * c:256 * c + 256], A.is_ge,
-               ["aw", "q16"] + ["vr%d" % i for i in range(16)], ["cc%d" % (c // 2) if c % 2 else "ccb%d" % (c // 2)])
+    def best(n):
+        c0, c1 = CHUNKS[n]
+        kb, hs, ls, k = KEYS[n], slice(c0, c1), slice(16 * c0, 16 * c1), "%d" % n
+        for q in range(c1 // 4 - 1, c0 // 4 - 1, -1):
+            score(q, n)
+        scan(T.kk[:, ls], T.rst[:, 0:16 * (c1 - c0)], T[kb][:, 0:16 * (c1 - c0)], 0.0, A.add, A.max, ["rst0"], [kb, "kk" + k])
+        tc(T.ki[:, hs], T.kk[:, 16 * c0 + 15:16 * c1:16], ["kk" + k], ["ki" + k])
+        ts(T.ni[:, hs], T.ki[:, hs], 8191, None, A.bitwise_and, None, ["ki" + k], ["ni" + k])
+        tc(T.nl[:, hs], T.ni[:, hs], ["ni" + k], ["nl" + k])
+        tt(T.ho[:, hs], T.ni[:, hs], T.basev[:, hs], A.add, ["ni" + k, "basev"], ["ho" + k])
+        tc(T.nh[:, ls], ind(T.hw[:], T.nl[:, hs]), ["hw", "hwc", "nl" + k], ["nh" + k])
+        pairs("rb5", T.nh, T.ho, ["nh%d" % i for i in range(n + 1)] + ["ho" + k], c0, c1)
 
-    def lines(h):
-        hs, n, ls = slice(12 * h, 12 * h + 12), "%d" % h, slice(192 * h, 192 * h + 192)
-        ts(T.ni[:, hs], T.ki[:, hs], 8191, None, A.bitwise_and, None, ["ki" + n], ["ni" + n])
-        tc(T.nl[:, hs], T.ni[:, hs], ["ni" + n], ["nl" + n])
-        ts(T.f1[:, hs], T.ni[:, hs], 4096.0, -6143.0, A.is_ge, A.mult, ["ni" + n], ["f1" + n])
-        ts(T.f2[:, hs], T.ni[:, hs], 2.0, -4096.0, A.mult, A.add, ["ni" + n], ["f2" + n])
-        tc(T.nh[:, ls], T.hw[:].indirect(T.nl[:, hs]), ["hw", "hwb", "hwc", "nl" + n], ["nh" + n if h == 0 else "nh"])
-        tt(T.f3[:, hs], T.f1[:, hs], T.basev[:, hs], A.add, ["f1" + n, "basev"], ["f3" + n])
-        tt(T.ho[:, hs], T.f3[:, hs], T.f2[:, hs], A.add, ["f3" + n, "f2" + n], ["ho" + n if h == 0 else "ho"])
+    def of_lines(c0, c1, nls, k):
+        hs, ls = slice(c0, c1), slice(16 * c0, 16 * c1)
+        act(T.p0[:, ls], ind(T.pw[:, 0:W], T.nl[:, hs]), F.Copy, ["pw15"] + nls, ["p0" + k], bias=-float(MID * PK), scale=float(PK))
+        act(T.ab[:, ls], T.p0[:, ls], F.Abs, ["p0" + k, "c_ctr"], ["ab" + k], bias=col(c_ctr), scale=1.0 / PK)
+        act(T.th[:, ls], T.ab[:, ls], F.Sign, ["ab" + k, "c_ts", "c_tb"], ["th" + k], bias=col(c_tb), scale=col(c_ts))
+        act(T.ag[:, ls], ind(T.aw[:, 0:W], T.nl[:, hs]), F.Copy, ["aw"] + nls, ["ag" + k])
+
+    def put_positions():
+        tt(ind(T.vw[:], T.ol[:]), T.xx[:], T.td[:], A.add, ["ol", "xx", "td"], ["vw", "vwp"])
 
     def send(s, to_buf):
         def fn(e):
@@ -319,139 +397,113 @@ def rank_program(g, core, T, topo):
             return e.remote_dma_fused(tr, local_sem=T.sem.sent)
         return fn
 
+    base = float(B * rank - MID)
     for s in range(RO):
         lk = "land%d" % s
         lks = [lk, lk + "o"]
+        own = OWN[s]
         if s:
             land = T[lk]
-            op("v", lambda e, land=land: e.transpose(T.tt[:], land[:]), lks, ["tt"])
-            ts(T.tqi[:], T.tt[:, 0::16], 1.0 / 512, -float(B * rank), A.mult, A.add, ["tt"], ["tqi"])
-            tc(T.tq[:], T.tqi[:], ["tqi"], ["tq"])
-            act(T.yy[:], land[:], F.Identity, lks, ["yy"], bias=BIG - B * rank, scale=1.0 / 512)
-            tc(T.li[:], land[:], lks, ["li"])
+            act(T.bq[:], land[:], F.Identity, lks, ["bq"], bias=-base, scale=1.0 / PK)
+            ts(T.ci[:], land[:], PK - 1, None, A.bitwise_and, None, lks, ["ci"])
+            spread(T.bq, ["bq"], 0)
+            tc(T.b16[:], T.bq[:], ["bq"], ["b16"])
+            queue, qk = T.qw[:, 0:B + 16], ["qw", "qwp"]
         else:
-            mm(T.rb[:, 0:L], T.bo[:], T.w16[:], True, True, ["bo", "w16"], ["rb"])
-        for cc in range(2):
-            for k in range(2):
-                mm(T.cv[:, cc:24:2], T.dsb[:, 2 * cc + k, :], T.tq[:, (cc ^ k)::2], k == 0, k == 1, dsb + ["tq"], ["cv"])
-        tc(T.bl[:], T.cv[:, 0:24], [], ["cv", "bl"])
-        act(T.bf[:], T.cv[:, 0:24], F.Copy, [], ["cv", "bf"])
-        tc(T.q16[:], T.qw[:, 0:B + 16].indirect(T.bl[:]), ["qw", "qwp", "bl"], ["q16"])
-        ts(T.qf[:], T.q16[:], col(c_i13), None, A.add, None, ["q16", "c_i13"], ["qf"])
-        op("v", lambda e: e.transpose(T.qt[:], T.qf[:]), ["qf"], ["qt"])
-        for cc in range(2):
-            for j in range(2):
-                gx = 16 * (cc ^ j)
-                mm(T.k1[:, :, cc, :], T.dsf[:, 2 * cc + j, :], T.qt[:, :, gx:gx + 16], j == 0, j == 1, dsf + ["qt"], ["k1"])
+            tc(T.bq[:], T.wkz[:], ["wkz"], ["bq"])
+            spread(T.bq, ["bq"], 0)
+            mm(T.rb1[:, 0:L], T.bo[:], T.bq[:], True, True, ["bo", "bq"], ["rb1"])
+            tc(T.b16[:], T.rb1[:, 0:L], [], ["rb1", "b16"])
+            queue, qk = T.qi[:], ["qi", "qip"]
+        ts(T.bl[:], T.cv[:, 0:24], 1.0 / (16 * SC if s else SC), None, A.mult, None, [], ["cv", "bl"])
+        tc(T.bf[:], T.bl[:], ["bl"], ["bf"])
+        tc(T.q16[:], ind(queue, T.bl[:]), qk + ["bl"], ["q16"])
+        act(T.qf[:], ind(queue, T.bl[:]), F.Copy, qk + ["bl"], ["qf"])
+        for h in range(2):
+            tc(T.bx[:, h::2], T.bl[:, 12 * h:12 * h + 12], ["bl"], ["bx%d" % h])
+        act(T.qx[:], ind(queue, T.bx[:]), F.Copy, qk + ["bx0", "bx1"], ["qx"])
+        op("v", lambda e: e.transpose(T.qt[:], T.qx[:]), ["qx"], ["qt"], 0.4)
         if s:
-            ts(T.ci[:], T.li[:], 511, None, A.bitwise_and, None, ["li"], ["ci"])
-            tt(T.x1[:], T.vw[:, 0:B + 16].indirect(T.bl[:]), T.ci[:], A.subtract, ["vw", "vwp", "bl", "ci"], ["x1"])
+            put_positions()
+            tt(T.x1[:], ind(T.vw[:, 0:B + 16], T.bl[:]), T.ci[:], A.subtract, ["vw", "vwp", "bl", "ci"], ["x1"])
             ts(T.xx[:], T.x1[:], -255.0, None, A.max, None, ["x1"], ["xx"])
+            ts(T.nx[:], T.xx[:], -1.0, 0.0, A.mult, A.max, ["xx"], ["nx"])
+            repeat(pcopy, own[:2], own[-1])
+            repeat(pcopy, own[2:], own[-1])
         else:
-            act(T.xx[:], T.vw[:, 0:B + 16].indirect(T.bl[:]), F.Copy, ["vw", "vwp", "bl"], ["xx"])
-        k0 = NA // 4
-        for k in range(k0, 3):
-            mm(T.cv[:, 128 * (k + 1):128 * (k + 2)], T.xx[:, 128 * k:128 * (k + 1)], T.idb[:], True, True, ["xx", "idb"], ["cv"])
-        units = list(range(NA, 12))
-        gather(units[0])
-        gather(units[1])
-        act(T.xt[:, 128 * k0:L], T.cv[:, 128 * (k0 + 1):512], F.Copy, [], ["cv", "xt"])
-        if s:
-            ts(T.b16[:], T.yy[:], -BIG, None, A.add, None, ["yy"], ["b16"])
-        else:
-            tc(T.b16[:], T.rb[:, 0:L], [], ["rb", "b16"])
-        ts(T.ng[:], T.xx[:], 0.0, 64.0, A.is_lt, A.add, ["xx"], ["ng"])
-        compare(T.b16, T.bf, "b16", "bf")
-        for i in range(16):
-            ts(T.vr[:, i:512 * NA:16], T.xx[:, 0:32 * NA], -1.0, None, A.mult, None, ["xx"], ["vr%d" % i])
-        addv(units[0])
-        for k in range(2, len(units) + 2):
-            if k < len(units):
-                gather(units[k])
-            sign(units[k - 2])
-            if k - 1 < len(units):
-                addv(units[k - 1])
-            own_units(*C_OWN.get(k, (0, 0)))
-            if K_PAIRS <= k < K_PAIRS + N_PAIRS:
-                pairs(k - K_PAIRS, N_PAIRS)
-            if k == K_ND:
-                ts(T.rb[:, 0:L], T.rb[:, 0:L], col(c_sgn), 0.0, A.mult, A.is_lt, ["c_sgn"], ["rb"])
-                tt(T.wv[:], T.ng[:], T.rb[:, 0:L], A.mult, ["ng"], ["rb", "wv"])
-            if k == K_VAL:
-                spread(T.wv, "wv", 48)
-            if k == K_BASE:
-                ts(T.basev[:], T.cv[:, 48:72], 1024.5 * SC, 20000.0, A.is_lt, A.mult, [], ["cv", "basev"])
-                ts(T.e1[:], T.cv[:, 48:72], 0.5 * SC, None, A.is_lt, None, [], ["cv", "e1"])
-                tt(T.e2[:], T.e1[:], T.trv[:], A.mult, ["e1", "trv"], ["e2"])
-                tt(T.e3[:], T.e2[:], T.bf[:], A.max, ["e2", "bf"], ["e3"])
-                tc(T.ol[:], T.e3[:], ["e3"], ["ol"])
-            if k == K_SCORE:
-                for q in range(NA // 2):
-                    score(q)
-                tc(T.k1s[:], T.k1[:], [], ["k1", "k1s"])
-            if units[k - 2] % 2:
-                score(units[k - 2] // 2)
-            if k == K_BEST:
-                best(0)
-                lines(0)
-                compare(T.nh, T.ho, "nh", "ho", 0)
-        act(T.k1[:], T.xx[:], F.Relu, ["xx"], ["k1"], scale=-1.0)
-        best(1)
-        lines(1)
-        act(T.p0[:], T.pw[:, 0:W].indirect(T.nl[:]), F.Copy, ["pw15", "nl0", "nl1"], ["p0"], scale=512.0)
-        act(T.ag[:], T.aw[:, 0:W].indirect(T.nl[:]), F.Copy, ["aw", "nl0", "nl1"], ["ag"])
-        act(T.ab[:], T.p0[:], F.Abs, ["p0", "c_ctr"], ["ab"], bias=col(c_ctr), scale=1.0 / 512)
-        compare(T.nh, T.ho, "nh", "ho", 1)
-        pairs()
-        ts(T.th[:], T.ab[:], 1024.0, col(c_sub), A.is_lt, A.subtract, ["ab", "c_sub"], ["th"])
-        tt(T.k1[:], T.ag[:], T.k1[:], A.min, ["ag"], ["k1"])
-        tt(T.ps2[:, 0:L], T.rb[:, 0:L], T.th[:], A.is_lt, ["th"], ["rb", "ps2"])
-        op("v", lambda e: e.tensor_tensor_scan(T.st[:], T.ps2[:, 0:L], T.zb[:], col(c_ini), A.add, A.add), ["zb", "c_ini"], ["ps2", "st"])
+            act(T.xx[:], ind(T.vw[:, 0:B + 16], T.bl[:]), F.Copy, ["vw", "vwp", "bl"], ["xx"])
+            act(T.nx[:], T.xx[:], F.Relu, ["xx"], ["nx"], scale=-1.0)
+            act(T.qw[:, 0:B], T.qi[:, 0:B], F.Copy, ["qi", "qf"], ["qw"])
+            repeat(lambda out, in_, n, r, w: tc(out, in_, r, w), own, own[-1])
+        for k in range(3):
+            mm(T.cv[:, 128 * (k + 1):128 * (k + 2)], T.nx[:, 128 * k:128 * (k + 1)], T.idb[:], True, True, ["nx", "idb"], ["cv"])
+        act(T.xt[:], T.cv[:, 128:512], F.Copy, [], ["cv", "xt"], scale=-1.0)
+        pairs("rb1", T.b16, T.bf, ["b16", "bf"], 12, 24)
+        mm(T.rb1[:, 0:L], T.dg1[:], T.nx[:], False, False, ["dg1", "nx"], ["rb1"])
+        pairs("rb1", T.b16, T.bf, ["b16", "bf"], 0, 12)
+        act(T.wv[:], T.rb1[:, 0:L], F.Copy, ["c_sc"], ["rb1", "wv"], scale=col(c_sc))
+        spread(T.wv, ["wv"], 48)
+        ts(T.basev[:], T.cv[:, 48:72], 0.5 * SC, 20000.0, A.is_lt, A.mult, [], ["cv", "basev"])
+        ts(T.e1[:], T.cv[:, 48:72], -0.5 * SC, None, A.is_lt, None, [], ["cv", "e1"])
+        tt(T.e2[:], T.e1[:], T.trv[:], A.mult, ["e1", "trv"], ["e2"])
+        tt(T.e3[:], T.e2[:], T.bf[:], A.max, ["e2", "bf"], ["e3"])
+        tc(T.ol[:], T.e3[:], ["e3"], ["ol"])
+        for n in range(len(CHUNKS)):
+            queue_keys(n)
+        for k, u in enumerate(u for u in range(11, -1, -1) if u not in own):
+            scalar_unit(u, "ps%d" % (k % 3))
+        for u in own:
+            vector_unit(u, own[-1])
+        for n in range(len(CHUNKS)):
+            best(n)
+        last = len(CHUNKS) - 1
+        nls = ["nl%d" % n for n in range(last + 1)]
+        of_lines(CHUNKS[last][1], 24, nls[:last], "a")
+        of_lines(0, CHUNKS[last][1], nls[last:], "b")
+        mm(T.ps1[:, 0:L], T.idb[:], T.nx[:], True, True, ["idb", "nx"], ["ps1"])
+        tt(T.ps1[:, 0:L], T.ag[:], T.ps1[:, 0:L], A.min, ["aga", "agb"], ["ps1"])
+        tt(T.pp[:], T.p0[:], T.ps1[:, 0:L], A.add, ["p0a", "p0b"], ["ps1", "pp"])
+        tt(T.ps2[:, 0:L], T.rb5[:, 0:L], T.th[:], A.is_lt, ["tha", "thb"], ["rb5", "ps2"])
+        scan(T.st[:], T.ps2[:, 0:L], T.zb[:], col(c_ini), A.add, A.add, ["zb", "c_ini"], ["ps2", "st"])
         tt(T.ss[:], T.st[:], T.ps2[:, 0:L], A.mult, ["st"], ["ps2", "ss"])
-        spread(T.ss, "ss", 24)
-        tt(T.pp[:], T.p0[:], T.k1[:], A.add, ["p0"], ["k1", "pp"])
+        spread(T.ss, ["ss"], 24)
         ts(T.sl[:], T.cv[:, 24:48], 1.0 / SC, 1592.0, A.mult, A.add, [], ["cv", "sl"])
         swk = ["sw%d_%d" % (s, d) for d in range(NR)]
-        tc(T["sw%d" % s][:].indirect(T.sl[:]), T.pp[:], ["sl", "pp"], swk)
+        tc(ind(T["sw%d" % s][:], T.sl[:]), T.pp[:], ["sl", "pp"], swk)
         nk = "land%d" % (s + 1)
-        op("p", send(s, nk), swk, [])
-        op("p", None, [], [nk], ext=("arr%d" % s, 2 * (NR - 1)))
-        if s < RO - 1:
-            act(T.g0[:], T.cv[:, 24:48], F.Sign, [], ["cv", "g0"], bias=-1600.0, scale=1.0 / SC)
-            act(T.g2[:], T.cv[:, 24:48], F.Copy, [], ["cv", "g2"], bias=4535.0, scale=1.0 / SC)
-            act(T.tn[:], T.k1[:], F.Copy, [], ["k1", "tn"], scale=-1.0)
-            act(T.g1[:], T.g0[:], F.Relu, ["g0"], ["g1"])
-            act(T.g4[:], T.g0[:], F.Relu, ["g0"], ["g4"], scale=16.0)
-        act(T.nd[:], T.rb[:, 0:L], F.Relu, ["c_sg2"], ["rb", "nd"], scale=col(c_sg2))
+        op("p", send(s, nk), swk, ["gone%d" % s], 1.0)
+        op("p", None, ["gone%d" % s], [nk], FLIGHT - 1.0, ext=("arr%d" % s, 2 * (NR - 1)))
+        act(T.tn[:], T.ps1[:, 0:L], F.Copy, [], ["ps1", "tn"], scale=-1.0)
+        mm(T.ps0[:, 0:L], T.idb[:], T.tn[:], True, False, ["idb", "tn"], ["ps0"])
+        mm(T.ps0[:, 0:L], T.row8[:], T.ss[:], False, True, ["row8", "ss"], ["ps0"])
+        act(T.td[:], T.ps0[:, 0:L], F.Relu, [], ["ps0", "td"], scale=-1.0)
         a0 = PITCH * rank + 1
         act(T[nk][:, CAP * rank:CAP * (rank + 1)], T["sw%d" % s][:, a0:a0 + CAP], F.Copy, swk, [nk + "o"])
         if s < RO - 1:
-            ts(T.ii[:], T.ki[:], 13, 15, A.arith_shift_right, A.bitwise_and, ["ki0", "ki1"], ["ii"])
-            tt(T.g3[:], T.g1[:], T.g2[:], A.mult, ["g1", "g2"], ["g3"])
-            tt(T.g5[:], T.g4[:], T.ii[:], A.add, ["g4", "ii"], ["g5"])
+            kis, nis = ["ki%d" % n for n in range(last + 1)], ["ni%d" % n for n in range(last + 1)]
+            ts(T.ii[:], T.ki[:], 13, 15, A.arith_shift_right, A.bitwise_and, kis, ["ii"])
+            act(T.g0[:], T.cv[:, 24:48], F.Sign, [], ["cv", "g0"], bias=-1600.0, scale=1.0 / SC)
+            act(T.g1[:], T.g0[:], F.Relu, ["g0"], ["g1"], scale=16.0)
+            tt(T.g3[:], T.g1[:], T.tra[:], A.mult, ["g1", "tra"], ["g3"])
+            tt(T.g5[:], T.g1[:], T.ii[:], A.add, ["g1", "ii"], ["g5"])
+            tt(T.g6[:], T.g3[:], T.ni[:], A.max, ["g3"] + nis, ["g6"])
             tc(T.il[:], T.g5[:], ["g5"], ["il"])
-            tt(T.qn[:], T.wn[:].indirect(T.il[:]), T.qf[:], A.max, ["wna", "wnb", "il", "qf"], ["qn"])
-            act(T.q2[:], T.qn[:], F.Identity, ["qn", "c_n13"], ["q2"], bias=col(c_n13))
-        tt(T.td[:], T.nd[:], T.k1[:], A.mult, ["nd"], ["k1", "td"])
-        if s < RO - 1:
-            tt(T.g6[:], T.g3[:], T.ni[:], A.max, ["g3", "ni0", "ni1"], ["g6"])
-            tc(T.qw[:].indirect(T.ol[:]), T.q2[:], ["ol", "q2"], ["qw", "qwp"])
             tc(T.al[:], T.g6[:], ["g6"], ["al"])
-        tt(T.vw[:].indirect(T.ol[:]), T.xx[:], T.td[:], A.add, ["ol", "xx", "td"], ["vw", "vwp"])
-        if s < RO - 1:
-            tt(T.aw[:].indirect(T.al[:]), T.ag[:], T.tn[:], A.add, ["al", "ag", "tn"], ["aw"])
+            act(T.mk[:], ind(T.wn[:], T.il[:]), F.Copy, ["wna", "wnb", "il"], ["mk"])
+            tt(ind(T.aw[:], T.al[:]), T.ag[:], T.tn[:], A.add, ["al", "aga", "agb", "tn"], ["aw"])
+            tt(ind(T.qw[:], T.ol[:]), T.qf[:], T.mk[:], A.max, ["ol", "qf", "mk"], ["qw", "qwp"])
         else:
-            op("s", lambda e: e.dma_start(T.yv[:], T.vw[:, 0:B]), ["vw"], ["yv"], dma=("dyv", 16))
+            put_positions()
+            op("s", lambda e: e.dma_start(T.yv[:], T.vw[:, 0:B]), ["vw"], ["yv"], 3.7, dma=("dyv", 16))
 
     lk = "land%d" % RO
     lks = [lk, lk + "o"]
-    act(T.yy[:], T[lk][:], F.Identity, lks, ["yy"], bias=BIG - B * rank, scale=1.0 / 512)
-    act(T.x1[:], T.yy[:], F.Identity, ["yy"], ["x1"], bias=-BIG)
-    op("a", lambda e: e.dma_start(T.yw[:], T.x1[0::16, :]), ["x1"], ["yw"], dma=("dyw", 16))
-    tc(T.li[:], T[lk][:], lks, ["li"])
-    ts(T.ci[:], T.li[:], 511, None, A.bitwise_and, None, ["li"], ["ci"])
+    ts(T.ci[:], T[lk][:], PK - 1, None, A.bitwise_and, None, lks, ["ci"])
+    ts(T.yi[:], T[lk][:], 10, None, A.arith_shift_right, None, lks, ["yi"])
     tc(T.cb[:], T.ci[:], ["ci"], ["cb"])
-    op("s", lambda e: e.dma_start(T.yc[:], T.cb[:]), ["cb"], ["yc"], dma=("dyc", 16))
+    op("s", lambda e: e.dma_start(T.yc[:], T.cb[:]), ["cb"], ["yc"], 2.0, dma=("dyc", 16))
+    act(T.ab[:], T.yi[:], F.Identity, ["yi"], ["aba", "abb"], bias=-base)
+    op("a", lambda e: e.dma_start(T.yw[:], T.ab[0::16, :]), ["aba", "abb"], ["yw"], 1.8, dma=("dyw", 16))
     emit()
     g.wait_ge(T.sem.sent, 2 * (NR - 1) * RO)
     for n in ("dyv", "dyw", "dyc", "dwk", "dvp", "dqu", "dam"):

@@ -1,3 +1,4 @@
+import numpy as np
 from concourse.bass import DstId, RemoteDMATransfer
 from concourse.mybir import AluOpType, ActivationFunctionType
 
@@ -12,31 +13,38 @@ SW = 3600
 PK = 1024
 MID = NR * B // 2
 SC = 131072.0
-OWN = [[8, 7, 6, 5, 4], [7, 6, 5], [7, 6, 5]]
+BIG = 8388608.0
+OWN = [[8, 7, 6, 5, 4], [7, 6, 5, 4], [7, 6, 5, 4]]
 CHUNKS = [(12, 24), (4, 12), (0, 4)]
 KEYS = ["key1", "key0", "rb1"]
-CYC, WAKE, FLIGHT = 0.9e-3, 0.1, 2.8
-SWEEPS = 4
+LEAD = 2
+FIRST = [-1, 2, 2]
+CUT = 4096
+CYC, PE, WAKE, FLIGHT = 0.9e-3, 0.51e-3, 0.1, 2.8
+SWEEPS, SHAKE = 300, 2.0
+ORDER = []
 
 SCRATCH = {
     "vw": ("sbuf", [128, VW], "bfloat16"), "qi": ("sbuf", [128, B + 16], "int32"), "qw": ("sbuf", [128, VW], "float32"),
     "aw": ("sbuf", [128, AW], "bfloat16"), "pw": ("sbuf", [128, W], "int32"), "hw": ("sbuf", [128, W], "float32"),
     "wn": ("sbuf", [128, 32], "float32"), "cc": ("sbuf", [128, 24, 256], "bfloat16"), "gg": ("sbuf", [128, L * 16], "bfloat16"),
-    "vr": ("sbuf", [128, 2560], "bfloat16"), "ee": ("sbuf", [128, 24, L], "bfloat16"),
+    "vr": ("sbuf", [128, 3072], "bfloat16"), "ee": ("sbuf", [128, 24, L], "bfloat16"),
     "lm": ("sbuf", [128, 16, 128], "bfloat16"), "tm": ("sbuf", [128, 16, 128], "bfloat16"),
-    "rm": ("sbuf", [128, 2048], "bfloat16"), "ir": ("sbuf", [128, 2048], "bfloat16"),
+    "rm": ("sbuf", [128, 2048], "bfloat16"), "tri": ("sbuf", [128, 24, 16], "bfloat16"), "dg": ("sbuf", [128, 24, 16], "bfloat16"),
     "bo": ("sbuf", [128, 128], "bfloat16"), "bp": ("sbuf", [128, 128], "bfloat16"), "idb": ("sbuf", [128, 128], "bfloat16"),
-    "dg1": ("sbuf", [128, 128], "bfloat16"), "row8": ("sbuf", [128, 128], "bfloat16"),
+    "dg1": ("sbuf", [128, 128], "bfloat16"), "idn": ("sbuf", [128, 128], "bfloat16"), "idk": ("sbuf", [128, 128], "bfloat16"),
+    "idf": ("sbuf", [128, 128], "float32"), "row0": ("sbuf", [128, 128], "float32"), "nd": ("sbuf", [128, L], "bfloat16"),
     "zb": ("sbuf", [128, L], "bfloat16"), "c32": ("sbuf", [128, L], "bfloat16"), "rowc": ("sbuf", [128, 192], "bfloat16"),
     "rst": ("sbuf", [128, 192], "bfloat16"), "dsf": ("sbuf", [128, 4, 128], "float32"),
     "pi": ("sbuf", [128, 4], "int32"), "io128": ("sbuf", [128, 128], "bfloat16"), "iog": ("sbuf", [128, 128], "bfloat16"),
     "io16": ("sbuf", [128, 16], "bfloat16"), "trv": ("sbuf", [128, 24], "float32"), "tra": ("sbuf", [128, 24], "float32"),
     "wc": ("sbuf", [128, 48], "float32"), "col": ("sbuf", [128, 20], "float32"), "wkz": ("sbuf", [128, L], "int32"),
-    "land1": ("sbuf", [128, L], "int32"), "land2": ("sbuf", [128, L], "int32"), "land3": ("sbuf", [128, L], "int32"),
-    "sw0": ("sbuf", [128, SW], "int32"), "sw1": ("sbuf", [128, SW], "int32"), "sw2": ("sbuf", [128, SW], "int32"),
+    "land1": ("sbuf", [128, L], "float32"), "land2": ("sbuf", [128, L], "float32"), "land3": ("sbuf", [128, L], "int32"),
+    "sw0": ("sbuf", [128, SW], "float32"), "sw1": ("sbuf", [128, SW], "float32"), "sw2": ("sbuf", [128, SW], "int32"),
     "bq": ("sbuf", [128, L], "float16"), "bl": ("sbuf", [128, 24], "uint16"), "bf": ("sbuf", [128, 24], "float32"),
-    "b16": ("sbuf", [128, L], "uint16"), "ci": ("sbuf", [128, L], "int32"), "yi": ("sbuf", [128, L], "int32"),
+    "b16": ("sbuf", [128, L], "float16"), "ci": ("sbuf", [128, L], "int32"), "yi": ("sbuf", [128, L], "float32"),
     "cb": ("sbuf", [128, L], "bfloat16"), "q16": ("sbuf", [128, L], "uint16"), "qf": ("sbuf", [128, L], "float32"),
+    "bx": ("sbuf", [128, 24], "uint16"), "qx": ("sbuf", [128, L], "float32"),
     "qt": ("sbuf", [128, 12, 32], "float32"), "kk": ("sbuf", [128, L], "float32"),
     "ki": ("sbuf", [128, 24], "int32"), "ni": ("sbuf", [128, 24], "int32"), "ii": ("sbuf", [128, 24], "int32"),
     "nl": ("sbuf", [128, 24], "uint16"), "il": ("sbuf", [128, 24], "uint16"), "sl": ("sbuf", [128, 24], "uint16"),
@@ -53,20 +61,22 @@ SCRATCH = {
     "ss": ("sbuf", [128, L], "float16"), "mk": ("sbuf", [128, L], "float32"),
     "ps0": ("psum", [128, 512], "float32"), "ps1": ("psum", [128, 512], "float32"), "ps2": ("psum", [128, 512], "float32"),
     "key0": ("psum", [128, 512], "float32"), "key1": ("psum", [128, 512], "float32"),
-    "bx": ("sbuf", [128, 24], "uint16"), "qx": ("sbuf", [128, L], "float32"),
     "cv": ("psum", [128, 512], "float32"), "rb1": ("psum", [128, 512], "float32"), "rb5": ("psum", [128, 512], "float32"),
 }
 BANKS = [k for k, v in SCRATCH.items() if v[0] == "psum"]
-SEMAPHORES = ["qv", "qa", "qt", "qp", "dwk", "dvp", "dqu", "dam", "dpay", "dyv", "dyw", "dyc", "arr0", "arr1", "arr2", "sent"]
+SEMAPHORES = ["qv", "qa", "qt", "qp", "dwk", "dvp", "dqu", "dam", "dpay", "dpay2", "dyv", "dyw", "dyc", "arr0", "arr1", "arr2", "sent"]
 
 
 def make_queues(g, T):
-    calls, last_w, readers = [], {}, {}
+    calls, last_w, readers, rows = [], {}, {}, {}
 
-    def op(q, fn, r=(), w=(), us=0.1, dma=None, ext=None):
+    def op(q, fn, r=(), w=(), us=0.1, dma=None, ext=None, row=None):
         deps = [(last_w[k], "raw") for k in r if k in last_w]
-        if q == "s":
-            deps += [(o["id"], "order") for o in calls if o["q"] == q][-1:]
+        row = q if q == "s" else row
+        if row in rows:
+            deps.append((rows[row], "order"))
+        if row:
+            rows[row] = len(calls)
         for k in w:
             if k in last_w:
                 deps.append((last_w[k], "waw"))
@@ -84,36 +94,51 @@ def make_queues(g, T):
 
     def order():
         before, after = [[] for o in calls], [[] for o in calls]
+        us = [o["us"] for o in calls]
+        hold = [0.05 if o["dma"] else 0.0 if o["ext"] else o["us"] for o in calls]
         for o in calls:
-            o["hold"] = 0.05 if o["dma"] else 0.0 if o["ext"] else o["us"]
             for j, kind in o["deps"]:
-                lag = 0.05 - calls[j]["us"] if kind == "order" else 0.0 if free_edge(o, calls[j], kind) else WAKE
+                lag = hold[j] - us[j] if kind == "order" else 0.0 if free_edge(o, calls[j], kind) else WAKE
                 before[o["id"]].append((j, lag))
                 after[j].append((o["id"], lag))
 
         def place(turn, edges, back):
-            end, busy = {}, {q: [] for q in "vatps"}
+            end, busy = [0.0] * len(calls), {q: [] for q in "vatps"}
             for i in turn:
-                o = calls[i]
-                skip = o["us"] - o["hold"] if back else 0.0
+                skip = us[i] - hold[i] if back else 0.0
                 t = max([end[j] + lag for j, lag in edges[i]] + [0.0]) + skip
-                row, k = busy[o["q"]], 0
-                for k in range(len(row) + 1):
-                    if k == len(row) or row[k][0] >= t + o["hold"]:
-                        break
+                row = busy[calls[i]["q"]]
+                k, hi = 0, len(row)
+                while k < hi:
+                    if row[(k + hi) // 2][1] <= t:
+                        k = (k + hi) // 2 + 1
+                    else:
+                        hi = (k + hi) // 2
+                while k < len(row) and row[k][0] < t + hold[i]:
                     t = max(t, row[k][1])
-                row.insert(k, (t, t + o["hold"]))
-                end[i] = t - skip + o["us"]
+                    k += 1
+                row.insert(k, (t, t + hold[i]))
+                end[i] = t - skip + us[i]
             return end
 
-        turn, best = list(range(len(calls))), None
-        for sweep in range(SWEEPS):
-            end = place(turn, before, False)
-            if best is None or max(end.values()) < max(best.values()):
-                best = end
-            end = place(sorted(turn, key=lambda i: (-end[i] + calls[i]["us"] - calls[i]["hold"], -i)), after, True)
-            turn = sorted(turn, key=lambda i: (-end[i], i))
-        return [calls[i] for i in sorted(turn, key=lambda i: (best[i] - calls[i]["us"], i))]
+        if not ORDER:
+            every = range(len(calls))
+            rng = np.random.default_rng(1)
+            best = end = place(every, before, False)
+            for sweep in range(SWEEPS):
+                back = place(sorted(every, key=lambda i: (us[i] - hold[i] - end[i], -i)), after, True)
+                end = place(sorted(every, key=lambda i: (-back[i], i)), before, False)
+                if max(end) <= max(best):
+                    best = end
+                if sweep % 2:
+                    at, when = float(rng.random()) * max(best), []
+                    for i in every:
+                        t = best[i] - us[i]
+                        t += SHAKE * float(rng.random()) if abs(t - at) < 2 * SHAKE else 0.0
+                        when.append(max([t] + [when[j] + 1e-6 for j, lag in before[i]]))
+                    end = place(sorted(every, key=lambda i: when[i]), before, False)
+            ORDER.extend(sorted(every, key=lambda i: (best[i] - us[i], i)))
+        return [calls[i] for i in ORDER]
 
     def emit():
         engine = {"v": g.vector, "a": g.scalar, "t": g.tensor, "p": g, "s": g.sync}
@@ -180,7 +205,7 @@ def rank_program(g, core, T, topo):
     if rank is None:
         return
     op, emit = make_queues(g, T)
-    c_m, c_g, c_p, c_x, c_h0, c_h1, c_ctr, c_sgn, c_ini, c_lt8, c_ts, c_tb, c_d1, c_d5, c_sc = range(15)
+    c_m, c_g, c_p, c_x, c_h0, c_h1, c_ctr, c_sgn, c_ini, c_lt8, c_ts, c_tb, c_d1, c_r0, c_sc = range(15)
 
     def col(k):
         return T.col[:, k:k + 1]
@@ -221,12 +246,15 @@ def rank_program(g, core, T, topo):
     def fill(out, k, w):
         op("v", lambda e: e.memset(out, k), [], w, length(out, out, None)[0])
 
-    def act(out, in_, f, r, w, bias=0.0, scale=1.0):
+    def act(out, in_, f, r, w, bias=0.0, scale=1.0, row=None):
         us, out, in_ = length(out, in_, 1.0)
-        op("a", lambda e: e.activation(out, in_, f, bias=bias, scale=scale), r, w, us)
+        op("a", lambda e: e.activation(out, in_, f, bias=bias, scale=scale), r, w, us, row=row)
 
     def mm(out, lhs, rhs, start, stop, r, w):
-        op("t", lambda e: e.matmul(out, lhs, rhs, start, stop), r, w, max(64, size(rhs)) * (2.0 if "32" in str(rhs.dtype) else 0.5) * CYC)
+        op("t", lambda e: e.matmul(out, lhs, rhs, start, stop), r, w, max(64, size(rhs)) * (4 if "32" in str(rhs.dtype) else 1) * PE)
+
+    def mms(run, r, w):
+        op("t", lambda e: [e.matmul(*c) for c in run][-1], r, w, len(run) * 64 * PE)
 
     def iota(out, pattern, base, cm, w):
         op("p", lambda e: e.iota(out, pattern, base, cm, allow_small_or_imprecise_dtypes=True), [], w, 0.14 + 2 * size(out) * CYC)
@@ -234,28 +262,31 @@ def rank_program(g, core, T, topo):
     def pcopy(out, in_, n, r, w):
         op("p", lambda e: e.affine_select(out, in_, [[0, n]], A.is_ge, 0.0, 0, 0), r, w, 0.19 + 2 * size(out) * CYC)
 
+    def payees(rows, r, us, sem):
+        for j in rows:
+            op("s", lambda e, j=j: e.dma_start(T.pw[j::16, :], T.pay[:]), r, ["pw%d" % j], us, dma=(sem, 128))
+
     fill(T.wkz[:], 0, ["wkz"])
     op("s", lambda e: e.dma_start(T.vw[:, 0:B], T.vp[:]), [], ["vw"], 3.7, dma=("dvp", 16))
     op("s", lambda e: e.dma_start(T.wkz[0::16, :], T.wk[:]), [], ["wkz"], 3.2, dma=("dwk", 16))
     op("s", lambda e: e.dma_start(T.qi[:, 0:B], T.qu[:]), [], ["qi"], 7.4, dma=("dqu", 16))
     op("s", lambda e: e.dma_start(T.aw[:, 0:W], T.am[:]), [], ["aw"], 13.4, dma=("dam", 16))
-    for j in range(16):
-        op("s", lambda e, j=j: e.dma_start(T.pw[j::16, :], T.pay[:]), ["aw"], ["pw%d" % j], 12.0, dma=("dpay", 256))
-
-    op("p", lambda e: e.iota(T.pi[:, 0:1], [[1, 1]], 0, 1), [], ["pi0"], 0.14)
+    iota(T.pi[:, 0:1], [[1, 1]], 0, 1, ["pi0"])
     iota(T.iog[:], [[1, 8], [0, 16]], 0, 0, ["iog"])
     iota(T.io128[:], [[1, 128]], 0, 0, ["io128"])
     iota(T.io16[:], [[1, 16]], 0, 0, ["io16"])
+    iota(T.pw[:, 0:CUT], [[0, CUT]], 0, 0, ["pwa"])
+    fill(T.pw[:, CUT:W], 0, ["pwb"])
+    payees(range(8), ["pwa", "pwb"], 10.0, "dpay")
+
     iota(T.rowc[:], [[0, 12], [8192, 16]], 0, 0, ["rowc"])
     iota(T.trv[:], [[16, 24]], 2064, 1, ["trv"])
-    iota(T.ir[:], [[1, 128], [0, 16]], 0, 0, ["ir"])
     iota(T.hw[:, 0:W - 1], [[1, W - 1]], 0, 0, ["hw"])
     iota(T.hw[:, W - 1:W], [[1, 1]], 60000, 0, ["hwc"])
     for s in range(RO):
         for d in range(NR):
             a0 = PITCH * d + 1
-            op("p", lambda e, s=s, d=d, a0=a0: e.iota(T["sw%d" % s][:, a0:a0 + CAP], [[0, CAP]], (d * B + B - MID) * PK, 0),
-               ["hw"], ["sw%d_%d" % (s, d)], 0.23)
+            iota(T["sw%d" % s][:, a0:a0 + CAP], [[0, CAP]], (d * B + B - MID) * PK, 0, ["sw%d_%d" % (s, d)])
     fill(T.lm[:], 0.0, ["lm0"])
     ts(T.pi[:, 1:2], T.pi[:, 0:1], 15, None, A.bitwise_and, None, ["pi0"], ["pi1"])
     ts(T.pi[:, 2:3], T.pi[:, 0:1], 4, None, A.arith_shift_right, None, ["pi0"], ["pi2"])
@@ -281,20 +312,29 @@ def rank_program(g, core, T, topo):
     tt(T.wc[:, 32:48], T.wc[:, 0:16], T.wc[:, 16:32], A.add, ["wc0", "wc1"], ["wc"])
     ts(T.bp[:, 8::16], T.bo[:, 8::16], -4.0, None, A.mult, None, ["bo", "bp0"], ["bp"])
     ts(T.idb[:], T.io128[:], col(c_p), None, A.is_equal, None, ["io128", "c_p"], ["idb"])
-    ts(col(c_d5), col(c_m), 8.0, None, A.is_equal, None, ["c_m"], ["c_d5"])
     ts(col(c_d1), col(c_sgn), -1.0 / 256, None, A.mult, None, ["c_sgn"], ["c_d1"])
     ts(col(c_sc), col(c_sgn), -256.0, None, A.mult, None, ["c_sgn"], ["c_sc"])
     for a in range(16):
         act(T.tm[:, a, :], T.bp[:], F.Copy, ["bp", "wc"], ["tm%d" % a], scale=T.wc[:, 32 + a:33 + a])
+    act(T.tri[:, 0, :], T.wc[:, 32:48], F.Copy, ["wc"], ["tri"])
+    for c in (1, 2, 4, 8, 16):
+        act(T.tri[:, c:min(2 * c, 24), :], T.tri[:, 0:min(c, 24 - c), :], F.Copy, ["tri"], ["tri"])
     fill(T.c32[:], 1.0 / 32, ["c32"])
     ts(T.dg1[:], T.io128[:], col(c_p), col(c_d1), A.is_equal, A.mult, ["io128", "c_p", "c_d1"], ["dg1"])
     for k, (pc, hc) in enumerate(((c_p, c_h0), (c_x, c_h0), (c_p, c_h1), (c_x, c_h1))):
         ts(T.dsf[:, k, :], T.io128[:], col(pc), col(hc), A.is_equal, A.mult, ["io128", "c_p", "c_x", "c_h0", "c_h1"], ["dsf%d" % k])
-    ts(T.rm[:], T.ir[:], col(c_p), None, A.is_equal, None, ["ir", "c_p"], ["rm"])
+    for i in (0, 8):
+        tc(T.rm[:, i::16], T.idb[:], ["idb"], ["rm%d" % i])
+    for k in (8, 4, 2):
+        tc(T.rm[:, k // 2::k], T.rm[:, 0::k], ["rm0", "rm8"], ["rm"])
     fill(T.zb[:], 0.0, ["zb"])
     fill(T.rst[:], 0.0, ["rst0"])
     fill(T.wn[:, 16:32], 0.0, ["wnb"])
-    ts(T.row8[:], T.bo[:], col(c_d5), None, A.mult, None, ["bo", "c_d5"], ["row8"])
+    act(T.idn[:], T.idb[:], F.Copy, ["idb"], ["idn"], scale=-1.0)
+    act(T.idk[:], T.idb[:], F.Copy, ["idb"], ["idk"], scale=-float(PK))
+    act(T.idf[:], T.idb[:], F.Copy, ["idb"], ["idf"])
+    ts(col(c_r0), col(c_m), 0.0, None, A.is_equal, None, ["c_m"], ["c_r0"])
+    act(T.row0[:], T.bo[:], F.Copy, ["bo", "c_r0"], ["row0"], scale=col(c_r0))
     ts(col(c_ctr), col(c_m), -2048.0, MID - 1023.5, A.mult, A.add, ["c_m"], ["c_ctr"])
     ts(col(c_ini), col(c_m), float(PITCH), -1592.0, A.mult, A.add, ["c_m"], ["c_ini"])
     ts(col(c_ts), col(c_m), 8.0, -1.0, A.is_lt, A.mult, ["c_m"], ["c_ts"])
@@ -316,19 +356,24 @@ def rank_program(g, core, T, topo):
             ts(T.ee[:, c, 0:L - 16 * c], buf[:, 16 * c:L], own[:, c:c + 1], None, A.is_equal, None, r, ["ee%d" % c])
             if c < 23:
                 mm(T[rb][:, 16 * (c + 1):L], T.bp[:], T.ee[:, c, 16:L - 16 * c], False, False, ["bp", "ee%d" % c], [rb])
-        if c0 == 0:
-            for a in range(16):
-                mm(T[rb][:, a:L:16], T.tm[:, a, :], T.ee[:, :, a], False, a == 15, tms + ees, [rb])
 
-    def spread(src, keys, c0):
-        for a in range(16):
-            mm(T.cv[:, c0:c0 + 24], T.lm[:, a, :], src[:, a::16], a == 0, a == 15, lms + keys, ["cv"])
+    def within(rb, c0):
+        mms([(T[rb][:, 16 * c0 + a:L:16], T.tm[:, a, :], T.ee[:, c0:, a], False, a == 15 and c0 == 0) for a in range(16)], tms + ees[c0:], [rb])
 
-    def scalar_unit(u, pk):
-        act(T.gg[:, 512 * u:512 * (u + 1)], ind(T.aw[:, 0:W], T.q16[:, 32 * u:32 * (u + 1)]), F.Copy, ["aw", "q16"], ["gg%d" % u])
+    def within_below(rb, c0):
+        tt(T.dg[:, 0:c0, :], T.ee[:, 0:c0, 0:16], T.tri[:, 0:c0, :], A.mult, ees[:c0] + ["tri"], ["dg"])
+        mm(T[rb][:, 0:16 * c0], T.bp[:], T.dg[:, 0:c0, :], False, True, ["bp", "dg"], [rb])
+
+    def spread(src, key, c0):
+        mms([(T.cv[:, c0:c0 + 24], T.lm[:, a, :], src[:, a::16], a == 0, a == 15) for a in range(16)], lms + [key], ["cv"])
+
+    def gather(u):
+        act(T.gg[:, 512 * u:512 * (u + 1)], ind(T.aw[:, 0:W], T.q16[:, 32 * u:32 * (u + 1)]), F.Copy, ["aw", "q16"], ["gg%d" % u], row="units")
+
+    def sign(u, pk):
         mm(T[pk][:], T.idb[:], T.gg[:, 512 * u:512 * (u + 1)], True, False, ["idb", "gg%d" % u], [pk])
-        mm(T[pk][:], T.xt[:, 128 * (u // 4):128 * (u // 4 + 1)], T.rm[:, 512 * (u % 4):512 * (u % 4 + 1)], False, True, ["xt", "rm"], [pk])
-        act(T.cc[:, 2 * u:2 * u + 2, :], T[pk][:], F.Sign, [], [pk, "cc%d" % (2 * u), "cc%d" % (2 * u + 1)], bias=0.5)
+        mm(T[pk][:], T.xt[:, 128 * (u // 4):128 * (u // 4 + 1)], T.rm[:, 512 * (u % 4):512 * (u % 4 + 1)], False, True, ["xt%d" % (u // 4), "rm"], [pk])
+        act(T.cc[:, 2 * u:2 * u + 2, :], T[pk][:], F.Sign, [], [pk, "cc%d" % (2 * u), "cc%d" % (2 * u + 1)], bias=0.5, row="units")
 
     def vector_unit(u, u0):
         for c in (2 * u + 1, 2 * u):
@@ -342,11 +387,13 @@ def rank_program(g, core, T, topo):
         for k in (8, 4, 2):
             copy(T.vr[:, lo + k // 2:hi:k], T.vr[:, lo:hi:k], (hi - lo) // k, [x + y for x in keys for y in ("_0", "_8")], keys)
 
+    def vcopy(out, in_, n, r, w):
+        tc(out, in_, r, w)
+
     def score(q, n):
         kb, off = KEYS[n], 64 * q - 16 * CHUNKS[n][0]
-        for a in range(16):
-            mm(T[kb][:, off:off + 64], T.lm[:, a, :], T.cc[:, 4 * q:4 * q + 4, 16 * a:16 * a + 16], False, a == 15 and off == 0,
-               lms + ["cc%d" % c for c in range(4 * q, 4 * q + 4)], [kb])
+        mms([(T[kb][:, off:off + 64], T.lm[:, a, :], T.cc[:, 4 * q:4 * q + 4, 16 * a:16 * a + 16], False, a == 15 and off == 0) for a in range(16)],
+            lms + ["cc%d" % c for c in range(4 * q, 4 * q + 4)], [kb])
 
     def queue_keys(n):
         (c0, c1), kb = CHUNKS[n], KEYS[n]
@@ -367,17 +414,34 @@ def rank_program(g, core, T, topo):
         tc(T.nl[:, hs], T.ni[:, hs], ["ni" + k], ["nl" + k])
         tt(T.ho[:, hs], T.ni[:, hs], T.basev[:, hs], A.add, ["ni" + k, "basev"], ["ho" + k])
         tc(T.nh[:, ls], ind(T.hw[:], T.nl[:, hs]), ["hw", "hwc", "nl" + k], ["nh" + k])
+        if c0 == 0:
+            within("rb5", c1)
         pairs("rb5", T.nh, T.ho, ["nh%d" % i for i in range(n + 1)] + ["ho" + k], c0, c1)
+        if c0 == 0:
+            within_below("rb5", c1)
 
-    def of_lines(c0, c1, nls, k):
+    def of_lines(c0, c1, r, k):
         hs, ls = slice(c0, c1), slice(16 * c0, 16 * c1)
-        act(T.p0[:, ls], ind(T.pw[:, 0:W], T.nl[:, hs]), F.Copy, ["pw15"] + nls, ["p0" + k], bias=-float(MID * PK), scale=float(PK))
+        act(T.p0[:, ls], ind(T.pw[:, 0:W], T.nl[:, hs]), F.Copy, ["pw7", "pw15"] + r, ["p0" + k], bias=-float(MID * PK), scale=float(PK))
         act(T.ab[:, ls], T.p0[:, ls], F.Abs, ["p0" + k, "c_ctr"], ["ab" + k], bias=col(c_ctr), scale=1.0 / PK)
         act(T.th[:, ls], T.ab[:, ls], F.Sign, ["ab" + k, "c_ts", "c_tb"], ["th" + k], bias=col(c_tb), scale=col(c_ts))
-        act(T.ag[:, ls], ind(T.aw[:, 0:W], T.nl[:, hs]), F.Copy, ["aw"] + nls, ["ag" + k])
+        act(T.ag[:, ls], ind(T.aw[:, 0:W], T.nl[:, hs]), F.Copy, ["aw"] + r, ["ag" + k])
 
-    def put_positions():
-        tt(ind(T.vw[:], T.ol[:]), T.xx[:], T.td[:], A.add, ["ol", "xx", "td"], ["vw", "vwp"])
+    def first_at_bank(masked):
+        pairs("rb1", T.b16, T.bf, ["b16", "bf"], 12, 24)
+        mm(T.rb1[:, 0:L], T.dg1[:], T.nx[:], False, False, ["dg1", "nx"], ["rb1"])
+        pairs("rb1", T.b16, T.bf, ["b16", "bf"], 0, 12)
+        if masked:
+            within_below("rb1", 24)
+        else:
+            within("rb1", 0)
+        act(T.wv[:], T.rb1[:, 0:L], F.Copy, ["c_sc"], ["rb1", "wv"], scale=col(c_sc), row="units")
+        spread(T.wv, "wv", 48)
+        ts(T.basev[:], T.cv[:, 48:72], 0.5 * SC, 20000.0, A.is_lt, A.mult, [], ["cv", "basev"])
+        ts(T.e1[:], T.cv[:, 48:72], -0.5 * SC, None, A.is_lt, None, [], ["cv", "e1"])
+        tt(T.e2[:], T.e1[:], T.trv[:], A.mult, ["e1", "trv"], ["e2"])
+        tt(T.e3[:], T.e2[:], T.bf[:], A.max, ["e2", "bf"], ["e3"])
+        tc(T.ol[:], T.e3[:], ["e3"], ["ol"])
 
     def send(s, to_buf):
         def fn(e):
@@ -402,81 +466,92 @@ def rank_program(g, core, T, topo):
         lk = "land%d" % s
         lks = [lk, lk + "o"]
         own = OWN[s]
+        units = [u for u in range(11, -1, -1) if u not in own]
         if s:
             land = T[lk]
             act(T.bq[:], land[:], F.Identity, lks, ["bq"], bias=-base, scale=1.0 / PK)
-            ts(T.ci[:], land[:], PK - 1, None, A.bitwise_and, None, lks, ["ci"])
-            spread(T.bq, ["bq"], 0)
-            tc(T.b16[:], T.bq[:], ["bq"], ["b16"])
+            spread(T.bq, "bq", 0)
+            act(T.yi[:], land[:], F.Identity, lks, ["yi"], bias=BIG - base, scale=1.0 / PK)
+            act(T.b16[:], T.yi[:], F.Identity, ["yi"], ["b16"], bias=-BIG)
+            mm(T.key0[:, 0:L], T.idf[:], land[:], True, False, ["idf"] + lks, ["key0"])
+            mm(T.key0[:, 0:L], T.idk[:], T.b16[:], False, True, ["idk", "b16"], ["key0"])
+            act(T.cb[:], T.key0[:, 0:L], F.Identity, [], ["key0", "cb"], bias=-base * PK)
             queue, qk = T.qw[:, 0:B + 16], ["qw", "qwp"]
         else:
             tc(T.bq[:], T.wkz[:], ["wkz"], ["bq"])
-            spread(T.bq, ["bq"], 0)
+            spread(T.bq, "bq", 0)
             mm(T.rb1[:, 0:L], T.bo[:], T.bq[:], True, True, ["bo", "bq"], ["rb1"])
             tc(T.b16[:], T.rb1[:, 0:L], [], ["rb1", "b16"])
             queue, qk = T.qi[:], ["qi", "qip"]
         ts(T.bl[:], T.cv[:, 0:24], 1.0 / (16 * SC if s else SC), None, A.mult, None, [], ["cv", "bl"])
         tc(T.bf[:], T.bl[:], ["bl"], ["bf"])
         tc(T.q16[:], ind(queue, T.bl[:]), qk + ["bl"], ["q16"])
-        act(T.qf[:], ind(queue, T.bl[:]), F.Copy, qk + ["bl"], ["qf"])
         for h in range(2):
             tc(T.bx[:, h::2], T.bl[:, 12 * h:12 * h + 12], ["bl"], ["bx%d" % h])
         act(T.qx[:], ind(queue, T.bx[:]), F.Copy, qk + ["bx0", "bx1"], ["qx"])
         op("v", lambda e: e.transpose(T.qt[:], T.qx[:]), ["qx"], ["qt"], 0.4)
+        queue_keys(0)
+        queue_keys(1)
         if s:
-            put_positions()
-            tt(T.x1[:], ind(T.vw[:, 0:B + 16], T.bl[:]), T.ci[:], A.subtract, ["vw", "vwp", "bl", "ci"], ["x1"])
+            tt(T.x1[:], ind(T.vw[:, 0:B + 16], T.bl[:]), T.cb[:], A.subtract, ["vw", "vwp", "bl", "cb"], ["x1"])
             ts(T.xx[:], T.x1[:], -255.0, None, A.max, None, ["x1"], ["xx"])
             ts(T.nx[:], T.xx[:], -1.0, 0.0, A.mult, A.max, ["xx"], ["nx"])
-            repeat(pcopy, own[:2], own[-1])
-            repeat(pcopy, own[2:], own[-1])
+            for k in range(0, len(own), 2):
+                repeat(pcopy, own[k:k + 2], own[-1])
         else:
             act(T.xx[:], ind(T.vw[:, 0:B + 16], T.bl[:]), F.Copy, ["vw", "vwp", "bl"], ["xx"])
             act(T.nx[:], T.xx[:], F.Relu, ["xx"], ["nx"], scale=-1.0)
-            act(T.qw[:, 0:B], T.qi[:, 0:B], F.Copy, ["qi", "qf"], ["qw"])
-            repeat(lambda out, in_, n, r, w: tc(out, in_, r, w), own, own[-1])
-        for k in range(3):
+            act(T.qw[:, 0:B], T.qi[:, 0:B], F.Copy, ["qi", "qx"], ["qw"])
+            repeat(vcopy, own, own[-1])
+        blocks = sorted(set(u // 4 for u in units), reverse=True)
+        for k in blocks:
             mm(T.cv[:, 128 * (k + 1):128 * (k + 2)], T.nx[:, 128 * k:128 * (k + 1)], T.idb[:], True, True, ["nx", "idb"], ["cv"])
-        act(T.xt[:], T.cv[:, 128:512], F.Copy, [], ["cv", "xt"], scale=-1.0)
-        pairs("rb1", T.b16, T.bf, ["b16", "bf"], 12, 24)
-        mm(T.rb1[:, 0:L], T.dg1[:], T.nx[:], False, False, ["dg1", "nx"], ["rb1"])
-        pairs("rb1", T.b16, T.bf, ["b16", "bf"], 0, 12)
-        act(T.wv[:], T.rb1[:, 0:L], F.Copy, ["c_sc"], ["rb1", "wv"], scale=col(c_sc))
-        spread(T.wv, ["wv"], 48)
-        ts(T.basev[:], T.cv[:, 48:72], 0.5 * SC, 20000.0, A.is_lt, A.mult, [], ["cv", "basev"])
-        ts(T.e1[:], T.cv[:, 48:72], -0.5 * SC, None, A.is_lt, None, [], ["cv", "e1"])
-        tt(T.e2[:], T.e1[:], T.trv[:], A.mult, ["e1", "trv"], ["e2"])
-        tt(T.e3[:], T.e2[:], T.bf[:], A.max, ["e2", "bf"], ["e3"])
-        tc(T.ol[:], T.e3[:], ["e3"], ["ol"])
-        for n in range(len(CHUNKS)):
-            queue_keys(n)
-        for k, u in enumerate(u for u in range(11, -1, -1) if u not in own):
-            scalar_unit(u, "ps%d" % (k % 3))
+        for k in blocks:
+            act(T.xt[:, 128 * k:128 * (k + 1)], T.cv[:, 128 * (k + 1):128 * (k + 2)], F.Copy, [], ["cv", "xt%d" % k], scale=-1.0)
+        if FIRST[s] < 0:
+            first_at_bank(False)
+        for u in units[:LEAD]:
+            gather(u)
+        for k, u in enumerate(units):
+            sign(u, "ps%d" % (k % 3))
+            if k + LEAD < len(units):
+                gather(units[k + LEAD])
+            if k == FIRST[s]:
+                first_at_bank(True)
+        queue_keys(2)
         for u in own:
             vector_unit(u, own[-1])
         for n in range(len(CHUNKS)):
             best(n)
         last = len(CHUNKS) - 1
         nls = ["nl%d" % n for n in range(last + 1)]
+        mm(T.ps1[:, 0:L], T.idb[:], T.nx[:], True, True, ["idb", "nx"], ["ps1"])
         of_lines(CHUNKS[last][1], 24, nls[:last], "a")
         of_lines(0, CHUNKS[last][1], nls[last:], "b")
-        mm(T.ps1[:, 0:L], T.idb[:], T.nx[:], True, True, ["idb", "nx"], ["ps1"])
         tt(T.ps1[:, 0:L], T.ag[:], T.ps1[:, 0:L], A.min, ["aga", "agb"], ["ps1"])
-        tt(T.pp[:], T.p0[:], T.ps1[:, 0:L], A.add, ["p0a", "p0b"], ["ps1", "pp"])
+        if s:
+            tt(T.pp[:], T.p0[:], T.ps1[:, 0:L], A.add, ["p0a", "p0b"], ["ps1", "pp"])
+        act(T.tn[:], T.ps1[:, 0:L], F.Copy, [], ["ps1", "tn"], scale=-1.0)
+        if s == 0:
+            mm(T.ps0[:, 0:L], T.row0[:], T.p0[:], True, False, ["row0", "p0a", "p0b"], ["ps0"])
+            mm(T.ps0[:, 0:L], T.idn[:], T.tn[:], False, True, ["idn", "tn"], ["ps0"])
+            act(T.pp[:], T.ps0[:, 0:L], F.Copy, [], ["ps0", "pp"])
         tt(T.ps2[:, 0:L], T.rb5[:, 0:L], T.th[:], A.is_lt, ["tha", "thb"], ["rb5", "ps2"])
+        act(T.nd[:], T.rb5[:, 0:L], F.Copy, ["c_sc"], ["rb5", "nd"], scale=col(c_sc))
         scan(T.st[:], T.ps2[:, 0:L], T.zb[:], col(c_ini), A.add, A.add, ["zb", "c_ini"], ["ps2", "st"])
         tt(T.ss[:], T.st[:], T.ps2[:, 0:L], A.mult, ["st"], ["ps2", "ss"])
-        spread(T.ss, ["ss"], 24)
+        spread(T.ss, "ss", 24)
         ts(T.sl[:], T.cv[:, 24:48], 1.0 / SC, 1592.0, A.mult, A.add, [], ["cv", "sl"])
         swk = ["sw%d_%d" % (s, d) for d in range(NR)]
         tc(ind(T["sw%d" % s][:], T.sl[:]), T.pp[:], ["sl", "pp"], swk)
         nk = "land%d" % (s + 1)
         op("p", send(s, nk), swk, ["gone%d" % s], 1.0)
-        op("p", None, ["gone%d" % s], [nk], FLIGHT - 1.0, ext=("arr%d" % s, 2 * (NR - 1)))
-        act(T.tn[:], T.ps1[:, 0:L], F.Copy, [], ["ps1", "tn"], scale=-1.0)
-        mm(T.ps0[:, 0:L], T.idb[:], T.tn[:], True, False, ["idb", "tn"], ["ps0"])
-        mm(T.ps0[:, 0:L], T.row8[:], T.ss[:], False, True, ["row8", "ss"], ["ps0"])
-        act(T.td[:], T.ps0[:, 0:L], F.Relu, [], ["ps0", "td"], scale=-1.0)
+        op("p", None, ["gone%d" % s], [nk], FLIGHT - (1.0 if s else 0.0), ext=("arr%d" % s, 2 * (NR - 1)))
+        if s == 0:
+            payees(range(8, 16), [nk, "p0a", "p0b"], 8.0, "dpay2")
+        mm(T.key1[:, 0:L], T.idn[:], T.tn[:], True, False, ["idn", "tn"], ["key1"])
+        mm(T.key1[:, 0:L], T.idb[:], T.nd[:], False, True, ["idb", "nd"], ["key1"])
+        act(T.td[:], T.key1[:, 0:L], F.Relu, [], ["key1", "td"])
         a0 = PITCH * rank + 1
         act(T[nk][:, CAP * rank:CAP * (rank + 1)], T["sw%d" % s][:, a0:a0 + CAP], F.Copy, swk, [nk + "o"])
         if s < RO - 1:
@@ -484,6 +559,7 @@ def rank_program(g, core, T, topo):
             ts(T.ii[:], T.ki[:], 13, 15, A.arith_shift_right, A.bitwise_and, kis, ["ii"])
             act(T.g0[:], T.cv[:, 24:48], F.Sign, [], ["cv", "g0"], bias=-1600.0, scale=1.0 / SC)
             act(T.g1[:], T.g0[:], F.Relu, ["g0"], ["g1"], scale=16.0)
+            act(T.qf[:], ind(queue, T.bl[:]), F.Copy, qk + ["bl", "nd"], ["qf"])
             tt(T.g3[:], T.g1[:], T.tra[:], A.mult, ["g1", "tra"], ["g3"])
             tt(T.g5[:], T.g1[:], T.ii[:], A.add, ["g1", "ii"], ["g5"])
             tt(T.g6[:], T.g3[:], T.ni[:], A.max, ["g3"] + nis, ["g6"])
@@ -492,20 +568,20 @@ def rank_program(g, core, T, topo):
             act(T.mk[:], ind(T.wn[:], T.il[:]), F.Copy, ["wna", "wnb", "il"], ["mk"])
             tt(ind(T.aw[:], T.al[:]), T.ag[:], T.tn[:], A.add, ["al", "aga", "agb", "tn"], ["aw"])
             tt(ind(T.qw[:], T.ol[:]), T.qf[:], T.mk[:], A.max, ["ol", "qf", "mk"], ["qw", "qwp"])
-        else:
-            put_positions()
-            op("s", lambda e: e.dma_start(T.yv[:], T.vw[:, 0:B]), ["vw"], ["yv"], 3.7, dma=("dyv", 16))
+        tt(ind(T.vw[:], T.ol[:]), T.xx[:], T.td[:], A.add, ["ol", "xx", "td"], ["vw", "vwp"])
+    op("s", lambda e: e.dma_start(T.yv[:], T.vw[:, 0:B]), ["vw"], ["yv"], 3.7, dma=("dyv", 16))
 
     lk = "land%d" % RO
     lks = [lk, lk + "o"]
     ts(T.ci[:], T[lk][:], PK - 1, None, A.bitwise_and, None, lks, ["ci"])
-    ts(T.yi[:], T[lk][:], 10, None, A.arith_shift_right, None, lks, ["yi"])
     tc(T.cb[:], T.ci[:], ["ci"], ["cb"])
     op("s", lambda e: e.dma_start(T.yc[:], T.cb[:]), ["cb"], ["yc"], 2.0, dma=("dyc", 16))
-    act(T.ab[:], T.yi[:], F.Identity, ["yi"], ["aba", "abb"], bias=-base)
+    act(T.mk[:], T[lk][:], F.Identity, lks, ["mk"], bias=BIG - base, scale=1.0 / PK)
+    act(T.ab[:], T.mk[:], F.Identity, ["mk"], ["aba", "abb"], bias=-BIG)
     op("a", lambda e: e.dma_start(T.yw[:], T.ab[0::16, :]), ["aba", "abb"], ["yw"], 1.8, dma=("dyw", 16))
     emit()
     g.wait_ge(T.sem.sent, 2 * (NR - 1) * RO)
     for n in ("dyv", "dyw", "dyc", "dwk", "dvp", "dqu", "dam"):
         g.wait_ge(T.sem[n], 16)
-    g.wait_ge(T.sem.dpay, 256)
+    for n in ("dpay", "dpay2"):
+        g.wait_ge(T.sem[n], 128)

@@ -7,29 +7,31 @@ F = ActivationFunctionType
 NR, B, W, CAP, RO = 8, 2048, 6144, 48, 3
 L = NR * CAP
 VW = 2560
-AW = 6640
+QZ = 6207
+AW = 6720
 PITCH = 400
 SW = 3600
 PK = 1024
 MID = NR * B // 2
 SC = 131072.0
 BIG = 8388608.0
-OWN = [[8, 7, 6, 5, 4], [7, 6, 5, 4], [7, 6, 5, 4]]
+OWN = [[9, 8, 7, 6, 5, 4], [8, 7, 6, 5, 4], [8, 7, 6, 5, 4]]
 CHUNKS = [(12, 24), (4, 12), (0, 4)]
 KEYS = ["key1", "key0", "rb1"]
 LEAD = 2
 FIRST = [-1, 2, 2]
-CUT = 4096
-CYC, PE, WAKE, FLIGHT = 0.9e-3, 0.51e-3, 0.1, 2.8
-SWEEPS, SHAKE = 300, 2.0
+CUT = 3072
+SELF = 2
+CYC, PE, WAKE, FLIGHT = 0.955e-3, 0.47e-3, 0.105, 3.0
+SWEEPS, SHAKE = 500, 2.0
 ORDER = []
 
 SCRATCH = {
     "vw": ("sbuf", [128, VW], "bfloat16"), "qi": ("sbuf", [128, B + 16], "int32"), "qw": ("sbuf", [128, VW], "float32"),
-    "aw": ("sbuf", [128, AW], "bfloat16"), "pw": ("sbuf", [128, W], "int32"), "hw": ("sbuf", [128, W], "float32"),
+    "aw": ("sbuf", [128, AW], "bfloat16"), "pw": ("sbuf", [128, QZ + 1], "int32"), "hw": ("sbuf", [128, QZ + 1], "float32"),
     "wn": ("sbuf", [128, 32], "float32"), "cc": ("sbuf", [128, 24, 256], "bfloat16"), "gg": ("sbuf", [128, L * 16], "bfloat16"),
     "vr": ("sbuf", [128, 3072], "bfloat16"), "ee": ("sbuf", [128, 24, L], "bfloat16"),
-    "lm": ("sbuf", [128, 16, 128], "bfloat16"), "tm": ("sbuf", [128, 16, 128], "bfloat16"),
+    "lm": ("sbuf", [128, 2048], "bfloat16"), "scs": ("sbuf", [128, 16], "bfloat16"), "tm": ("sbuf", [128, 16, 128], "bfloat16"),
     "rm": ("sbuf", [128, 2048], "bfloat16"), "tri": ("sbuf", [128, 24, 16], "bfloat16"), "dg": ("sbuf", [128, 24, 16], "bfloat16"),
     "bo": ("sbuf", [128, 128], "bfloat16"), "bp": ("sbuf", [128, 128], "bfloat16"), "idb": ("sbuf", [128, 128], "bfloat16"),
     "dg1": ("sbuf", [128, 128], "bfloat16"), "idn": ("sbuf", [128, 128], "bfloat16"), "idk": ("sbuf", [128, 128], "bfloat16"),
@@ -39,13 +41,13 @@ SCRATCH = {
     "pi": ("sbuf", [128, 4], "int32"), "io128": ("sbuf", [128, 128], "bfloat16"), "iog": ("sbuf", [128, 128], "bfloat16"),
     "io16": ("sbuf", [128, 16], "bfloat16"), "trv": ("sbuf", [128, 24], "float32"), "tra": ("sbuf", [128, 24], "float32"),
     "wc": ("sbuf", [128, 48], "float32"), "col": ("sbuf", [128, 20], "float32"), "wkz": ("sbuf", [128, L], "int32"),
-    "land1": ("sbuf", [128, L], "float32"), "land2": ("sbuf", [128, L], "float32"), "land3": ("sbuf", [128, L], "int32"),
-    "sw0": ("sbuf", [128, SW], "float32"), "sw1": ("sbuf", [128, SW], "float32"), "sw2": ("sbuf", [128, SW], "int32"),
+    "land1": ("sbuf", [128, L], "int32"), "land2": ("sbuf", [128, L], "int32"), "land3": ("sbuf", [128, L], "int32"),
+    "sw0": ("sbuf", [128, SW], "int32"), "sw1": ("sbuf", [128, SW], "int32"), "sw2": ("sbuf", [128, SW], "int32"),
     "bq": ("sbuf", [128, L], "float16"), "bl": ("sbuf", [128, 24], "uint16"), "bf": ("sbuf", [128, 24], "float32"),
-    "b16": ("sbuf", [128, L], "float16"), "ci": ("sbuf", [128, L], "int32"), "yi": ("sbuf", [128, L], "float32"),
+    "b16": ("sbuf", [128, L], "uint16"), "ci": ("sbuf", [128, L], "int32"), "yi": ("sbuf", [128, L], "float32"),
     "cb": ("sbuf", [128, L], "bfloat16"), "q16": ("sbuf", [128, L], "uint16"), "qf": ("sbuf", [128, L], "float32"),
     "bx": ("sbuf", [128, 24], "uint16"), "qx": ("sbuf", [128, L], "float32"),
-    "qt": ("sbuf", [128, 12, 32], "float32"), "kk": ("sbuf", [128, L], "float32"),
+    "qt": ("sbuf", [128, 12, 32], "float32"), "kk": ("sbuf", [128, L], "int32"),
     "ki": ("sbuf", [128, 24], "int32"), "ni": ("sbuf", [128, 24], "int32"), "ii": ("sbuf", [128, 24], "int32"),
     "nl": ("sbuf", [128, 24], "uint16"), "il": ("sbuf", [128, 24], "uint16"), "sl": ("sbuf", [128, 24], "uint16"),
     "ol": ("sbuf", [128, 24], "uint16"), "al": ("sbuf", [128, 24], "uint16"),
@@ -58,7 +60,7 @@ SCRATCH = {
     "nh": ("sbuf", [128, L], "uint16"), "ag": ("sbuf", [128, L], "bfloat16"), "p0": ("sbuf", [128, L], "float32"),
     "ab": ("sbuf", [128, L], "float32"), "th": ("sbuf", [128, L], "bfloat16"), "tn": ("sbuf", [128, L], "bfloat16"),
     "td": ("sbuf", [128, L], "bfloat16"), "pp": ("sbuf", [128, L], "float32"), "st": ("sbuf", [128, L], "float32"),
-    "ss": ("sbuf", [128, L], "float16"), "mk": ("sbuf", [128, L], "float32"),
+    "ss": ("sbuf", [128, L], "float16"), "mk": ("sbuf", [128, L], "bfloat16"), "qn": ("sbuf", [128, L], "float32"),
     "ps0": ("psum", [128, 512], "float32"), "ps1": ("psum", [128, 512], "float32"), "ps2": ("psum", [128, 512], "float32"),
     "key0": ("psum", [128, 512], "float32"), "key1": ("psum", [128, 512], "float32"),
     "cv": ("psum", [128, 512], "float32"), "rb1": ("psum", [128, 512], "float32"), "rb5": ("psum", [128, 512], "float32"),
@@ -140,7 +142,7 @@ def make_queues(g, T):
             ORDER.extend(sorted(every, key=lambda i: (best[i] - us[i], i)))
         return [calls[i] for i in ORDER]
 
-    def emit():
+    def emit(past):
         engine = {"v": g.vector, "a": g.scalar, "t": g.tensor, "p": g, "s": g.sync}
         sem = {"v": T.sem.qv, "a": T.sem.qa, "t": T.sem.qt, "p": T.sem.qp}
         known = {q: {} for q in engine}
@@ -194,7 +196,9 @@ def make_queues(g, T):
                 ins.then_inc(T.sem[o["dma"][0]], 16)
             elif o["inc"]:
                 ins.then_inc(sem[o["q"]], 1)
-        for q in sem:
+        for name, val in past:
+            g.wait_ge(T.sem[name], val)
+        for q in "ptva":
             if count[q]:
                 g.wait_ge(sem[q], count[q])
     return op, emit
@@ -226,7 +230,7 @@ def rank_program(g, core, T, topo):
             return 0.06 + in_[1] * 1.56 * CYC, out, in_[0]
         if cycles is None:
             cycles = 0.5 if all("16" in str(x.dtype) for x in (out, in_) + others) else 1.0
-        return 0.055 + size(out) * cycles * CYC, out, in_
+        return 0.047 + size(out) * cycles * CYC, out, in_
 
     def ts(out, in0, s1, s2, o0, o1, r, w):
         us, out, in0 = length(out, in0, None)
@@ -247,42 +251,63 @@ def rank_program(g, core, T, topo):
         op("v", lambda e: e.memset(out, k), [], w, length(out, out, None)[0])
 
     def act(out, in_, f, r, w, bias=0.0, scale=1.0, row=None):
+        fixed = (0.0 if isinstance(in_, tuple) else 0.005) + (1.3 if f == F.Silu and scale != 1.0 else 0.0)
         us, out, in_ = length(out, in_, 1.0)
-        op("a", lambda e: e.activation(out, in_, f, bias=bias, scale=scale), r, w, us, row=row)
+        us += fixed
+        if bias == 0.0 and scale == 1.0:
+            op("a", lambda e: e.activation(out, in_, f), r, w, us, row=row)
+        else:
+            op("a", lambda e: e.activation(out, in_, f, bias=bias, scale=scale), r, w, us, row=row)
+
+    sums = {}
+
+    def in_group(start, stop, r, w):
+        bank = w[0]
+        if start:
+            sums[bank] = []
+            return r, w + [bank + "+"]
+        if stop:
+            return r + sums[bank] + [bank + "+"], w
+        sums[bank].append("%s+%d" % (bank, len(sums[bank])))
+        return r + [bank + "+"], sums[bank][-1:]
 
     def mm(out, lhs, rhs, start, stop, r, w):
+        r, w = in_group(start, stop, r, w)
         op("t", lambda e: e.matmul(out, lhs, rhs, start, stop), r, w, max(64, size(rhs)) * (4 if "32" in str(rhs.dtype) else 1) * PE)
 
     def mms(run, r, w):
+        r, w = in_group(run[0][3], run[-1][4], r, w)
         op("t", lambda e: [e.matmul(*c) for c in run][-1], r, w, len(run) * 64 * PE)
 
     def iota(out, pattern, base, cm, w):
-        op("p", lambda e: e.iota(out, pattern, base, cm, allow_small_or_imprecise_dtypes=True), [], w, 0.14 + 2 * size(out) * CYC)
+        op("p", lambda e: e.iota(out, pattern, base, cm, allow_small_or_imprecise_dtypes=True), [], w, 0.145 + 2 * size(out) * CYC)
 
     def pcopy(out, in_, n, r, w):
         op("p", lambda e: e.affine_select(out, in_, [[0, n]], A.is_ge, 0.0, 0, 0), r, w, 0.19 + 2 * size(out) * CYC)
 
     def payees(rows, r, us, sem):
         for j in rows:
-            op("s", lambda e, j=j: e.dma_start(T.pw[j::16, :], T.pay[:]), r, ["pw%d" % j], us, dma=(sem, 128))
+            op("s", lambda e, j=j: e.dma_start(T.pw[j::16, 0:W], T.pay[:]), r, ["pw%d" % j], us, dma=(sem, 128))
 
     fill(T.wkz[:], 0, ["wkz"])
-    op("s", lambda e: e.dma_start(T.vw[:, 0:B], T.vp[:]), [], ["vw"], 3.7, dma=("dvp", 16))
-    op("s", lambda e: e.dma_start(T.wkz[0::16, :], T.wk[:]), [], ["wkz"], 3.2, dma=("dwk", 16))
-    op("s", lambda e: e.dma_start(T.qi[:, 0:B], T.qu[:]), [], ["qi"], 7.4, dma=("dqu", 16))
-    op("s", lambda e: e.dma_start(T.aw[:, 0:W], T.am[:]), [], ["aw"], 13.4, dma=("dam", 16))
+    op("s", lambda e: e.dma_start(T.vw[:, 0:B], T.vp[:]), [], ["vw"], 3.5, dma=("dvp", 16))
+    op("s", lambda e: e.dma_start(T.wkz[0::16, :], T.wk[:]), [], ["wkz"], 3.0, dma=("dwk", 16))
+    op("s", lambda e: e.dma_start(T.qi[:, 0:B], T.qu[:]), [], ["qi"], 6.8, dma=("dqu", 16))
+    op("s", lambda e: e.dma_start(T.aw[:, 0:W], T.am[:]), [], ["aw"], 12.3, dma=("dam", 16))
     iota(T.pi[:, 0:1], [[1, 1]], 0, 1, ["pi0"])
     iota(T.iog[:], [[1, 8], [0, 16]], 0, 0, ["iog"])
     iota(T.io128[:], [[1, 128]], 0, 0, ["io128"])
     iota(T.io16[:], [[1, 16]], 0, 0, ["io16"])
     iota(T.pw[:, 0:CUT], [[0, CUT]], 0, 0, ["pwa"])
-    fill(T.pw[:, CUT:W], 0, ["pwb"])
-    payees(range(8), ["pwa", "pwb"], 10.0, "dpay")
+    act(T.pw[:, CUT:CUT + B], T.vw[:, 0:B], F.Copy, ["vw"], ["pwc"], scale=0.0)
+    fill(T.pw[:, CUT + B:], 0, ["pwb"])
+    fill(T.aw[:, W:QZ + 1], 0.0, ["awp"])
+    payees(range(8), ["pwa", "pwb", "pwc"], 10.0, "dpay")
 
     iota(T.rowc[:], [[0, 12], [8192, 16]], 0, 0, ["rowc"])
     iota(T.trv[:], [[16, 24]], 2064, 1, ["trv"])
     iota(T.hw[:, 0:W - 1], [[1, W - 1]], 0, 0, ["hw"])
-    iota(T.hw[:, W - 1:W], [[1, 1]], 60000, 0, ["hwc"])
+    iota(T.hw[:, W - 1:], [[0, QZ + 2 - W]], 60000, 0, ["hwc"])
     for s in range(RO):
         for d in range(NR):
             a0 = PITCH * d + 1
@@ -296,10 +321,11 @@ def rank_program(g, core, T, topo):
     tc(col(c_m), T.pi[:, 1:2], ["pi1"], ["c_m"])
     tc(col(c_h1), T.pi[:, 3:4], ["pi3"], ["c_h1"])
     ts(T.bo[:], T.iog[:], col(c_g), None, A.is_equal, None, ["iog", "c_g"], ["bo"])
-    for a in range(16):
-        act(T.lm[:, a, a::16], T.bo[:, 0::16], F.Copy, ["bo", "lm0"], ["lm%d" % (a + 1)], scale=SC)
+    fill(T.scs[:], SC, ["scs"])
+    for k in range(8):
+        ts(T.lm[:, 16 * k:2048 - 112 + 16 * k:129], T.scs[:], T.bo[:, 16 * k:16 * k + 1], None, A.mult, None, ["bo", "lm0", "scs"], ["lm%d" % (k + 1)])
     fill(T.vw[:, B:B + 16], 0.0, ["vwp"])
-    fill(T.qw[:, B:B + 16], W - 1.0, ["qwp"])
+    fill(T.qw[:, B:B + 16], 0.0, ["qwp"])
     fill(T.qi[:, B:B + 16], W - 1, ["qip"])
     ts(col(c_sgn), col(c_m), 8.0, -2.0, A.is_equal, A.mult, ["c_m"], ["c_sgn0"])
     ts(col(c_h0), col(c_h1), -1.0, 1.0, A.mult, A.add, ["c_h1"], ["c_h0"])
@@ -317,21 +343,20 @@ def rank_program(g, core, T, topo):
     for a in range(16):
         act(T.tm[:, a, :], T.bp[:], F.Copy, ["bp", "wc"], ["tm%d" % a], scale=T.wc[:, 32 + a:33 + a])
     act(T.tri[:, 0, :], T.wc[:, 32:48], F.Copy, ["wc"], ["tri"])
-    for c in (1, 2, 4, 8, 16):
+    for c in (1, 2):
         act(T.tri[:, c:min(2 * c, 24), :], T.tri[:, 0:min(c, 24 - c), :], F.Copy, ["tri"], ["tri"])
     fill(T.c32[:], 1.0 / 32, ["c32"])
     ts(T.dg1[:], T.io128[:], col(c_p), col(c_d1), A.is_equal, A.mult, ["io128", "c_p", "c_d1"], ["dg1"])
     for k, (pc, hc) in enumerate(((c_p, c_h0), (c_x, c_h0), (c_p, c_h1), (c_x, c_h1))):
         ts(T.dsf[:, k, :], T.io128[:], col(pc), col(hc), A.is_equal, A.mult, ["io128", "c_p", "c_x", "c_h0", "c_h1"], ["dsf%d" % k])
     for i in (0, 8):
-        tc(T.rm[:, i::16], T.idb[:], ["idb"], ["rm%d" % i])
+        act(T.rm[:, i::16], T.idb[:], F.Copy, ["idb"], ["rm%d" % i])
     for k in (8, 4, 2):
-        tc(T.rm[:, k // 2::k], T.rm[:, 0::k], ["rm0", "rm8"], ["rm"])
+        act(T.rm[:, k // 2::k], T.rm[:, 0::k], F.Copy, ["rm0", "rm8"], ["rm"])
     fill(T.zb[:], 0.0, ["zb"])
     fill(T.rst[:], 0.0, ["rst0"])
     fill(T.wn[:, 16:32], 0.0, ["wnb"])
     act(T.idn[:], T.idb[:], F.Copy, ["idb"], ["idn"], scale=-1.0)
-    act(T.idk[:], T.idb[:], F.Copy, ["idb"], ["idk"], scale=-float(PK))
     act(T.idf[:], T.idb[:], F.Copy, ["idb"], ["idf"])
     ts(col(c_r0), col(c_m), 0.0, None, A.is_equal, None, ["c_m"], ["c_r0"])
     act(T.row0[:], T.bo[:], F.Copy, ["bo", "c_r0"], ["row0"], scale=col(c_r0))
@@ -339,12 +364,12 @@ def rank_program(g, core, T, topo):
     ts(col(c_ini), col(c_m), float(PITCH), -1592.0, A.mult, A.add, ["c_m"], ["c_ini"])
     ts(col(c_ts), col(c_m), 8.0, -1.0, A.is_lt, A.mult, ["c_m"], ["c_ts"])
     ts(col(c_lt8), col(c_m), 8.0, 1025.0, A.is_lt, A.mult, ["c_m"], ["c_lt8"])
-    ts(T.wn[:, 0:16], T.io16[:], col(c_m), float(W - 1), A.is_equal, A.mult, ["io16", "c_m"], ["wna"])
-    ts(T.tra[:], T.trv[:], 1.0 / 16, (W - 2064.0) / 16, A.mult, A.add, ["trv"], ["tra"])
+    ts(T.wn[:, 0:16], T.io16[:], col(c_m), -8192.0, A.is_equal, A.mult, ["io16", "c_m"], ["wna"])
+    ts(T.tra[:], T.trv[:], 1.0 / 16, (QZ + 1 - 2064.0) / 16, A.mult, A.add, ["trv"], ["tra"])
     fill(T.rst[:, 0::16], -16777216.0, ["rst0"])
     ts(col(c_tb), col(c_lt8), -1.0, None, A.add, None, ["c_lt8"], ["c_tb"])
 
-    lms = ["lm%d" % a for a in range(17)]
+    lms = ["lm%d" % a for a in range(9)]
     tms = ["tm%d" % a for a in range(16)]
     ees = ["ee%d" % c for c in range(24)]
     dsf = ["dsf%d" % k for k in range(4)]
@@ -364,21 +389,21 @@ def rank_program(g, core, T, topo):
         tt(T.dg[:, 0:c0, :], T.ee[:, 0:c0, 0:16], T.tri[:, 0:c0, :], A.mult, ees[:c0] + ["tri"], ["dg"])
         mm(T[rb][:, 0:16 * c0], T.bp[:], T.dg[:, 0:c0, :], False, True, ["bp", "dg"], [rb])
 
-    def spread(src, key, c0):
-        mms([(T.cv[:, c0:c0 + 24], T.lm[:, a, :], src[:, a::16], a == 0, a == 15) for a in range(16)], lms + [key], ["cv"])
+    def spread(src, key, c0, bank="cv"):
+        mms([(T[bank][:, c0:c0 + 24], T.lm[:, 128 * a:128 * a + 128], src[:, a::16], a == 0, a == 15) for a in range(16)], lms + [key], [bank])
 
     def gather(u):
-        act(T.gg[:, 512 * u:512 * (u + 1)], ind(T.aw[:, 0:W], T.q16[:, 32 * u:32 * (u + 1)]), F.Copy, ["aw", "q16"], ["gg%d" % u], row="units")
+        act(T.gg[:, 512 * u:512 * (u + 1)], ind(T.aw[:, 0:QZ + 1], T.q16[:, 32 * u:32 * (u + 1)]), F.Copy, ["aw", "awp", "q16"], ["gg%d" % u], row="units")
 
     def sign(u, pk):
         mm(T[pk][:], T.idb[:], T.gg[:, 512 * u:512 * (u + 1)], True, False, ["idb", "gg%d" % u], [pk])
-        mm(T[pk][:], T.xt[:, 128 * (u // 4):128 * (u // 4 + 1)], T.rm[:, 512 * (u % 4):512 * (u % 4 + 1)], False, True, ["xt%d" % (u // 4), "rm"], [pk])
+        mm(T[pk][:], T.xt[:, 128 * blocks.index(u // 4):128 * blocks.index(u // 4) + 128], T.rm[:, 512 * (u % 4):512 * (u % 4 + 1)], False, True, ["xt", "rm"], [pk])
         act(T.cc[:, 2 * u:2 * u + 2, :], T[pk][:], F.Sign, [], [pk, "cc%d" % (2 * u), "cc%d" % (2 * u + 1)], bias=0.5, row="units")
 
     def vector_unit(u, u0):
         for c in (2 * u + 1, 2 * u):
-            tt(T.cc[:, c, :], ind(T.aw[:, 0:W], T.q16[:, 16 * c:16 * (c + 1)]), T.vr[:, 256 * (c - 2 * u0):256 * (c - 2 * u0 + 1)],
-               A.is_ge, ["aw", "q16", "vr%d" % u], ["cc%d" % c])
+            tt(T.cc[:, c, :], ind(T.aw[:, 0:QZ + 1], T.q16[:, 16 * c:16 * (c + 1)]), T.vr[:, 256 * (c - 2 * u0):256 * (c - 2 * u0 + 1)],
+               A.is_ge, ["aw", "awp", "q16", "vr%d" % u], ["cc%d" % c])
 
     def repeat(copy, units, u0):
         lo, hi, keys = 512 * (units[-1] - u0), 512 * (units[0] - u0 + 1), ["vr%d" % u for u in units]
@@ -392,7 +417,7 @@ def rank_program(g, core, T, topo):
 
     def score(q, n):
         kb, off = KEYS[n], 64 * q - 16 * CHUNKS[n][0]
-        mms([(T[kb][:, off:off + 64], T.lm[:, a, :], T.cc[:, 4 * q:4 * q + 4, 16 * a:16 * a + 16], False, a == 15 and off == 0) for a in range(16)],
+        mms([(T[kb][:, off:off + 64], T.lm[:, 128 * a:128 * a + 128], T.cc[:, 4 * q:4 * q + 4, 16 * a:16 * a + 16], False, a == 15 and off == 0) for a in range(16)],
             lms + ["cc%d" % c for c in range(4 * q, 4 * q + 4)], [kb])
 
     def queue_keys(n):
@@ -409,8 +434,7 @@ def rank_program(g, core, T, topo):
         for q in range(c1 // 4 - 1, c0 // 4 - 1, -1):
             score(q, n)
         scan(T.kk[:, ls], T.rst[:, 0:16 * (c1 - c0)], T[kb][:, 0:16 * (c1 - c0)], 0.0, A.add, A.max, ["rst0"], [kb, "kk" + k])
-        tc(T.ki[:, hs], T.kk[:, 16 * c0 + 15:16 * c1:16], ["kk" + k], ["ki" + k])
-        ts(T.ni[:, hs], T.ki[:, hs], 8191, None, A.bitwise_and, None, ["ki" + k], ["ni" + k])
+        ts(T.ni[:, hs], T.kk[:, 16 * c0 + 15:16 * c1:16], 8191, None, A.bitwise_and, None, ["kk" + k], ["ni" + k])
         tc(T.nl[:, hs], T.ni[:, hs], ["ni" + k], ["nl" + k])
         tt(T.ho[:, hs], T.ni[:, hs], T.basev[:, hs], A.add, ["ni" + k, "basev"], ["ho" + k])
         tc(T.nh[:, ls], ind(T.hw[:], T.nl[:, hs]), ["hw", "hwc", "nl" + k], ["nh" + k])
@@ -422,10 +446,10 @@ def rank_program(g, core, T, topo):
 
     def of_lines(c0, c1, r, k):
         hs, ls = slice(c0, c1), slice(16 * c0, 16 * c1)
-        act(T.p0[:, ls], ind(T.pw[:, 0:W], T.nl[:, hs]), F.Copy, ["pw7", "pw15"] + r, ["p0" + k], bias=-float(MID * PK), scale=float(PK))
+        act(T.p0[:, ls], ind(T.pw[:], T.nl[:, hs]), F.Copy, ["pw7", "pw15"] + r, ["p0" + k], bias=-float(MID * PK), scale=float(PK))
         act(T.ab[:, ls], T.p0[:, ls], F.Abs, ["p0" + k, "c_ctr"], ["ab" + k], bias=col(c_ctr), scale=1.0 / PK)
         act(T.th[:, ls], T.ab[:, ls], F.Sign, ["ab" + k, "c_ts", "c_tb"], ["th" + k], bias=col(c_tb), scale=col(c_ts))
-        act(T.ag[:, ls], ind(T.aw[:, 0:W], T.nl[:, hs]), F.Copy, ["aw"] + r, ["ag" + k])
+        act(T.ag[:, ls], ind(T.aw[:, 0:QZ + 1], T.nl[:, hs]), F.Copy, ["aw", "awp"] + r, ["ag" + k])
 
     def first_at_bank(masked):
         pairs("rb1", T.b16, T.bf, ["b16", "bf"], 12, 24)
@@ -461,6 +485,7 @@ def rank_program(g, core, T, topo):
             return e.remote_dma_fused(tr, local_sem=T.sem.sent)
         return fn
 
+    blocks = []
     base = float(B * rank - MID)
     for s in range(RO):
         lk = "land%d" % s
@@ -471,11 +496,8 @@ def rank_program(g, core, T, topo):
             land = T[lk]
             act(T.bq[:], land[:], F.Identity, lks, ["bq"], bias=-base, scale=1.0 / PK)
             spread(T.bq, "bq", 0)
-            act(T.yi[:], land[:], F.Identity, lks, ["yi"], bias=BIG - base, scale=1.0 / PK)
-            act(T.b16[:], T.yi[:], F.Identity, ["yi"], ["b16"], bias=-BIG)
-            mm(T.key0[:, 0:L], T.idf[:], land[:], True, False, ["idf"] + lks, ["key0"])
-            mm(T.key0[:, 0:L], T.idk[:], T.b16[:], False, True, ["idk", "b16"], ["key0"])
-            act(T.cb[:], T.key0[:, 0:L], F.Identity, [], ["key0", "cb"], bias=-base * PK)
+            ts(T.ci[:], land[:], PK - 1, None, A.bitwise_and, None, lks, ["ci"])
+            tc(T.b16[:], T.bq[:], ["bq"], ["b16"])
             queue, qk = T.qw[:, 0:B + 16], ["qw", "qwp"]
         else:
             tc(T.bq[:], T.wkz[:], ["wkz"], ["bq"])
@@ -485,29 +507,28 @@ def rank_program(g, core, T, topo):
             queue, qk = T.qi[:], ["qi", "qip"]
         ts(T.bl[:], T.cv[:, 0:24], 1.0 / (16 * SC if s else SC), None, A.mult, None, [], ["cv", "bl"])
         tc(T.bf[:], T.bl[:], ["bl"], ["bf"])
-        tc(T.q16[:], ind(queue, T.bl[:]), qk + ["bl"], ["q16"])
+        sg, q0 = (-1.0, QZ + 0.25) if s else (1.0, 0.0)
+        act(T.q16[:], ind(queue, T.bl[:]), F.Copy, qk + ["bl"], ["q16"], scale=sg, bias=q0)
         for h in range(2):
             tc(T.bx[:, h::2], T.bl[:, 12 * h:12 * h + 12], ["bl"], ["bx%d" % h])
-        act(T.qx[:], ind(queue, T.bx[:]), F.Copy, qk + ["bx0", "bx1"], ["qx"])
+        act(T.qx[:], ind(queue, T.bx[:]), F.Copy, qk + ["bx0", "bx1"], ["qx"], scale=sg, bias=q0)
         op("v", lambda e: e.transpose(T.qt[:], T.qx[:]), ["qx"], ["qt"], 0.4)
         queue_keys(0)
         queue_keys(1)
         if s:
-            tt(T.x1[:], ind(T.vw[:, 0:B + 16], T.bl[:]), T.cb[:], A.subtract, ["vw", "vwp", "bl", "cb"], ["x1"])
+            tt(T.x1[:], ind(T.vw[:, 0:B + 16], T.bl[:]), T.ci[:], A.subtract, ["vw", "vwp", "bl", "ci"], ["x1"])
             ts(T.xx[:], T.x1[:], -255.0, None, A.max, None, ["x1"], ["xx"])
             ts(T.nx[:], T.xx[:], -1.0, 0.0, A.mult, A.max, ["xx"], ["nx"])
-            for k in range(0, len(own), 2):
-                repeat(pcopy, own[k:k + 2], own[-1])
+            for copy, k0, k1 in ((vcopy, 0, 1), (pcopy, 1, 3), (pcopy, 3, 5)):
+                repeat(copy, own[k0:k1], own[-1])
         else:
             act(T.xx[:], ind(T.vw[:, 0:B + 16], T.bl[:]), F.Copy, ["vw", "vwp", "bl"], ["xx"])
             act(T.nx[:], T.xx[:], F.Relu, ["xx"], ["nx"], scale=-1.0)
-            act(T.qw[:, 0:B], T.qi[:, 0:B], F.Copy, ["qi", "qx"], ["qw"])
             repeat(vcopy, own, own[-1])
-        blocks = sorted(set(u // 4 for u in units), reverse=True)
-        for k in blocks:
-            mm(T.cv[:, 128 * (k + 1):128 * (k + 2)], T.nx[:, 128 * k:128 * (k + 1)], T.idb[:], True, True, ["nx", "idb"], ["cv"])
-        for k in blocks:
-            act(T.xt[:, 128 * k:128 * (k + 1)], T.cv[:, 128 * (k + 1):128 * (k + 2)], F.Copy, [], ["cv", "xt%d" % k], scale=-1.0)
+        blocks[:] = sorted(set(u // 4 for u in units), reverse=True)
+        for i, k in enumerate(blocks):
+            mm(T.cv[:, 128 * (i + 1):128 * (i + 2)], T.nx[:, 128 * k:128 * (k + 1)], T.idb[:], True, True, ["nx", "idb"], ["cv"])
+        act(T.xt[:, 0:128 * len(blocks)], T.cv[:, 128:128 * (len(blocks) + 1)], F.Copy, [], ["cv", "xt"], scale=-1.0)
         if FIRST[s] < 0:
             first_at_bank(False)
         for u in units[:LEAD]:
@@ -517,7 +538,7 @@ def rank_program(g, core, T, topo):
             if k + LEAD < len(units):
                 gather(units[k + LEAD])
             if k == FIRST[s]:
-                first_at_bank(True)
+                first_at_bank(False)
         queue_keys(2)
         for u in own:
             vector_unit(u, own[-1])
@@ -538,6 +559,8 @@ def rank_program(g, core, T, topo):
             act(T.pp[:], T.ps0[:, 0:L], F.Copy, [], ["ps0", "pp"])
         tt(T.ps2[:, 0:L], T.rb5[:, 0:L], T.th[:], A.is_lt, ["tha", "thb"], ["rb5", "ps2"])
         act(T.nd[:], T.rb5[:, 0:L], F.Copy, ["c_sc"], ["rb5", "nd"], scale=col(c_sc))
+        if s < RO - 1:
+            spread(T.nd, "nd", 0, "key0")
         scan(T.st[:], T.ps2[:, 0:L], T.zb[:], col(c_ini), A.add, A.add, ["zb", "c_ini"], ["ps2", "st"])
         tt(T.ss[:], T.st[:], T.ps2[:, 0:L], A.mult, ["st"], ["ps2", "ss"])
         spread(T.ss, "ss", 24)
@@ -555,19 +578,23 @@ def rank_program(g, core, T, topo):
         a0 = PITCH * rank + 1
         act(T[nk][:, CAP * rank:CAP * (rank + 1)], T["sw%d" % s][:, a0:a0 + CAP], F.Copy, swk, [nk + "o"])
         if s < RO - 1:
-            kis, nis = ["ki%d" % n for n in range(last + 1)], ["ni%d" % n for n in range(last + 1)]
-            ts(T.ii[:], T.ki[:], 13, 15, A.arith_shift_right, A.bitwise_and, kis, ["ii"])
-            act(T.g0[:], T.cv[:, 24:48], F.Sign, [], ["cv", "g0"], bias=-1600.0, scale=1.0 / SC)
-            act(T.g1[:], T.g0[:], F.Relu, ["g0"], ["g1"], scale=16.0)
-            act(T.qf[:], ind(queue, T.bl[:]), F.Copy, qk + ["bl", "nd"], ["qf"])
+            kis, nis = ["kk%d" % n for n in range(last + 1)], ["ni%d" % n for n in range(last + 1)]
+            ts(T.ii[:], T.kk[:, 15::16], 13, 15, A.arith_shift_right, A.bitwise_and, kis, ["ii"])
+            ts(T.g1[:], T.key0[:, 0:24], -SC, 16.0, A.is_lt, A.mult, [], ["key0", "g1"])
+            if s == 0:
+                act(T.qw[:, 0:B], T.qi[:, 0:B], F.Silu, ["qi", "cc0"], ["qw"], scale=-1.0, bias=float(QZ))
+            act(T.qf[:], ind(T.qw[:, 0:B + 16], T.bl[:]), F.Copy, ["qw", "qwp", "bl"], ["qf"])
+            mm(T.ps0[:, 0:L], T.idf[:], T.qf[:], True, False, ["idf", "qf"], ["ps0"])
             tt(T.g3[:], T.g1[:], T.tra[:], A.mult, ["g1", "tra"], ["g3"])
             tt(T.g5[:], T.g1[:], T.ii[:], A.add, ["g1", "ii"], ["g5"])
             tt(T.g6[:], T.g3[:], T.ni[:], A.max, ["g3"] + nis, ["g6"])
             tc(T.il[:], T.g5[:], ["g5"], ["il"])
             tc(T.al[:], T.g6[:], ["g6"], ["al"])
             act(T.mk[:], ind(T.wn[:], T.il[:]), F.Copy, ["wna", "wnb", "il"], ["mk"])
-            tt(ind(T.aw[:], T.al[:]), T.ag[:], T.tn[:], A.add, ["al", "aga", "agb", "tn"], ["aw"])
-            tt(ind(T.qw[:], T.ol[:]), T.qf[:], T.mk[:], A.max, ["ol", "qf", "mk"], ["qw", "qwp"])
+            tt(ind(T.aw[:], T.al[:]), T.ag[:], T.tn[:], A.add, ["al", "aga", "agb", "tn"], ["aw", "awp"])
+            mm(T.ps0[:, 0:L], T.idb[:], T.mk[:], False, True, ["idb", "mk"], ["ps0"])
+            act(T.qn[:], T.ps0[:, 0:L], F.Relu, [], ["ps0", "qn"])
+            act(ind(T.qw[:], T.ol[:]), T.qn[:], F.Silu, ["ol", "qn"], ["qw", "qwp"])
         tt(ind(T.vw[:], T.ol[:]), T.xx[:], T.td[:], A.add, ["ol", "xx", "td"], ["vw", "vwp"])
     op("s", lambda e: e.dma_start(T.yv[:], T.vw[:, 0:B]), ["vw"], ["yv"], 3.7, dma=("dyv", 16))
 
@@ -576,12 +603,9 @@ def rank_program(g, core, T, topo):
     ts(T.ci[:], T[lk][:], PK - 1, None, A.bitwise_and, None, lks, ["ci"])
     tc(T.cb[:], T.ci[:], ["ci"], ["cb"])
     op("s", lambda e: e.dma_start(T.yc[:], T.cb[:]), ["cb"], ["yc"], 2.0, dma=("dyc", 16))
-    act(T.mk[:], T[lk][:], F.Identity, lks, ["mk"], bias=BIG - base, scale=1.0 / PK)
-    act(T.ab[:], T.mk[:], F.Identity, ["mk"], ["aba", "abb"], bias=-BIG)
+    act(T.yi[:], T[lk][:], F.Identity, lks, ["yi"], bias=BIG - base, scale=1.0 / PK)
+    act(T.ab[:], T.yi[:], F.Identity, ["yi"], ["aba", "abb"], bias=-BIG)
     op("a", lambda e: e.dma_start(T.yw[:], T.ab[0::16, :]), ["aba", "abb"], ["yw"], 1.8, dma=("dyw", 16))
-    emit()
-    g.wait_ge(T.sem.sent, 2 * (NR - 1) * RO)
-    for n in ("dyv", "dyw", "dyc", "dwk", "dvp", "dqu", "dam"):
+    emit([("dwk", 16), ("dvp", 16), ("dqu", 16), ("dam", 16), ("dpay", 128), ("dpay2", 128), ("sent", 2 * (NR - 1) * RO)])
+    for n in ("dyv", "dyw", "dyc"):
         g.wait_ge(T.sem[n], 16)
-    for n in ("dpay", "dpay2"):
-        g.wait_ge(T.sem[n], 128)

import numpy as np
from concourse.bass import DstId, RemoteDMATransfer
from concourse.mybir import AluOpType, ActivationFunctionType

A = AluOpType
F = ActivationFunctionType
NR, B, W, CAP, RO = 8, 2048, 6144, 48, 3
L = NR * CAP
VW = 2560
QZ = 6207
AW = 6720
PITCH = 400
SW = 3600
PK = 1024
MID = NR * B // 2
SC = 131072.0
BIG = 8388608.0
OWN = [[9, 8, 7, 6, 5, 4], [8, 7, 6, 5, 4], [8, 7, 6, 5, 4]]
CHUNKS = [(12, 24), (4, 12), (0, 4)]
KEYS = ["key1", "key0", "rb1"]
LEAD = 2
FIRST = [-1, 2, 2]
CUT = 3072
SELF = 2
CYC, PE, WAKE, FLIGHT = 0.955e-3, 0.47e-3, 0.105, 3.0
SWEEPS, SHAKE = 500, 2.0
ORDER = []

SCRATCH = {
    "vw": ("sbuf", [128, VW], "bfloat16"), "qi": ("sbuf", [128, B + 16], "int32"), "qw": ("sbuf", [128, VW], "float32"),
    "aw": ("sbuf", [128, AW], "bfloat16"), "pw": ("sbuf", [128, QZ + 1], "int32"), "hw": ("sbuf", [128, QZ + 1], "float32"),
    "wn": ("sbuf", [128, 32], "float32"), "cc": ("sbuf", [128, 24, 256], "bfloat16"), "gg": ("sbuf", [128, L * 16], "bfloat16"),
    "vr": ("sbuf", [128, 3072], "bfloat16"), "ee": ("sbuf", [128, 24, L], "bfloat16"),
    "lm": ("sbuf", [128, 2048], "bfloat16"), "scs": ("sbuf", [128, 16], "bfloat16"), "tm": ("sbuf", [128, 16, 128], "bfloat16"),
    "rm": ("sbuf", [128, 2048], "bfloat16"), "tri": ("sbuf", [128, 24, 16], "bfloat16"), "dg": ("sbuf", [128, 24, 16], "bfloat16"),
    "bo": ("sbuf", [128, 128], "bfloat16"), "bp": ("sbuf", [128, 128], "bfloat16"), "idb": ("sbuf", [128, 128], "bfloat16"),
    "dg1": ("sbuf", [128, 128], "bfloat16"), "idn": ("sbuf", [128, 128], "bfloat16"), "idk": ("sbuf", [128, 128], "bfloat16"),
    "idf": ("sbuf", [128, 128], "float32"), "row0": ("sbuf", [128, 128], "float32"), "nd": ("sbuf", [128, L], "bfloat16"),
    "zb": ("sbuf", [128, L], "bfloat16"), "c32": ("sbuf", [128, L], "bfloat16"), "rowc": ("sbuf", [128, 192], "bfloat16"),
    "rst": ("sbuf", [128, 192], "bfloat16"), "dsf": ("sbuf", [128, 4, 128], "float32"),
    "pi": ("sbuf", [128, 4], "int32"), "io128": ("sbuf", [128, 128], "bfloat16"), "iog": ("sbuf", [128, 128], "bfloat16"),
    "io16": ("sbuf", [128, 16], "bfloat16"), "trv": ("sbuf", [128, 24], "float32"), "tra": ("sbuf", [128, 24], "float32"),
    "wc": ("sbuf", [128, 48], "float32"), "col": ("sbuf", [128, 20], "float32"), "wkz": ("sbuf", [128, L], "int32"),
    "land1": ("sbuf", [128, L], "int32"), "land2": ("sbuf", [128, L], "int32"), "land3": ("sbuf", [128, L], "int32"),
    "sw0": ("sbuf", [128, SW], "int32"), "sw1": ("sbuf", [128, SW], "int32"), "sw2": ("sbuf", [128, SW], "int32"),
    "bq": ("sbuf", [128, L], "float16"), "bl": ("sbuf", [128, 24], "uint16"), "bf": ("sbuf", [128, 24], "float32"),
    "b16": ("sbuf", [128, L], "uint16"), "ci": ("sbuf", [128, L], "int32"), "yi": ("sbuf", [128, L], "float32"),
    "cb": ("sbuf", [128, L], "bfloat16"), "q16": ("sbuf", [128, L], "uint16"), "qf": ("sbuf", [128, L], "float32"),
    "bx": ("sbuf", [128, 24], "uint16"), "qx": ("sbuf", [128, L], "float32"),
    "qt": ("sbuf", [128, 12, 32], "float32"), "kk": ("sbuf", [128, L], "int32"),
    "ki": ("sbuf", [128, 24], "int32"), "ni": ("sbuf", [128, 24], "int32"), "ii": ("sbuf", [128, 24], "int32"),
    "nl": ("sbuf", [128, 24], "uint16"), "il": ("sbuf", [128, 24], "uint16"), "sl": ("sbuf", [128, 24], "uint16"),
    "ol": ("sbuf", [128, 24], "uint16"), "al": ("sbuf", [128, 24], "uint16"),
    "e1": ("sbuf", [128, 24], "float32"), "e2": ("sbuf", [128, 24], "float32"), "e3": ("sbuf", [128, 24], "float32"),
    "g0": ("sbuf", [128, 24], "float32"), "g1": ("sbuf", [128, 24], "float32"), "g3": ("sbuf", [128, 24], "float32"),
    "g5": ("sbuf", [128, 24], "float32"), "g6": ("sbuf", [128, 24], "float32"),
    "basev": ("sbuf", [128, 24], "float32"), "ho": ("sbuf", [128, 24], "float32"),
    "x1": ("sbuf", [128, L], "bfloat16"), "xx": ("sbuf", [128, L], "bfloat16"), "xt": ("sbuf", [128, L], "bfloat16"),
    "nx": ("sbuf", [128, L], "bfloat16"), "wv": ("sbuf", [128, L], "bfloat16"),
    "nh": ("sbuf", [128, L], "uint16"), "ag": ("sbuf", [128, L], "bfloat16"), "p0": ("sbuf", [128, L], "float32"),
    "ab": ("sbuf", [128, L], "float32"), "th": ("sbuf", [128, L], "bfloat16"), "tn": ("sbuf", [128, L], "bfloat16"),
    "td": ("sbuf", [128, L], "bfloat16"), "pp": ("sbuf", [128, L], "float32"), "st": ("sbuf", [128, L], "float32"),
    "ss": ("sbuf", [128, L], "float16"), "mk": ("sbuf", [128, L], "bfloat16"), "qn": ("sbuf", [128, L], "float32"),
    "ps0": ("psum", [128, 512], "float32"), "ps1": ("psum", [128, 512], "float32"), "ps2": ("psum", [128, 512], "float32"),
    "key0": ("psum", [128, 512], "float32"), "key1": ("psum", [128, 512], "float32"),
    "cv": ("psum", [128, 512], "float32"), "rb1": ("psum", [128, 512], "float32"), "rb5": ("psum", [128, 512], "float32"),
}
BANKS = [k for k, v in SCRATCH.items() if v[0] == "psum"]
SEMAPHORES = ["qv", "qa", "qt", "qp", "dwk", "dvp", "dqu", "dam", "dpay", "dpay2", "dyv", "dyw", "dyc", "arr0", "arr1", "arr2", "sent"]


def make_queues(g, T):
    calls, last_w, readers, rows = [], {}, {}, {}

    def op(q, fn, r=(), w=(), us=0.1, dma=None, ext=None, row=None):
        deps = [(last_w[k], "raw") for k in r if k in last_w]
        row = q if q == "s" else row
        if row in rows:
            deps.append((rows[row], "order"))
        if row:
            rows[row] = len(calls)
        for k in w:
            if k in last_w:
                deps.append((last_w[k], "waw"))
            deps += [(o, "war") for o in readers.get(k, ())]
        i = len(calls)
        calls.append({"q": q, "fn": fn, "deps": deps, "dma": dma, "ext": ext, "inc": False, "us": us, "id": i})
        for k in w:
            last_w[k] = i
            readers[k] = []
        for k in r:
            readers.setdefault(k, []).append(i)

    def free_edge(o, d, kind):
        return d["q"] == o["q"] and o["dma"] is None and d["dma"] is None and d["ext"] is None and (kind == "war" or o["q"] == "t")

    def order():
        before, after = [[] for o in calls], [[] for o in calls]
        us = [o["us"] for o in calls]
        hold = [0.05 if o["dma"] else 0.0 if o["ext"] else o["us"] for o in calls]
        for o in calls:
            for j, kind in o["deps"]:
                lag = hold[j] - us[j] if kind == "order" else 0.0 if free_edge(o, calls[j], kind) else WAKE
                before[o["id"]].append((j, lag))
                after[j].append((o["id"], lag))

        def place(turn, edges, back):
            end, busy = [0.0] * len(calls), {q: [] for q in "vatps"}
            for i in turn:
                skip = us[i] - hold[i] if back else 0.0
                t = max([end[j] + lag for j, lag in edges[i]] + [0.0]) + skip
                row = busy[calls[i]["q"]]
                k, hi = 0, len(row)
                while k < hi:
                    if row[(k + hi) // 2][1] <= t:
                        k = (k + hi) // 2 + 1
                    else:
                        hi = (k + hi) // 2
                while k < len(row) and row[k][0] < t + hold[i]:
                    t = max(t, row[k][1])
                    k += 1
                row.insert(k, (t, t + hold[i]))
                end[i] = t - skip + us[i]
            return end

        if not ORDER:
            every = range(len(calls))
            rng = np.random.default_rng(1)
            best = end = place(every, before, False)
            for sweep in range(SWEEPS):
                back = place(sorted(every, key=lambda i: (us[i] - hold[i] - end[i], -i)), after, True)
                end = place(sorted(every, key=lambda i: (-back[i], i)), before, False)
                if max(end) <= max(best):
                    best = end
                if sweep % 2:
                    at, when = float(rng.random()) * max(best), []
                    for i in every:
                        t = best[i] - us[i]
                        t += SHAKE * float(rng.random()) if abs(t - at) < 2 * SHAKE else 0.0
                        when.append(max([t] + [when[j] + 1e-6 for j, lag in before[i]]))
                    end = place(sorted(every, key=lambda i: when[i]), before, False)
            ORDER.extend(sorted(every, key=lambda i: (best[i] - us[i], i)))
        return [calls[i] for i in ORDER]

    def emit(past):
        engine = {"v": g.vector, "a": g.scalar, "t": g.tensor, "p": g, "s": g.sync}
        sem = {"v": T.sem.qv, "a": T.sem.qa, "t": T.sem.qt, "p": T.sem.qp}
        known = {q: {} for q in engine}
        seq = {q: 0 for q in engine}
        ops = order()
        for o in ops:
            o["seq"] = seq[o["q"]]
            o["waits"] = []
            o["clock"] = {}
            if o["ext"] is not None:
                continue
            seq[o["q"]] += 1
            need = {}
            kn = known[o["q"]]
            for j, kind in o["deps"]:
                d = calls[j]
                if kind == "order":
                    continue
                if d["ext"] is not None or d["dma"] is not None:
                    name = d["ext"] or d["dma"]
                    if kn.get(name[0], 0) < name[1]:
                        need[name[0]] = (max(need.get(name[0], (0, 0))[0], name[1]), j)
                    continue
                if free_edge(o, d, kind):
                    continue
                if kn.get(d["q"], -1) < d["seq"] and need.get(d["q"], (-1, 0))[0] < d["seq"]:
                    need[d["q"]] = (d["seq"], j)
            for key, (val, j) in need.items():
                for k2, v2 in calls[j]["clock"].items():
                    if k2 != key and kn.get(k2, -1) < v2:
                        kn[k2] = v2
            for key, (val, j) in need.items():
                if not any(k2 != key and calls[j2]["clock"].get(key, -1) >= val for k2, (v2, j2) in need.items()):
                    o["waits"].append((key, val, j))
                    if key in sem:
                        calls[j]["inc"] = True
                kn[key] = max(kn.get(key, -1), val)
            o["clock"] = dict(kn)
        count = {q: 0 for q in engine}
        for o in ops:
            count[o["q"]] += 1 if o["inc"] else 0
            o["count"] = count[o["q"]]
        for o in ops:
            if o["ext"] is not None:
                continue
            e = engine[o["q"]]
            for key, val, j in o["waits"]:
                e.wait_ge(sem[key] if key in sem else T.sem[key], calls[j]["count"] if key in sem else val)
            ins = o["fn"](e)
            if o["dma"] is not None:
                ins.then_inc(T.sem[o["dma"][0]], 16)
            elif o["inc"]:
                ins.then_inc(sem[o["q"]], 1)
        for name, val in past:
            g.wait_ge(T.sem[name], val)
        for q in "ptva":
            if count[q]:
                g.wait_ge(sem[q], count[q])
    return op, emit


def rank_program(g, core, T, topo):
    rank = T.rank_of(core)
    if rank is None:
        return
    op, emit = make_queues(g, T)
    c_m, c_g, c_p, c_x, c_h0, c_h1, c_ctr, c_sgn, c_ini, c_lt8, c_ts, c_tb, c_d1, c_r0, c_sc = range(15)

    def col(k):
        return T.col[:, k:k + 1]

    def size(ap):
        n = 1
        for k in ap.shape[1:]:
            n *= k
        return n

    def ind(win, off):
        return (win.indirect(off), 16 * size(off))

    def length(out, in_, cycles, *others):
        if isinstance(out, tuple):
            return 0.055 + out[1] * 3.8 * CYC, out[0], in_
        if isinstance(in_, tuple):
            return 0.06 + in_[1] * 1.56 * CYC, out, in_[0]
        if cycles is None:
            cycles = 0.5 if all("16" in str(x.dtype) for x in (out, in_) + others) else 1.0
        return 0.047 + size(out) * cycles * CYC, out, in_

    def ts(out, in0, s1, s2, o0, o1, r, w):
        us, out, in0 = length(out, in0, None)
        op("v", (lambda e: e.tensor_scalar(out, in0, s1, s2, o0, o1)) if o1 else (lambda e: e.tensor_scalar(out, in0, s1, None, o0)), r, w, us)

    def tt(out, in0, in1, o, r, w):
        us, out, in0 = length(out, in0, 1.0 if any(k in BANKS for k in w) else 2.0)
        op("v", lambda e: e.tensor_tensor(out, in0, in1, o), r, w, us)

    def tc(out, in_, r, w):
        us, out, in_ = length(out, in_, None)
        op("v", lambda e: e.tensor_copy(out, in_), r, w, us)

    def scan(out, d0, d1, ini, o0, o1, r, w):
        op("v", lambda e: e.tensor_tensor_scan(out, d0, d1, ini, o0, o1), r, w, length(out, d0, None, d1)[0])

    def fill(out, k, w):
        op("v", lambda e: e.memset(out, k), [], w, length(out, out, None)[0])

    def act(out, in_, f, r, w, bias=0.0, scale=1.0, row=None):
        fixed = (0.0 if isinstance(in_, tuple) else 0.005) + (1.3 if f == F.Silu and scale != 1.0 else 0.0)
        us, out, in_ = length(out, in_, 1.0)
        us += fixed
        if bias == 0.0 and scale == 1.0:
            op("a", lambda e: e.activation(out, in_, f), r, w, us, row=row)
        else:
            op("a", lambda e: e.activation(out, in_, f, bias=bias, scale=scale), r, w, us, row=row)

    sums = {}

    def in_group(start, stop, r, w):
        bank = w[0]
        if start:
            sums[bank] = []
            return r, w + [bank + "+"]
        if stop:
            return r + sums[bank] + [bank + "+"], w
        sums[bank].append("%s+%d" % (bank, len(sums[bank])))
        return r + [bank + "+"], sums[bank][-1:]

    def mm(out, lhs, rhs, start, stop, r, w):
        r, w = in_group(start, stop, r, w)
        op("t", lambda e: e.matmul(out, lhs, rhs, start, stop), r, w, max(64, size(rhs)) * (4 if "32" in str(rhs.dtype) else 1) * PE)

    def mms(run, r, w):
        r, w = in_group(run[0][3], run[-1][4], r, w)
        op("t", lambda e: [e.matmul(*c) for c in run][-1], r, w, len(run) * 64 * PE)

    def iota(out, pattern, base, cm, w):
        op("p", lambda e: e.iota(out, pattern, base, cm, allow_small_or_imprecise_dtypes=True), [], w, 0.145 + 2 * size(out) * CYC)

    def pcopy(out, in_, n, r, w):
        op("p", lambda e: e.affine_select(out, in_, [[0, n]], A.is_ge, 0.0, 0, 0), r, w, 0.19 + 2 * size(out) * CYC)

    def payees(rows, r, us, sem):
        for j in rows:
            op("s", lambda e, j=j: e.dma_start(T.pw[j::16, 0:W], T.pay[:]), r, ["pw%d" % j], us, dma=(sem, 128))

    fill(T.wkz[:], 0, ["wkz"])
    op("s", lambda e: e.dma_start(T.vw[:, 0:B], T.vp[:]), [], ["vw"], 3.5, dma=("dvp", 16))
    op("s", lambda e: e.dma_start(T.wkz[0::16, :], T.wk[:]), [], ["wkz"], 3.0, dma=("dwk", 16))
    op("s", lambda e: e.dma_start(T.qi[:, 0:B], T.qu[:]), [], ["qi"], 6.8, dma=("dqu", 16))
    op("s", lambda e: e.dma_start(T.aw[:, 0:W], T.am[:]), [], ["aw"], 12.3, dma=("dam", 16))
    iota(T.pi[:, 0:1], [[1, 1]], 0, 1, ["pi0"])
    iota(T.iog[:], [[1, 8], [0, 16]], 0, 0, ["iog"])
    iota(T.io128[:], [[1, 128]], 0, 0, ["io128"])
    iota(T.io16[:], [[1, 16]], 0, 0, ["io16"])
    iota(T.pw[:, 0:CUT], [[0, CUT]], 0, 0, ["pwa"])
    act(T.pw[:, CUT:CUT + B], T.vw[:, 0:B], F.Copy, ["vw"], ["pwc"], scale=0.0)
    fill(T.pw[:, CUT + B:], 0, ["pwb"])
    fill(T.aw[:, W:QZ + 1], 0.0, ["awp"])
    payees(range(8), ["pwa", "pwb", "pwc"], 10.0, "dpay")

    iota(T.rowc[:], [[0, 12], [8192, 16]], 0, 0, ["rowc"])
    iota(T.trv[:], [[16, 24]], 2064, 1, ["trv"])
    iota(T.hw[:, 0:W - 1], [[1, W - 1]], 0, 0, ["hw"])
    iota(T.hw[:, W - 1:], [[0, QZ + 2 - W]], 60000, 0, ["hwc"])
    for s in range(RO):
        for d in range(NR):
            a0 = PITCH * d + 1
            iota(T["sw%d" % s][:, a0:a0 + CAP], [[0, CAP]], (d * B + B - MID) * PK, 0, ["sw%d_%d" % (s, d)])
    fill(T.lm[:], 0.0, ["lm0"])
    ts(T.pi[:, 1:2], T.pi[:, 0:1], 15, None, A.bitwise_and, None, ["pi0"], ["pi1"])
    ts(T.pi[:, 2:3], T.pi[:, 0:1], 4, None, A.arith_shift_right, None, ["pi0"], ["pi2"])
    ts(T.pi[:, 3:4], T.pi[:, 0:1], 4, 1, A.arith_shift_right, A.bitwise_and, ["pi0"], ["pi3"])
    tc(col(c_p), T.pi[:, 0:1], ["pi0"], ["c_p"])
    tc(col(c_g), T.pi[:, 2:3], ["pi2"], ["c_g"])
    tc(col(c_m), T.pi[:, 1:2], ["pi1"], ["c_m"])
    tc(col(c_h1), T.pi[:, 3:4], ["pi3"], ["c_h1"])
    ts(T.bo[:], T.iog[:], col(c_g), None, A.is_equal, None, ["iog", "c_g"], ["bo"])
    fill(T.scs[:], SC, ["scs"])
    for k in range(8):
        ts(T.lm[:, 16 * k:2048 - 112 + 16 * k:129], T.scs[:], T.bo[:, 16 * k:16 * k + 1], None, A.mult, None, ["bo", "lm0", "scs"], ["lm%d" % (k + 1)])
    fill(T.vw[:, B:B + 16], 0.0, ["vwp"])
    fill(T.qw[:, B:B + 16], 0.0, ["qwp"])
    fill(T.qi[:, B:B + 16], W - 1, ["qip"])
    ts(col(c_sgn), col(c_m), 8.0, -2.0, A.is_equal, A.mult, ["c_m"], ["c_sgn0"])
    ts(col(c_h0), col(c_h1), -1.0, 1.0, A.mult, A.add, ["c_h1"], ["c_h0"])
    ts(col(c_x), col(c_h1), -32.0, 16.0, A.mult, A.add, ["c_h1"], ["c_x0"])
    ts(T.wc[:, 0:16], T.io16[:], col(c_m), None, A.is_gt, None, ["io16", "c_m"], ["wc0"])
    ts(T.wc[:, 16:32], T.io16[:], col(c_m), -0.5, A.is_equal, A.mult, ["io16", "c_m"], ["wc1"])
    ts(T.bp[:], T.bo[:], 4.0, None, A.mult, None, ["bo"], ["bp0"])
    ts(col(c_sgn), col(c_sgn), 1.0, None, A.add, None, ["c_sgn0"], ["c_sgn"])
    tt(col(c_x), col(c_x), col(c_p), A.add, ["c_x0", "c_p"], ["c_x"])
    tt(T.wc[:, 32:48], T.wc[:, 0:16], T.wc[:, 16:32], A.add, ["wc0", "wc1"], ["wc"])
    ts(T.bp[:, 8::16], T.bo[:, 8::16], -4.0, None, A.mult, None, ["bo", "bp0"], ["bp"])
    ts(T.idb[:], T.io128[:], col(c_p), None, A.is_equal, None, ["io128", "c_p"], ["idb"])
    ts(col(c_d1), col(c_sgn), -1.0 / 256, None, A.mult, None, ["c_sgn"], ["c_d1"])
    ts(col(c_sc), col(c_sgn), -256.0, None, A.mult, None, ["c_sgn"], ["c_sc"])
    for a in range(16):
        act(T.tm[:, a, :], T.bp[:], F.Copy, ["bp", "wc"], ["tm%d" % a], scale=T.wc[:, 32 + a:33 + a])
    act(T.tri[:, 0, :], T.wc[:, 32:48], F.Copy, ["wc"], ["tri"])
    for c in (1, 2):
        act(T.tri[:, c:min(2 * c, 24), :], T.tri[:, 0:min(c, 24 - c), :], F.Copy, ["tri"], ["tri"])
    fill(T.c32[:], 1.0 / 32, ["c32"])
    ts(T.dg1[:], T.io128[:], col(c_p), col(c_d1), A.is_equal, A.mult, ["io128", "c_p", "c_d1"], ["dg1"])
    for k, (pc, hc) in enumerate(((c_p, c_h0), (c_x, c_h0), (c_p, c_h1), (c_x, c_h1))):
        ts(T.dsf[:, k, :], T.io128[:], col(pc), col(hc), A.is_equal, A.mult, ["io128", "c_p", "c_x", "c_h0", "c_h1"], ["dsf%d" % k])
    for i in (0, 8):
        act(T.rm[:, i::16], T.idb[:], F.Copy, ["idb"], ["rm%d" % i])
    for k in (8, 4, 2):
        act(T.rm[:, k // 2::k], T.rm[:, 0::k], F.Copy, ["rm0", "rm8"], ["rm"])
    fill(T.zb[:], 0.0, ["zb"])
    fill(T.rst[:], 0.0, ["rst0"])
    fill(T.wn[:, 16:32], 0.0, ["wnb"])
    act(T.idn[:], T.idb[:], F.Copy, ["idb"], ["idn"], scale=-1.0)
    act(T.idf[:], T.idb[:], F.Copy, ["idb"], ["idf"])
    ts(col(c_r0), col(c_m), 0.0, None, A.is_equal, None, ["c_m"], ["c_r0"])
    act(T.row0[:], T.bo[:], F.Copy, ["bo", "c_r0"], ["row0"], scale=col(c_r0))
    ts(col(c_ctr), col(c_m), -2048.0, MID - 1023.5, A.mult, A.add, ["c_m"], ["c_ctr"])
    ts(col(c_ini), col(c_m), float(PITCH), -1592.0, A.mult, A.add, ["c_m"], ["c_ini"])
    ts(col(c_ts), col(c_m), 8.0, -1.0, A.is_lt, A.mult, ["c_m"], ["c_ts"])
    ts(col(c_lt8), col(c_m), 8.0, 1025.0, A.is_lt, A.mult, ["c_m"], ["c_lt8"])
    ts(T.wn[:, 0:16], T.io16[:], col(c_m), -8192.0, A.is_equal, A.mult, ["io16", "c_m"], ["wna"])
    ts(T.tra[:], T.trv[:], 1.0 / 16, (QZ + 1 - 2064.0) / 16, A.mult, A.add, ["trv"], ["tra"])
    fill(T.rst[:, 0::16], -16777216.0, ["rst0"])
    ts(col(c_tb), col(c_lt8), -1.0, None, A.add, None, ["c_lt8"], ["c_tb"])

    lms = ["lm%d" % a for a in range(9)]
    tms = ["tm%d" % a for a in range(16)]
    ees = ["ee%d" % c for c in range(24)]
    dsf = ["dsf%d" % k for k in range(4)]

    def pairs(rb, buf, own, r, c0, c1):
        if c1 == 24:
            mm(T[rb][:, 0:L], T.bp[:], T.c32[:], True, False, ["bp", "c32"], [rb])
        for c in range(c1 - 1, c0 - 1, -1):
            ts(T.ee[:, c, 0:L - 16 * c], buf[:, 16 * c:L], own[:, c:c + 1], None, A.is_equal, None, r, ["ee%d" % c])
            if c < 23:
                mm(T[rb][:, 16 * (c + 1):L], T.bp[:], T.ee[:, c, 16:L - 16 * c], False, False, ["bp", "ee%d" % c], [rb])

    def within(rb, c0):
        mms([(T[rb][:, 16 * c0 + a:L:16], T.tm[:, a, :], T.ee[:, c0:, a], False, a == 15 and c0 == 0) for a in range(16)], tms + ees[c0:], [rb])

    def within_below(rb, c0):
        tt(T.dg[:, 0:c0, :], T.ee[:, 0:c0, 0:16], T.tri[:, 0:c0, :], A.mult, ees[:c0] + ["tri"], ["dg"])
        mm(T[rb][:, 0:16 * c0], T.bp[:], T.dg[:, 0:c0, :], False, True, ["bp", "dg"], [rb])

    def spread(src, key, c0, bank="cv"):
        mms([(T[bank][:, c0:c0 + 24], T.lm[:, 128 * a:128 * a + 128], src[:, a::16], a == 0, a == 15) for a in range(16)], lms + [key], [bank])

    def gather(u):
        act(T.gg[:, 512 * u:512 * (u + 1)], ind(T.aw[:, 0:QZ + 1], T.q16[:, 32 * u:32 * (u + 1)]), F.Copy, ["aw", "awp", "q16"], ["gg%d" % u], row="units")

    def sign(u, pk):
        mm(T[pk][:], T.idb[:], T.gg[:, 512 * u:512 * (u + 1)], True, False, ["idb", "gg%d" % u], [pk])
        mm(T[pk][:], T.xt[:, 128 * blocks.index(u // 4):128 * blocks.index(u // 4) + 128], T.rm[:, 512 * (u % 4):512 * (u % 4 + 1)], False, True, ["xt", "rm"], [pk])
        act(T.cc[:, 2 * u:2 * u + 2, :], T[pk][:], F.Sign, [], [pk, "cc%d" % (2 * u), "cc%d" % (2 * u + 1)], bias=0.5, row="units")

    def vector_unit(u, u0):
        for c in (2 * u + 1, 2 * u):
            tt(T.cc[:, c, :], ind(T.aw[:, 0:QZ + 1], T.q16[:, 16 * c:16 * (c + 1)]), T.vr[:, 256 * (c - 2 * u0):256 * (c - 2 * u0 + 1)],
               A.is_ge, ["aw", "awp", "q16", "vr%d" % u], ["cc%d" % c])

    def repeat(copy, units, u0):
        lo, hi, keys = 512 * (units[-1] - u0), 512 * (units[0] - u0 + 1), ["vr%d" % u for u in units]
        for i in (0, 8):
            copy(T.vr[:, lo + i:hi:16], T.nx[:, 32 * units[-1]:32 * units[0] + 32], (hi - lo) // 16, ["nx"], [k + "_%d" % i for k in keys])
        for k in (8, 4, 2):
            copy(T.vr[:, lo + k // 2:hi:k], T.vr[:, lo:hi:k], (hi - lo) // k, [x + y for x in keys for y in ("_0", "_8")], keys)

    def vcopy(out, in_, n, r, w):
        tc(out, in_, r, w)

    def score(q, n):
        kb, off = KEYS[n], 64 * q - 16 * CHUNKS[n][0]
        mms([(T[kb][:, off:off + 64], T.lm[:, 128 * a:128 * a + 128], T.cc[:, 4 * q:4 * q + 4, 16 * a:16 * a + 16], False, a == 15 and off == 0) for a in range(16)],
            lms + ["cc%d" % c for c in range(4 * q, 4 * q + 4)], [kb])

    def queue_keys(n):
        (c0, c1), kb = CHUNKS[n], KEYS[n]
        h = c0 // 12
        mm(T[kb][:, 0:16 * (c1 - c0)], T.idb[:], T.rowc[:, 0:16 * (c1 - c0)], True, False, ["idb", "rowc"], [kb])
        for j in range(2):
            gx = 16 * (h ^ j)
            mm(T[kb][:, 0:16 * (c1 - c0)], T.dsf[:, 2 * h + j, :], T.qt[:, c0 - 12 * h:c1 - 12 * h, gx:gx + 16], False, False, dsf + ["qt"], [kb])

    def best(n):
        c0, c1 = CHUNKS[n]
        kb, hs, ls, k = KEYS[n], slice(c0, c1), slice(16 * c0, 16 * c1), "%d" % n
        for q in range(c1 // 4 - 1, c0 // 4 - 1, -1):
            score(q, n)
        scan(T.kk[:, ls], T.rst[:, 0:16 * (c1 - c0)], T[kb][:, 0:16 * (c1 - c0)], 0.0, A.add, A.max, ["rst0"], [kb, "kk" + k])
        ts(T.ni[:, hs], T.kk[:, 16 * c0 + 15:16 * c1:16], 8191, None, A.bitwise_and, None, ["kk" + k], ["ni" + k])
        tc(T.nl[:, hs], T.ni[:, hs], ["ni" + k], ["nl" + k])
        tt(T.ho[:, hs], T.ni[:, hs], T.basev[:, hs], A.add, ["ni" + k, "basev"], ["ho" + k])
        tc(T.nh[:, ls], ind(T.hw[:], T.nl[:, hs]), ["hw", "hwc", "nl" + k], ["nh" + k])
        if c0 == 0:
            within("rb5", c1)
        pairs("rb5", T.nh, T.ho, ["nh%d" % i for i in range(n + 1)] + ["ho" + k], c0, c1)
        if c0 == 0:
            within_below("rb5", c1)

    def of_lines(c0, c1, r, k):
        hs, ls = slice(c0, c1), slice(16 * c0, 16 * c1)
        act(T.p0[:, ls], ind(T.pw[:], T.nl[:, hs]), F.Copy, ["pw7", "pw15"] + r, ["p0" + k], bias=-float(MID * PK), scale=float(PK))
        act(T.ab[:, ls], T.p0[:, ls], F.Abs, ["p0" + k, "c_ctr"], ["ab" + k], bias=col(c_ctr), scale=1.0 / PK)
        act(T.th[:, ls], T.ab[:, ls], F.Sign, ["ab" + k, "c_ts", "c_tb"], ["th" + k], bias=col(c_tb), scale=col(c_ts))
        act(T.ag[:, ls], ind(T.aw[:, 0:QZ + 1], T.nl[:, hs]), F.Copy, ["aw", "awp"] + r, ["ag" + k])

    def first_at_bank(masked):
        pairs("rb1", T.b16, T.bf, ["b16", "bf"], 12, 24)
        mm(T.rb1[:, 0:L], T.dg1[:], T.nx[:], False, False, ["dg1", "nx"], ["rb1"])
        pairs("rb1", T.b16, T.bf, ["b16", "bf"], 0, 12)
        if masked:
            within_below("rb1", 24)
        else:
            within("rb1", 0)
        act(T.wv[:], T.rb1[:, 0:L], F.Copy, ["c_sc"], ["rb1", "wv"], scale=col(c_sc), row="units")
        spread(T.wv, "wv", 48)
        ts(T.basev[:], T.cv[:, 48:72], 0.5 * SC, 20000.0, A.is_lt, A.mult, [], ["cv", "basev"])
        ts(T.e1[:], T.cv[:, 48:72], -0.5 * SC, None, A.is_lt, None, [], ["cv", "e1"])
        tt(T.e2[:], T.e1[:], T.trv[:], A.mult, ["e1", "trv"], ["e2"])
        tt(T.e3[:], T.e2[:], T.bf[:], A.max, ["e2", "bf"], ["e3"])
        tc(T.ol[:], T.e3[:], ["e3"], ["ol"])

    def send(s, to_buf):
        def fn(e):
            tr = []
            nth = [0, 0]
            for d in range(1, NR):
                to = (rank + d) % NR
                dst = T.cores[to]
                rid, pid, _ = topo.addr(dst)
                near = int(topo.die(dst) == topo.die(core))
                k = 4 * nth[near] + near
                nth[near] += 1
                m = sum(1 << x for x in topo.engines(core, dst)[k:k + 3:2])
                tr.append(RemoteDMATransfer(dst_ids=[DstId(rid=rid, pnc=pid)], dma_engine_mask=m, remote_sem=T.sem["arr%d" % s],
                                            srcs=[T["sw%d" % s][:, PITCH * to + 1:PITCH * to + 1 + CAP]],
                                            dsts=[T[to_buf][:, CAP * rank:CAP * (rank + 1)]]))
            return e.remote_dma_fused(tr, local_sem=T.sem.sent)
        return fn

    blocks = []
    base = float(B * rank - MID)
    for s in range(RO):
        lk = "land%d" % s
        lks = [lk, lk + "o"]
        own = OWN[s]
        units = [u for u in range(11, -1, -1) if u not in own]
        if s:
            land = T[lk]
            act(T.bq[:], land[:], F.Identity, lks, ["bq"], bias=-base, scale=1.0 / PK)
            spread(T.bq, "bq", 0)
            ts(T.ci[:], land[:], PK - 1, None, A.bitwise_and, None, lks, ["ci"])
            tc(T.b16[:], T.bq[:], ["bq"], ["b16"])
            queue, qk = T.qw[:, 0:B + 16], ["qw", "qwp"]
        else:
            tc(T.bq[:], T.wkz[:], ["wkz"], ["bq"])
            spread(T.bq, "bq", 0)
            mm(T.rb1[:, 0:L], T.bo[:], T.bq[:], True, True, ["bo", "bq"], ["rb1"])
            tc(T.b16[:], T.rb1[:, 0:L], [], ["rb1", "b16"])
            queue, qk = T.qi[:], ["qi", "qip"]
        ts(T.bl[:], T.cv[:, 0:24], 1.0 / (16 * SC if s else SC), None, A.mult, None, [], ["cv", "bl"])
        tc(T.bf[:], T.bl[:], ["bl"], ["bf"])
        sg, q0 = (-1.0, QZ + 0.25) if s else (1.0, 0.0)
        act(T.q16[:], ind(queue, T.bl[:]), F.Copy, qk + ["bl"], ["q16"], scale=sg, bias=q0)
        for h in range(2):
            tc(T.bx[:, h::2], T.bl[:, 12 * h:12 * h + 12], ["bl"], ["bx%d" % h])
        act(T.qx[:], ind(queue, T.bx[:]), F.Copy, qk + ["bx0", "bx1"], ["qx"], scale=sg, bias=q0)
        op("v", lambda e: e.transpose(T.qt[:], T.qx[:]), ["qx"], ["qt"], 0.4)
        queue_keys(0)
        queue_keys(1)
        if s:
            tt(T.x1[:], ind(T.vw[:, 0:B + 16], T.bl[:]), T.ci[:], A.subtract, ["vw", "vwp", "bl", "ci"], ["x1"])
            ts(T.xx[:], T.x1[:], -255.0, None, A.max, None, ["x1"], ["xx"])
            ts(T.nx[:], T.xx[:], -1.0, 0.0, A.mult, A.max, ["xx"], ["nx"])
            for copy, k0, k1 in ((vcopy, 0, 1), (pcopy, 1, 3), (pcopy, 3, 5)):
                repeat(copy, own[k0:k1], own[-1])
        else:
            act(T.xx[:], ind(T.vw[:, 0:B + 16], T.bl[:]), F.Copy, ["vw", "vwp", "bl"], ["xx"])
            act(T.nx[:], T.xx[:], F.Relu, ["xx"], ["nx"], scale=-1.0)
            repeat(vcopy, own, own[-1])
        blocks[:] = sorted(set(u // 4 for u in units), reverse=True)
        for i, k in enumerate(blocks):
            mm(T.cv[:, 128 * (i + 1):128 * (i + 2)], T.nx[:, 128 * k:128 * (k + 1)], T.idb[:], True, True, ["nx", "idb"], ["cv"])
        act(T.xt[:, 0:128 * len(blocks)], T.cv[:, 128:128 * (len(blocks) + 1)], F.Copy, [], ["cv", "xt"], scale=-1.0)
        if FIRST[s] < 0:
            first_at_bank(False)
        for u in units[:LEAD]:
            gather(u)
        for k, u in enumerate(units):
            sign(u, "ps%d" % (k % 3))
            if k + LEAD < len(units):
                gather(units[k + LEAD])
            if k == FIRST[s]:
                first_at_bank(False)
        queue_keys(2)
        for u in own:
            vector_unit(u, own[-1])
        for n in range(len(CHUNKS)):
            best(n)
        last = len(CHUNKS) - 1
        nls = ["nl%d" % n for n in range(last + 1)]
        mm(T.ps1[:, 0:L], T.idb[:], T.nx[:], True, True, ["idb", "nx"], ["ps1"])
        of_lines(CHUNKS[last][1], 24, nls[:last], "a")
        of_lines(0, CHUNKS[last][1], nls[last:], "b")
        tt(T.ps1[:, 0:L], T.ag[:], T.ps1[:, 0:L], A.min, ["aga", "agb"], ["ps1"])
        if s:
            tt(T.pp[:], T.p0[:], T.ps1[:, 0:L], A.add, ["p0a", "p0b"], ["ps1", "pp"])
        act(T.tn[:], T.ps1[:, 0:L], F.Copy, [], ["ps1", "tn"], scale=-1.0)
        if s == 0:
            mm(T.ps0[:, 0:L], T.row0[:], T.p0[:], True, False, ["row0", "p0a", "p0b"], ["ps0"])
            mm(T.ps0[:, 0:L], T.idn[:], T.tn[:], False, True, ["idn", "tn"], ["ps0"])
            act(T.pp[:], T.ps0[:, 0:L], F.Copy, [], ["ps0", "pp"])
        tt(T.ps2[:, 0:L], T.rb5[:, 0:L], T.th[:], A.is_lt, ["tha", "thb"], ["rb5", "ps2"])
        act(T.nd[:], T.rb5[:, 0:L], F.Copy, ["c_sc"], ["rb5", "nd"], scale=col(c_sc))
        if s < RO - 1:
            spread(T.nd, "nd", 0, "key0")
        scan(T.st[:], T.ps2[:, 0:L], T.zb[:], col(c_ini), A.add, A.add, ["zb", "c_ini"], ["ps2", "st"])
        tt(T.ss[:], T.st[:], T.ps2[:, 0:L], A.mult, ["st"], ["ps2", "ss"])
        spread(T.ss, "ss", 24)
        ts(T.sl[:], T.cv[:, 24:48], 1.0 / SC, 1592.0, A.mult, A.add, [], ["cv", "sl"])
        swk = ["sw%d_%d" % (s, d) for d in range(NR)]
        tc(ind(T["sw%d" % s][:], T.sl[:]), T.pp[:], ["sl", "pp"], swk)
        nk = "land%d" % (s + 1)
        op("p", send(s, nk), swk, ["gone%d" % s], 1.0)
        op("p", None, ["gone%d" % s], [nk], FLIGHT - (1.0 if s else 0.0), ext=("arr%d" % s, 2 * (NR - 1)))
        if s == 0:
            payees(range(8, 16), [nk, "p0a", "p0b"], 8.0, "dpay2")
        mm(T.key1[:, 0:L], T.idn[:], T.tn[:], True, False, ["idn", "tn"], ["key1"])
        mm(T.key1[:, 0:L], T.idb[:], T.nd[:], False, True, ["idb", "nd"], ["key1"])
        act(T.td[:], T.key1[:, 0:L], F.Relu, [], ["key1", "td"])
        a0 = PITCH * rank + 1
        act(T[nk][:, CAP * rank:CAP * (rank + 1)], T["sw%d" % s][:, a0:a0 + CAP], F.Copy, swk, [nk + "o"])
        if s < RO - 1:
            kis, nis = ["kk%d" % n for n in range(last + 1)], ["ni%d" % n for n in range(last + 1)]
            ts(T.ii[:], T.kk[:, 15::16], 13, 15, A.arith_shift_right, A.bitwise_and, kis, ["ii"])
            ts(T.g1[:], T.key0[:, 0:24], -SC, 16.0, A.is_lt, A.mult, [], ["key0", "g1"])
            if s == 0:
                act(T.qw[:, 0:B], T.qi[:, 0:B], F.Silu, ["qi", "cc0"], ["qw"], scale=-1.0, bias=float(QZ))
            act(T.qf[:], ind(T.qw[:, 0:B + 16], T.bl[:]), F.Copy, ["qw", "qwp", "bl"], ["qf"])
            mm(T.ps0[:, 0:L], T.idf[:], T.qf[:], True, False, ["idf", "qf"], ["ps0"])
            tt(T.g3[:], T.g1[:], T.tra[:], A.mult, ["g1", "tra"], ["g3"])
            tt(T.g5[:], T.g1[:], T.ii[:], A.add, ["g1", "ii"], ["g5"])
            tt(T.g6[:], T.g3[:], T.ni[:], A.max, ["g3"] + nis, ["g6"])
            tc(T.il[:], T.g5[:], ["g5"], ["il"])
            tc(T.al[:], T.g6[:], ["g6"], ["al"])
            act(T.mk[:], ind(T.wn[:], T.il[:]), F.Copy, ["wna", "wnb", "il"], ["mk"])
            tt(ind(T.aw[:], T.al[:]), T.ag[:], T.tn[:], A.add, ["al", "aga", "agb", "tn"], ["aw", "awp"])
            mm(T.ps0[:, 0:L], T.idb[:], T.mk[:], False, True, ["idb", "mk"], ["ps0"])
            act(T.qn[:], T.ps0[:, 0:L], F.Relu, [], ["ps0", "qn"])
            act(ind(T.qw[:], T.ol[:]), T.qn[:], F.Silu, ["ol", "qn"], ["qw", "qwp"])
        tt(ind(T.vw[:], T.ol[:]), T.xx[:], T.td[:], A.add, ["ol", "xx", "td"], ["vw", "vwp"])
    op("s", lambda e: e.dma_start(T.yv[:], T.vw[:, 0:B]), ["vw"], ["yv"], 3.7, dma=("dyv", 16))

    lk = "land%d" % RO
    lks = [lk, lk + "o"]
    ts(T.ci[:], T[lk][:], PK - 1, None, A.bitwise_and, None, lks, ["ci"])
    tc(T.cb[:], T.ci[:], ["ci"], ["cb"])
    op("s", lambda e: e.dma_start(T.yc[:], T.cb[:]), ["cb"], ["yc"], 2.0, dma=("dyc", 16))
    act(T.yi[:], T[lk][:], F.Identity, lks, ["yi"], bias=BIG - base, scale=1.0 / PK)
    act(T.ab[:], T.yi[:], F.Identity, ["yi"], ["aba", "abb"], bias=-BIG)
    op("a", lambda e: e.dma_start(T.yw[:], T.ab[0::16, :]), ["aba", "abb"], ["yw"], 1.8, dma=("dyw", 16))
    emit([("dwk", 16), ("dvp", 16), ("dqu", 16), ("dam", 16), ("dpay", 128), ("dpay2", 128), ("sent", 2 * (NR - 1) * RO)])
    for n in ("dyv", "dyw", "dyc"):
        g.wait_ge(T.sem[n], 16)
